import numpy as np
import ml_dtypes


def mxq(x, axis, fmt="e4m3"):
    dtype, down = {"e4m3": (ml_dtypes.float8_e4m3fn, 7), "e5m2": (ml_dtypes.float8_e5m2, 14)}[fmt]
    v = np.moveaxis(np.asarray(x, np.float32).astype(ml_dtypes.bfloat16).astype(np.float64), axis, -1)
    blocks = v.reshape(v.shape[:-1] + (-1, 32))
    amax = np.abs(blocks).max(-1, keepdims=True)
    byte = np.maximum(np.where(amax > 0, np.frexp(amax)[1] - 1 + 127, 0) - down, 1)
    scale = np.exp2(byte - 127.0)
    codes = (blocks / scale).astype(np.float32).astype(dtype).astype(np.float64)
    return np.moveaxis((codes * scale).reshape(v.shape), -1, axis)


WIDE = False


def mx_kscale(k):
    if not WIDE:
        return np.ones(k)
    levels = np.array([18, -18])
    if k % 512:
        return np.exp2(np.random.permutation(np.resize(levels, k // 32))).repeat(32)
    a = np.empty((k // 512, 16))
    for p in range(k // 512):
        a[p, :8] = np.random.permutation(np.resize(levels, 8))
        for g in range(8):
            far = levels[np.abs(levels - a[p, g]) >= 10]
            a[p, g + 8] = far[np.random.randint(len(far))]
    return np.exp2(a.ravel()).repeat(32)


def f64(x):
    return np.asarray(x).astype(np.float64)


def striped(idx):
    return np.tile(np.asarray(idx).reshape(-1, 16).T, (8, 1)).astype(np.uint16)


def unstriped(offs):
    return offs[:16].T.reshape(-1).astype(np.int64)


B, N, T, D, R = 1, 512, 1024, 512, 512
LR = 0.1
BETA = 0.5
RHO = 0.9
EPS = 0.001


def setup_inputs():
    n = np.random.standard_normal
    idx = np.random.permutation(T)[:B * N]
    s = mx_kscale(D)[:, None]
    z = mx_kscale(R)[:, None]
    x = n((B, D, R))
    return {
        "xT": (x * s).astype(np.float32),
        "wT": (n((D, T)) * (1.00 / np.sqrt(D)) / s).astype(np.float32),
        "y": n((B, R, N)).astype(np.float32),
        "wt": (np.random.uniform(0.5, 1.5, (B, R, 1)) * 1.0 / np.sqrt(R) * z).astype(np.float32),
        "xm": (x.transpose(0, 2, 1) / z).astype(np.float32),
        "mT": (0.3 * n((D, T))).astype(np.float32),
        "vT": (np.random.uniform(0.1, 0.5, (D, T))).astype(np.float32),
        "offs": striped(idx),
    }


def reference(xT, wT, y, wt, xm, mT, vT, offs):
    idx = unstriped(offs)
    pick = lambda x: x[:, idx].reshape(x.shape[0], B, N).transpose(1, 0, 2)
    a = mxq(f64(xT), 1, "e4m3").transpose(0, 2, 1) @ mxq(pick(f64(wT)), 1, "e4m3")
    g = f64(wt) * np.tanh(a - f64(y))
    dw = mxq(f64(xm), 1, "e4m3").transpose(0, 2, 1) @ mxq(g, 1, "e5m2")
    nm = BETA * pick(f64(mT)) + (1.0 - BETA) * dw
    nv = RHO * pick(f64(vT)) + (1.0 - RHO) * dw * dw
    nw = -LR * nm / (np.sqrt(nv) + EPS)
    tables = []
    for old, new in ((wT, nw), (mT, nm), (vT, nv),):
        table = f64(old) if old is not wT else np.zeros((D, T))
        table[:, idx] = new.transpose(1, 0, 2).reshape(D, B * N)
        tables.append(table)
    return tuple(tables)

@@ -1,0 +1,179 @@
+import math
+from contextlib import ExitStack
+
+import concourse.mybir as mybir
+
+N, T, D, R = 512, 1024, 512, 512
+LR, BETA, RHO, EPS = 0.1, 0.5, 0.9, 0.001
+FLOPS = 2 * 2 * R * D * N
+
+F32 = mybir.dt.float32
+BF16 = mybir.dt.bfloat16
+U32 = mybir.dt.uint32
+U16 = mybir.dt.uint16
+U8 = mybir.dt.uint8
+E4M3 = mybir.dt.float8_e4m3fn_x4
+E5M2 = mybir.dt.float8_e5m2_x4
+ACT = mybir.ActivationFunctionType
+ALU = mybir.AluOpType
+
+P = 128
+PACK = 4
+BLOCKS = D // P
+CHUNK = 128
+CHUNKS = N // CHUNK
+HALF = T // 2
+
+
+def tile_attend_glch_adam_kernel(tc, xT, wT, y, wt, xm, mT, vT, offs, out_0, out_1, out_2):
+    nc = tc.nc
+    with ExitStack() as ctx:
+        keep = ctx.enter_context(tc.tile_pool(name="keep", bufs=1))
+        psum = ctx.enter_context(tc.psum_pool(name="psum", bufs=1))
+
+        def sb(name, shape, dtype):
+            return keep.tile(shape, dtype, name=name, align_bytes=64)
+
+        offsets = keep.tile([P, N // 16], U16, name="offsets")
+        nc.sync.dma_start(offsets[:], offs)
+
+        w_rows = wT.rearrange("(p u e) t -> u p e t", u=2, e=2)
+        w_raw = [[sb("w_raw%d%d" % (u, h), [P, 2, HALF], F32) for h in range(2)] for u in range(2)]
+        for u in range(2):
+            for h in range(2):
+                nc.sync.dma_start(w_raw[u][h][:], w_rows[u][:, :, h * HALF:(h + 1) * HALF])
+        x_raw = sb("x_raw", [P, PACK, R], F32)
+        nc.sync.dma_start(x_raw[:], xT[0].rearrange("(p j) r -> p j r", j=PACK))
+        y_sb = sb("y_sb", [P, PACK, N], F32)
+        nc.sync.dma_start(y_sb[:], y[0].rearrange("(p t) i -> p t i", t=PACK))
+        wt_sb = sb("wt_sb", [P, PACK], F32)
+        nc.sync.dma_start(wt_sb[:], wt[0].rearrange("(p t) o -> p (t o)", t=PACK))
+        xm_raw = sb("xm_raw", [P, PACK, D], F32)
+        nc.sync.dma_start(xm_raw[:], xm[0].rearrange("(p t) d -> p t d", t=PACK))
+        m_old = [sb("m_old%d" % k, [P, T], F32) for k in range(BLOCKS)]
+        v_old = [sb("v_old%d" % k, [P, T], F32) for k in range(BLOCKS)]
+        m_new = [sb("m_new%d" % k, [P, T], F32) for k in range(BLOCKS)]
+        v_new = [sb("v_new%d" % k, [P, T], F32) for k in range(BLOCKS)]
+        step = [sb("step%d" % k, [P, T], F32) for k in range(BLOCKS)]
+        for tiles, table in ((v_old, vT), (m_old, mT), (v_new, vT), (m_new, mT)):
+            for k in range(BLOCKS):
+                nc.sync.dma_start(tiles[k][:], table[k * P:(k + 1) * P, :])
+
+        ones = sb("ones", [P, N], F32)
+        nc.vector.memset(ones[:], 1.0)
+        beta = sb("beta", [P, N], F32)
+        nc.scalar.activation(beta[:], ones[:], ACT.Copy, scale=BETA)
+        eps_col = sb("eps_col", [P, 1], F32)
+        nc.vector.tensor_scalar(eps_col[:], ones[:, 0:1], EPS / LR, None, ALU.mult)
+        for k in range(BLOCKS):
+            nc.vector.memset(step[k][:], 0.0)
+
+        w_pairs = [sb("w_pairs%d" % u, [P, T], U32) for u in range(2)]
+        w_picked = sb("w_picked", [P, N, 2], U32)
+        for u in range(2):
+            for h in range(2):
+                dst = w_pairs[u][:, h * HALF:(h + 1) * HALF].bitcast(BF16).rearrange("p (c i e) -> p c e i", i=4, e=2)
+                src = w_raw[u][h][:].rearrange("p e (c i) -> p c e i", i=4)
+                if h == 0:
+                    nc.scalar.activation(dst, src, ACT.Copy)
+                else:
+                    nc.vector.tensor_copy(dst, src)
+            nc.vector.tensor_copy(w_picked[:, :, u], w_pairs[u][:].indirect(offsets[:]))
+        w_codes = sb("w_codes", [P, N], U32)
+        w_scales = sb("w_scales", [P, N], U8)
+        nc.vector.quantize_mx(
+            out=w_codes[:].bitcast(E4M3), scales=w_scales[:],
+            in_=w_picked[:].rearrange("p i u -> p (i u)").bitcast(BF16))
+
+        x_bf = sb("x_bf", [P, PACK, P, PACK], BF16)
+        for h in range(2):
+            ms = slice(h * (P // 2), (h + 1) * (P // 2))
+            dst = x_bf[:, :, ms, :].rearrange("p t m j -> p m j t")
+            src = x_raw[:].rearrange("p j (m t) -> p m j t", t=PACK)[:, ms, :, :]
+            if h == 0:
+                nc.scalar.activation(dst, src, ACT.Copy)
+            else:
+                nc.vector.tensor_copy(dst, src)
+        x_codes = sb("x_codes", [P, R], U32)
+        x_scales = sb("x_scales", [P, R], U8)
+        nc.vector.quantize_mx(
+            out=x_codes[:].bitcast(E4M3), scales=x_scales[:],
+            in_=x_bf[:].rearrange("p t m j -> p (t m j)"))
+
+        g_codes = sb("g_codes", [P, N], U32)
+        g_scales = sb("g_scales", [P, N], U8)
+        g_bf = []
+        for c in range(CHUNKS):
+            cols = slice(c * CHUNK, (c + 1) * CHUNK)
+            a = psum.tile([P, PACK, CHUNK], F32, name="a%d" % c)
+            for t in range(PACK):
+                rows = slice(t * P, (t + 1) * P)
+                nc.tensor.matmul_mx(
+                    out=a[:, t, :],
+                    lhsT=x_codes[:, rows].bitcast(E4M3), lhsT_scale=x_scales[:, rows],
+                    rhs=w_codes[:, cols].bitcast(E4M3), rhs_scale=w_scales[:, cols],
+                    start=True, stop=True)
+            diff = sb("diff%d" % c, [P, PACK, CHUNK], F32)
+            nc.vector.tensor_tensor(diff[:], a[:], y_sb[:, :, cols], ALU.subtract)
+            th = sb("th%d" % c, [P, CHUNK, PACK], F32)
+            nc.scalar.activation(th[:], diff[:].rearrange("p t i -> p i t"), ACT.Tanh)
+            g = sb("g%d" % c, [P, CHUNK, PACK], BF16)
+            g_bf.append((g, th, cols))
+        for g, th, cols in g_bf:
+            nc.vector.tensor_tensor(g[:], th[:], wt_sb[:].unsqueeze(1).to_broadcast([P, CHUNK, PACK]), ALU.mult)
+        for g, th, cols in g_bf:
+            nc.vector.quantize_mx(
+                out=g_codes[:, cols].bitcast(E5M2), scales=g_scales[:, cols],
+                in_=g[:].rearrange("p i t -> p (i t)"))
+
+        xm_bf = sb("xm_bf", [P, D, PACK], BF16)
+        nc.scalar.activation(
+            xm_bf[:].rearrange("p (c i) t -> p c t i", i=4),
+            xm_raw[:].rearrange("p t (c i) -> p c t i", i=4), ACT.Copy)
+        xm_codes = sb("xm_codes", [P, D], U32)
+        xm_scales = sb("xm_scales", [P, D], U8)
+        nc.vector.quantize_mx(
+            out=xm_codes[:].bitcast(E4M3), scales=xm_scales[:],
+            in_=xm_bf[:].rearrange("p d t -> p (d t)"))
+
+        dw = []
+        for k in range(BLOCKS):
+            rows = slice(k * P, (k + 1) * P)
+            bank = psum.tile([P, N], F32, name="dw%d" % k)
+            nc.tensor.matmul_mx(
+                out=bank[:],
+                lhsT=xm_codes[:, rows].bitcast(E4M3), lhsT_scale=xm_scales[:, rows],
+                rhs=g_codes[:].bitcast(E5M2), rhs_scale=g_scales[:],
+                start=True, stop=True)
+            dw.append(bank)
+
+        nv = sb("nv", [P, BLOCKS, N], F32)
+        nm = sb("nm", [P, BLOCKS, N], F32)
+        sq = sb("sq", [P, BLOCKS, N], F32)
+        rate = sb("rate", [P, BLOCKS, N], F32)
+        v_picked = [sb("v_picked%d" % k, [P, N], F32) for k in range(BLOCKS)]
+        m_picked = [sb("m_picked%d" % k, [P, N], F32) for k in range(BLOCKS)]
+        for k in range(BLOCKS):
+            nc.scalar.activation(sq[:, k, :], dw[k][:], ACT.Square, scale=math.sqrt(1.0 - RHO))
+        for k in range(BLOCKS):
+            nc.vector.tensor_copy(v_picked[k][:], v_old[k][:].indirect(offsets[:]))
+        for k in range(BLOCKS):
+            nc.vector.scalar_tensor_tensor(nv[:, k, :], v_picked[k][:], RHO, sq[:, k, :], ALU.mult, ALU.add)
+        flat = "p k i -> p (k i)"
+        nc.scalar.activation(sq[:].rearrange(flat), nv[:].rearrange(flat), ACT.Sqrt)
+        nc.scalar.activation(rate[:].rearrange(flat), sq[:].rearrange(flat), ACT.Ln, bias=eps_col[:], scale=1.0 / LR)
+        nc.scalar.activation(sq[:].rearrange(flat), rate[:].rearrange(flat), ACT.Exp, scale=-1.0)
+        nc.scalar.activation(rate[:].rearrange(flat), sq[:].rearrange(flat), ACT.Copy, scale=-1.0)
+        for k in range(BLOCKS):
+            nc.vector.tensor_tensor(m_picked[k][:], m_old[k][:].indirect(offsets[:]), beta[:], ALU.mult)
+        for k in range(BLOCKS):
+            nc.vector.scalar_tensor_tensor(nm[:, k, :], dw[k][:], 1.0 - BETA, m_picked[k][:], ALU.mult, ALU.add)
+        for k in range(BLOCKS):
+            nc.vector.tensor_copy(v_new[k][:].indirect(offsets[:]), nv[:, k, :])
+            nc.sync.dma_start(out_2[k * P:(k + 1) * P, :], v_new[k][:])
+        for k in range(BLOCKS):
+            nc.vector.tensor_copy(m_new[k][:].indirect(offsets[:]), nm[:, k, :])
+            nc.sync.dma_start(out_1[k * P:(k + 1) * P, :], m_new[k][:])
+        for k in range(BLOCKS):
+            nc.vector.tensor_tensor(step[k][:].indirect(offsets[:]), nm[:, k, :], rate[:, k, :], ALU.mult)
+            nc.sync.dma_start(out_0[k * P:(k + 1) * P, :], step[k][:])

@@ -31,12 +31,14 @@ def tile_attend_glch_adam_kernel(tc, xT, wT, y, wt, xm, mT, vT, offs, out_0, out
         keep = ctx.enter_context(tc.tile_pool(name="keep", bufs=1))
         psum = ctx.enter_context(tc.psum_pool(name="psum", bufs=1))
 
-        def sb(name, shape, dtype):
-            return keep.tile(shape, dtype, name=name, align_bytes=64)
+        def sb(name, shape, dtype, tag=None):
+            return keep.tile(shape, dtype, name=name, tag=tag or name, align_bytes=64)
 
         offsets = keep.tile([P, N // 16], U16, name="offsets")
         nc.sync.dma_start(offsets[:], offs)
 
+        wt_sb = sb("wt_sb", [P, PACK], F32)
+        nc.sync.dma_start(wt_sb[:], wt[0].rearrange("(p t) o -> p (t o)", t=PACK))
         w_rows = wT.rearrange("(p u e) t -> u p e t", u=2, e=2)
         w_raw = [[sb("w_raw%d%d" % (u, h), [P, 2, HALF], F32) for h in range(2)] for u in range(2)]
         for u in range(2):
@@ -46,27 +48,34 @@ def tile_attend_glch_adam_kernel(tc, xT, wT, y, wt, xm, mT, vT, offs, out_0, out
         nc.sync.dma_start(x_raw[:], xT[0].rearrange("(p j) r -> p j r", j=PACK))
         y_sb = sb("y_sb", [P, PACK, N], F32)
         nc.sync.dma_start(y_sb[:], y[0].rearrange("(p t) i -> p t i", t=PACK))
-        wt_sb = sb("wt_sb", [P, PACK], F32)
-        nc.sync.dma_start(wt_sb[:], wt[0].rearrange("(p t) o -> p (t o)", t=PACK))
         xm_raw = sb("xm_raw", [P, PACK, D], F32)
-        nc.sync.dma_start(xm_raw[:], xm[0].rearrange("(p t) d -> p t d", t=PACK))
         m_old = [sb("m_old%d" % k, [P, T], F32) for k in range(BLOCKS)]
         v_old = [sb("v_old%d" % k, [P, T], F32) for k in range(BLOCKS)]
         m_new = [sb("m_new%d" % k, [P, T], F32) for k in range(BLOCKS)]
         v_new = [sb("v_new%d" % k, [P, T], F32) for k in range(BLOCKS)]
         step = [sb("step%d" % k, [P, T], F32) for k in range(BLOCKS)]
-        for tiles, table in ((v_old, vT), (m_old, mT), (v_new, vT), (m_new, mT)):
-            for k in range(BLOCKS):
-                nc.sync.dma_start(tiles[k][:], table[k * P:(k + 1) * P, :])
 
-        ones = sb("ones", [P, N], F32)
-        nc.vector.memset(ones[:], 1.0)
-        beta = sb("beta", [P, N], F32)
-        nc.scalar.activation(beta[:], ones[:], ACT.Copy, scale=BETA)
+        def load_block(tiles, table, k):
+            nc.sync.dma_start(tiles[k][:], table[k * P:(k + 1) * P, :])
+
+        load_block(v_old, vT, 0)
+        nc.sync.dma_start(xm_raw[:], xm[0].rearrange("(p t) d -> p t d", t=PACK))
+        for k in range(1, BLOCKS):
+            load_block(v_old, vT, k)
+        for tiles, table in ((m_old, mT), (v_new, vT), (m_new, mT)):
+            for k in range(BLOCKS):
+                load_block(tiles, table, k)
+
+        one = sb("one", [P, 1], F32)
+        nc.vector.memset(one[:], 1.0)
         eps_col = sb("eps_col", [P, 1], F32)
-        nc.vector.tensor_scalar(eps_col[:], ones[:, 0:1], EPS / LR, None, ALU.mult)
+        nc.scalar.activation(eps_col[:], one[:], ACT.Copy, scale=EPS / (LR * BETA))
+        minus_beta = sb("minus_beta", [P, N], F32)
+        nc.vector.memset(minus_beta[:], -BETA)
         for k in range(BLOCKS):
-            nc.vector.memset(step[k][:], 0.0)
+            (nc.vector if k % 2 else nc.gpsimd).memset(step[k][:], 0.0)
+        wt_wide = sb("wt_wide", [P, CHUNK, PACK], F32)
+        nc.scalar.activation(wt_wide[:], wt_sb[:].unsqueeze(1).to_broadcast([P, CHUNK, PACK]), ACT.Copy)
 
         w_pairs = [sb("w_pairs%d" % u, [P, T], U32) for u in range(2)]
         w_picked = sb("w_picked", [P, N, 2], U32)
@@ -100,9 +109,10 @@ def tile_attend_glch_adam_kernel(tc, xT, wT, y, wt, xm, mT, vT, offs, out_0, out
             out=x_codes[:].bitcast(E4M3), scales=x_scales[:],
             in_=x_bf[:].rearrange("p t m j -> p (t m j)"))
 
-        g_codes = sb("g_codes", [P, N], U32)
+        dw_codes = sb("dw_codes", [P, N + D], U32, tag="m_old0")
+        g_codes, xm_codes = dw_codes[:, 0:N], dw_codes[:, N:N + D]
         g_scales = sb("g_scales", [P, N], U8)
-        g_bf = []
+        g_bf = sb("g_bf", [P, N, PACK], BF16)
         for c in range(CHUNKS):
             cols = slice(c * CHUNK, (c + 1) * CHUNK)
             a = psum.tile([P, PACK, CHUNK], F32, name="a%d" % c)
@@ -117,23 +127,19 @@ def tile_attend_glch_adam_kernel(tc, xT, wT, y, wt, xm, mT, vT, offs, out_0, out
             nc.vector.tensor_tensor(diff[:], a[:], y_sb[:, :, cols], ALU.subtract)
             th = sb("th%d" % c, [P, CHUNK, PACK], F32)
             nc.scalar.activation(th[:], diff[:].rearrange("p t i -> p i t"), ACT.Tanh)
-            g = sb("g%d" % c, [P, CHUNK, PACK], BF16)
-            g_bf.append((g, th, cols))
-        for g, th, cols in g_bf:
-            nc.vector.tensor_tensor(g[:], th[:], wt_sb[:].unsqueeze(1).to_broadcast([P, CHUNK, PACK]), ALU.mult)
-        for g, th, cols in g_bf:
-            nc.vector.quantize_mx(
-                out=g_codes[:, cols].bitcast(E5M2), scales=g_scales[:, cols],
-                in_=g[:].rearrange("p i t -> p (i t)"))
+            nc.gpsimd.tensor_tensor(
+                g_bf[:, cols, :], th[:], wt_wide[:], ALU.mult)
+        nc.vector.quantize_mx(
+            out=g_codes.bitcast(E5M2), scales=g_scales[:],
+            in_=g_bf[:].rearrange("p i t -> p (i t)"))
 
-        xm_bf = sb("xm_bf", [P, D, PACK], BF16)
+        xm_bf = sb("xm_bf", [P, D, PACK], BF16, tag="diff%d" % (CHUNKS - 1))
         nc.scalar.activation(
             xm_bf[:].rearrange("p (c i) t -> p c t i", i=4),
             xm_raw[:].rearrange("p t (c i) -> p c t i", i=4), ACT.Copy)
-        xm_codes = sb("xm_codes", [P, D], U32)
         xm_scales = sb("xm_scales", [P, D], U8)
         nc.vector.quantize_mx(
-            out=xm_codes[:].bitcast(E4M3), scales=xm_scales[:],
+            out=xm_codes.bitcast(E4M3), scales=xm_scales[:],
             in_=xm_bf[:].rearrange("p d t -> p (d t)"))
 
         dw = []
@@ -143,37 +149,43 @@ def tile_attend_glch_adam_kernel(tc, xT, wT, y, wt, xm, mT, vT, offs, out_0, out
             nc.tensor.matmul_mx(
                 out=bank[:],
                 lhsT=xm_codes[:, rows].bitcast(E4M3), lhsT_scale=xm_scales[:, rows],
-                rhs=g_codes[:].bitcast(E5M2), rhs_scale=g_scales[:],
+                rhs=g_codes.bitcast(E5M2), rhs_scale=g_scales[:],
                 start=True, stop=True)
             dw.append(bank)
 
         nv = sb("nv", [P, BLOCKS, N], F32)
-        nm = sb("nm", [P, BLOCKS, N], F32)
         sq = sb("sq", [P, BLOCKS, N], F32)
-        rate = sb("rate", [P, BLOCKS, N], F32)
-        v_picked = [sb("v_picked%d" % k, [P, N], F32) for k in range(BLOCKS)]
-        m_picked = [sb("m_picked%d" % k, [P, N], F32) for k in range(BLOCKS)]
+        minus_dw = sb("minus_dw", [P, BLOCKS, N], F32, tag="x_raw")
+        minus_sum = sb("minus_sum", [P, BLOCKS, N], F32)
+        v_picked = sb("v_picked", [P, BLOCKS, N], F32, tag="y_sb")
+        v_kept = [sb("v_kept%d" % k, [P, N], F32, tag="w_raw%d%d" % divmod(k, 2)) for k in range(BLOCKS)]
+        m_first = sb("m_first", [P, N], F32)
+        m_rest = sb("m_rest", [P, BLOCKS - 1, N], F32, tag="diff%d" % (CHUNKS - 1))
+        m_picked = [m_first[:]] + [m_rest[:, k, :] for k in range(BLOCKS - 1)]
+        for k in range(BLOCKS):
+            nc.vector.tensor_copy(v_picked[:, k, :], v_old[k][:].indirect(offsets[:]))
+            nc.scalar.activation(v_kept[k][:], v_picked[:, k, :], ACT.Copy, scale=RHO)
+        for k in range(BLOCKS):
+            nc.vector.tensor_copy(m_picked[k], m_old[k][:].indirect(offsets[:]))
         for k in range(BLOCKS):
             nc.scalar.activation(sq[:, k, :], dw[k][:], ACT.Square, scale=math.sqrt(1.0 - RHO))
+            nc.gpsimd.tensor_tensor(nv[:, k, :], v_kept[k][:], sq[:, k, :], ALU.add)
         for k in range(BLOCKS):
-            nc.vector.tensor_copy(v_picked[k][:], v_old[k][:].indirect(offsets[:]))
-        for k in range(BLOCKS):
-            nc.vector.scalar_tensor_tensor(nv[:, k, :], v_picked[k][:], RHO, sq[:, k, :], ALU.mult, ALU.add)
+            nc.scalar.activation(minus_dw[:, k, :], dw[k][:], ACT.Copy, scale=-1.0)
+            nc.gpsimd.tensor_tensor(minus_sum[:, k, :], minus_dw[:, k, :], m_picked[k], ALU.subtract)
         flat = "p k i -> p (k i)"
-        nc.scalar.activation(sq[:].rearrange(flat), nv[:].rearrange(flat), ACT.Sqrt)
-        nc.scalar.activation(rate[:].rearrange(flat), sq[:].rearrange(flat), ACT.Ln, bias=eps_col[:], scale=1.0 / LR)
-        nc.scalar.activation(sq[:].rearrange(flat), rate[:].rearrange(flat), ACT.Exp, scale=-1.0)
-        nc.scalar.activation(rate[:].rearrange(flat), sq[:].rearrange(flat), ACT.Copy, scale=-1.0)
-        for k in range(BLOCKS):
-            nc.vector.tensor_tensor(m_picked[k][:], m_old[k][:].indirect(offsets[:]), beta[:], ALU.mult)
-        for k in range(BLOCKS):
-            nc.vector.scalar_tensor_tensor(nm[:, k, :], dw[k][:], 1.0 - BETA, m_picked[k][:], ALU.mult, ALU.add)
+        root = sb("root", [P, BLOCKS * N], F32, tag="xm_raw")
+        log_den = sb("log_den", [P, BLOCKS * N], F32, tag="y_sb")
+        rate = sb("rate", [P, BLOCKS, N], F32, tag="sq")
+        nc.scalar.activation(root[:], nv[:].rearrange(flat), ACT.Sqrt)
+        nc.scalar.activation(log_den[:], root[:], ACT.Ln, bias=eps_col[:], scale=1.0 / (LR * BETA))
+        nc.scalar.activation(rate[:].rearrange(flat), log_den[:], ACT.Exp, scale=-1.0)
         for k in range(BLOCKS):
             nc.vector.tensor_copy(v_new[k][:].indirect(offsets[:]), nv[:, k, :])
             nc.sync.dma_start(out_2[k * P:(k + 1) * P, :], v_new[k][:])
         for k in range(BLOCKS):
-            nc.vector.tensor_copy(m_new[k][:].indirect(offsets[:]), nm[:, k, :])
+            nc.vector.tensor_tensor(m_new[k][:].indirect(offsets[:]), minus_sum[:, k, :], minus_beta[:], ALU.mult)
             nc.sync.dma_start(out_1[k * P:(k + 1) * P, :], m_new[k][:])
         for k in range(BLOCKS):
-            nc.vector.tensor_tensor(step[k][:].indirect(offsets[:]), nm[:, k, :], rate[:, k, :], ALU.mult)
+            nc.vector.tensor_tensor(step[k][:].indirect(offsets[:]), minus_sum[:, k, :], rate[:, k, :], ALU.mult)
             nc.sync.dma_start(out_0[k * P:(k + 1) * P, :], step[k][:])

@@ -23,6 +23,7 @@ BLOCKS = D // P
 CHUNK = 128
 CHUNKS = N // CHUNK
 HALF = T // 2
+FIRST_CUT = 384
 
 
 def tile_attend_glch_adam_kernel(tc, xT, wT, y, wt, xm, mT, vT, offs, out_0, out_1, out_2):
@@ -34,18 +35,18 @@ def tile_attend_glch_adam_kernel(tc, xT, wT, y, wt, xm, mT, vT, offs, out_0, out
         def sb(name, shape, dtype, tag=None):
             return keep.tile(shape, dtype, name=name, tag=tag or name, align_bytes=64)
 
+        w_rows = wT.rearrange("(p u e) t -> u p e t", u=2, e=2)
+        w_first = sb("w_first", [P, 2, T], F32)
+        nc.sync.dma_start(w_first[:], w_rows[0])
         offsets = keep.tile([P, N // 16], U16, name="offsets")
         nc.sync.dma_start(offsets[:], offs)
-
-        wt_sb = sb("wt_sb", [P, PACK], F32)
-        nc.sync.dma_start(wt_sb[:], wt[0].rearrange("(p t) o -> p (t o)", t=PACK))
-        w_rows = wT.rearrange("(p u e) t -> u p e t", u=2, e=2)
-        w_raw = [[sb("w_raw%d%d" % (u, h), [P, 2, HALF], F32) for h in range(2)] for u in range(2)]
-        for u in range(2):
-            for h in range(2):
-                nc.sync.dma_start(w_raw[u][h][:], w_rows[u][:, :, h * HALF:(h + 1) * HALF])
+        w_second = [sb("w_second%d" % h, [P, 2, HALF], F32) for h in range(2)]
+        for h in range(2):
+            nc.sync.dma_start(w_second[h][:], w_rows[1][:, :, h * HALF:(h + 1) * HALF])
         x_raw = sb("x_raw", [P, PACK, R], F32)
         nc.sync.dma_start(x_raw[:], xT[0].rearrange("(p j) r -> p j r", j=PACK))
+        wt_sb = sb("wt_sb", [P, PACK], F32)
+        nc.sync.dma_start(wt_sb[:], wt[0].rearrange("(p t) o -> p (t o)", t=PACK))
         y_sb = sb("y_sb", [P, PACK, N], F32)
         nc.sync.dma_start(y_sb[:], y[0].rearrange("(p t) i -> p t i", t=PACK))
         xm_raw = sb("xm_raw", [P, PACK, D], F32)
@@ -69,9 +70,7 @@ def tile_attend_glch_adam_kernel(tc, xT, wT, y, wt, xm, mT, vT, offs, out_0, out
         one = sb("one", [P, 1], F32)
         nc.vector.memset(one[:], 1.0)
         eps_col = sb("eps_col", [P, 1], F32)
-        nc.scalar.activation(eps_col[:], one[:], ACT.Copy, scale=EPS / (LR * BETA))
-        minus_beta = sb("minus_beta", [P, N], F32)
-        nc.vector.memset(minus_beta[:], -BETA)
+        nc.scalar.activation(eps_col[:], one[:], ACT.Copy, scale=EPS / LR)
         for k in range(BLOCKS):
             (nc.vector if k % 2 else nc.gpsimd).memset(step[k][:], 0.0)
         wt_wide = sb("wt_wide", [P, CHUNK, PACK], F32)
@@ -79,15 +78,19 @@ def tile_attend_glch_adam_kernel(tc, xT, wT, y, wt, xm, mT, vT, offs, out_0, out
 
         w_pairs = [sb("w_pairs%d" % u, [P, T], U32) for u in range(2)]
         w_picked = sb("w_picked", [P, N, 2], U32)
-        for u in range(2):
-            for h in range(2):
-                dst = w_pairs[u][:, h * HALF:(h + 1) * HALF].bitcast(BF16).rearrange("p (c i e) -> p c e i", i=4, e=2)
-                src = w_raw[u][h][:].rearrange("p e (c i) -> p c e i", i=4)
-                if h == 0:
-                    nc.scalar.activation(dst, src, ACT.Copy)
-                else:
-                    nc.vector.tensor_copy(dst, src)
-            nc.vector.tensor_copy(w_picked[:, :, u], w_pairs[u][:].indirect(offsets[:]))
+
+        def pair_views(u, lo, src):
+            width = src.shape[2]
+            dst = w_pairs[u][:, lo:lo + width].bitcast(BF16).rearrange("p (c i e) -> p c e i", i=4, e=2)
+            return dst, src.rearrange("p e (c i) -> p c e i", i=4)
+
+        nc.scalar.activation(*pair_views(0, 0, w_first[:, :, 0:FIRST_CUT]), ACT.Copy)
+        nc.vector.tensor_copy(*pair_views(0, FIRST_CUT, w_first[:, :, FIRST_CUT:T]))
+        nc.vector.tensor_copy(w_picked[:, :, 0], w_pairs[0][:].indirect(offsets[:]))
+        nc.scalar.activation(*pair_views(1, 0, w_second[0][:]), ACT.Copy)
+        nc.scalar.activation(*pair_views(1, HALF, w_second[1][:, :, 0:HALF // 2]), ACT.Copy)
+        nc.vector.tensor_copy(*pair_views(1, HALF + HALF // 2, w_second[1][:, :, HALF // 2:HALF]))
+        nc.vector.tensor_copy(w_picked[:, :, 1], w_pairs[1][:].indirect(offsets[:]))
         w_codes = sb("w_codes", [P, N], U32)
         w_scales = sb("w_scales", [P, N], U8)
         nc.vector.quantize_mx(
@@ -105,9 +108,11 @@ def tile_attend_glch_adam_kernel(tc, xT, wT, y, wt, xm, mT, vT, offs, out_0, out
                 nc.vector.tensor_copy(dst, src)
         x_codes = sb("x_codes", [P, R], U32)
         x_scales = sb("x_scales", [P, R], U8)
-        nc.vector.quantize_mx(
-            out=x_codes[:].bitcast(E4M3), scales=x_scales[:],
-            in_=x_bf[:].rearrange("p t m j -> p (t m j)"))
+        for h in range(2):
+            rows = slice(h * 2 * P, (h + 1) * 2 * P)
+            nc.vector.quantize_mx(
+                out=x_codes[:, rows].bitcast(E4M3), scales=x_scales[:, rows],
+                in_=x_bf[:, 2 * h:2 * h + 2, :, :].rearrange("p t m j -> p (t m j)"))
 
         dw_codes = sb("dw_codes", [P, N + D], U32, tag="m_old0")
         g_codes, xm_codes = dw_codes[:, 0:N], dw_codes[:, N:N + D]
@@ -154,38 +159,40 @@ def tile_attend_glch_adam_kernel(tc, xT, wT, y, wt, xm, mT, vT, offs, out_0, out
             dw.append(bank)
 
         nv = sb("nv", [P, BLOCKS, N], F32)
+        nm = sb("nm", [P, BLOCKS, N], F32)
         sq = sb("sq", [P, BLOCKS, N], F32)
-        minus_dw = sb("minus_dw", [P, BLOCKS, N], F32, tag="x_raw")
-        minus_sum = sb("minus_sum", [P, BLOCKS, N], F32)
+        dw_part = sb("dw_part", [P, BLOCKS, N], F32, tag="x_raw")
         v_picked = sb("v_picked", [P, BLOCKS, N], F32, tag="y_sb")
-        v_kept = [sb("v_kept%d" % k, [P, N], F32, tag="w_raw%d%d" % divmod(k, 2)) for k in range(BLOCKS)]
+        v_kept = sb("v_kept", [P, BLOCKS, N], F32, tag="w_first")
         m_first = sb("m_first", [P, N], F32)
         m_rest = sb("m_rest", [P, BLOCKS - 1, N], F32, tag="diff%d" % (CHUNKS - 1))
         m_picked = [m_first[:]] + [m_rest[:, k, :] for k in range(BLOCKS - 1)]
+        m_kept = [sb("m_kept%d" % k, [P, N], F32, tag="th%d" % k) for k in range(BLOCKS)]
         for k in range(BLOCKS):
             nc.vector.tensor_copy(v_picked[:, k, :], v_old[k][:].indirect(offsets[:]))
-            nc.scalar.activation(v_kept[k][:], v_picked[:, k, :], ACT.Copy, scale=RHO)
+            nc.scalar.activation(v_kept[:, k, :], v_picked[:, k, :], ACT.Copy, scale=RHO)
         for k in range(BLOCKS):
             nc.vector.tensor_copy(m_picked[k], m_old[k][:].indirect(offsets[:]))
         for k in range(BLOCKS):
             nc.scalar.activation(sq[:, k, :], dw[k][:], ACT.Square, scale=math.sqrt(1.0 - RHO))
-            nc.gpsimd.tensor_tensor(nv[:, k, :], v_kept[k][:], sq[:, k, :], ALU.add)
+            nc.gpsimd.tensor_tensor(nv[:, k, :], v_kept[:, k, :], sq[:, k, :], ALU.add)
         for k in range(BLOCKS):
-            nc.scalar.activation(minus_dw[:, k, :], dw[k][:], ACT.Copy, scale=-1.0)
-            nc.gpsimd.tensor_tensor(minus_sum[:, k, :], minus_dw[:, k, :], m_picked[k], ALU.subtract)
+            nc.scalar.activation(m_kept[k][:], m_picked[k], ACT.Copy, scale=BETA)
+            nc.scalar.activation(dw_part[:, k, :], dw[k][:], ACT.Copy, scale=1.0 - BETA)
+            nc.gpsimd.tensor_tensor(nm[:, k, :], dw_part[:, k, :], m_kept[k][:], ALU.add)
         flat = "p k i -> p (k i)"
         root = sb("root", [P, BLOCKS * N], F32, tag="xm_raw")
         log_den = sb("log_den", [P, BLOCKS * N], F32, tag="y_sb")
-        rate = sb("rate", [P, BLOCKS, N], F32, tag="sq")
+        rate = sb("rate", [P, BLOCKS * N], F32, tag="sq")
+        minus_rate = sb("minus_rate", [P, BLOCKS, N], F32, tag="xm_raw")
+        nw = sb("nw", [P, BLOCKS, N], F32, tag="x_raw")
         nc.scalar.activation(root[:], nv[:].rearrange(flat), ACT.Sqrt)
-        nc.scalar.activation(log_den[:], root[:], ACT.Ln, bias=eps_col[:], scale=1.0 / (LR * BETA))
-        nc.scalar.activation(rate[:].rearrange(flat), log_den[:], ACT.Exp, scale=-1.0)
+        nc.scalar.activation(log_den[:], root[:], ACT.Ln, bias=eps_col[:], scale=1.0 / LR)
+        nc.scalar.activation(rate[:], log_den[:], ACT.Exp, scale=-1.0)
+        nc.scalar.activation(minus_rate[:].rearrange(flat), rate[:], ACT.Copy, scale=-1.0)
         for k in range(BLOCKS):
-            nc.vector.tensor_copy(v_new[k][:].indirect(offsets[:]), nv[:, k, :])
-            nc.sync.dma_start(out_2[k * P:(k + 1) * P, :], v_new[k][:])
-        for k in range(BLOCKS):
-            nc.vector.tensor_tensor(m_new[k][:].indirect(offsets[:]), minus_sum[:, k, :], minus_beta[:], ALU.mult)
-            nc.sync.dma_start(out_1[k * P:(k + 1) * P, :], m_new[k][:])
-        for k in range(BLOCKS):
-            nc.vector.tensor_tensor(step[k][:].indirect(offsets[:]), minus_sum[:, k, :], rate[:, k, :], ALU.mult)
-            nc.sync.dma_start(out_0[k * P:(k + 1) * P, :], step[k][:])
+            nc.gpsimd.tensor_tensor(nw[:, k, :], nm[:, k, :], minus_rate[:, k, :], ALU.mult)
+        for tiles, new, out in ((v_new, nv, out_2), (m_new, nm, out_1), (step, nw, out_0)):
+            for k in range(BLOCKS):
+                nc.vector.tensor_copy(tiles[k][:].indirect(offsets[:]), new[:, k, :])
+                nc.sync.dma_start(out[k * P:(k + 1) * P, :], tiles[k][:])

@@ -48,8 +48,8 @@ def tile_attend_glch_adam_kernel(tc, xT, wT, y, wt, xm, mT, vT, offs, out_0, out
         wt_sb = sb("wt_sb", [P, PACK], F32)
         nc.sync.dma_start(wt_sb[:], wt[0].rearrange("(p t) o -> p (t o)", t=PACK))
         y_sb = sb("y_sb", [P, PACK, N], F32)
-        nc.sync.dma_start(y_sb[:], y[0].rearrange("(p t) i -> p t i", t=PACK))
-        xm_raw = sb("xm_raw", [P, PACK, D], F32)
+        xm_rows = xm[0].rearrange("(p t) d -> p t d", t=PACK)
+        xm_raw = [sb("xm_raw%d" % h, [P, PACK, D // 2], F32) for h in range(2)]
         m_old = [sb("m_old%d" % k, [P, T], F32) for k in range(BLOCKS)]
         v_old = [sb("v_old%d" % k, [P, T], F32) for k in range(BLOCKS)]
         m_new = [sb("m_new%d" % k, [P, T], F32) for k in range(BLOCKS)]
@@ -60,11 +60,17 @@ def tile_attend_glch_adam_kernel(tc, xT, wT, y, wt, xm, mT, vT, offs, out_0, out
             nc.sync.dma_start(tiles[k][:], table[k * P:(k + 1) * P, :])
 
         load_block(v_old, vT, 0)
-        nc.sync.dma_start(xm_raw[:], xm[0].rearrange("(p t) d -> p t d", t=PACK))
+        nc.sync.dma_start(y_sb[:], y[0].rearrange("(p t) i -> p t i", t=PACK))
+        nc.sync.dma_start(xm_raw[0][:], xm_rows[:, :, 0:D // 2])
         for k in range(1, BLOCKS):
             load_block(v_old, vT, k)
-        for tiles, table in ((m_old, mT), (v_new, vT), (m_new, mT)):
-            for k in range(BLOCKS):
+        for k in range(BLOCKS):
+            load_block(m_old, mT, k)
+        load_block(v_new, vT, 0)
+        nc.sync.dma_start(xm_raw[1][:], xm_rows[:, :, D // 2:D])
+        load_block(v_new, vT, 1)
+        for tiles, table, blocks in ((m_new, mT, (0, 1)), (v_new, vT, (2, 3)), (m_new, mT, (2, 3))):
+            for k in blocks:
                 load_block(tiles, table, k)
 
         one = sb("one", [P, 1], F32)
@@ -114,8 +120,8 @@ def tile_attend_glch_adam_kernel(tc, xT, wT, y, wt, xm, mT, vT, offs, out_0, out
                 out=x_codes[:, rows].bitcast(E4M3), scales=x_scales[:, rows],
                 in_=x_bf[:, 2 * h:2 * h + 2, :, :].rearrange("p t m j -> p (t m j)"))
 
-        dw_codes = sb("dw_codes", [P, N + D], U32, tag="m_old0")
-        g_codes, xm_codes = dw_codes[:, 0:N], dw_codes[:, N:N + D]
+        dw_codes = sb("dw_codes", [P, N + D // 2], U32, tag="m_old0")
+        g_codes = dw_codes[:, 0:N]
         g_scales = sb("g_scales", [P, N], U8)
         g_bf = sb("g_bf", [P, N, PACK], BF16)
         for c in range(CHUNKS):
@@ -130,69 +136,92 @@ def tile_attend_glch_adam_kernel(tc, xT, wT, y, wt, xm, mT, vT, offs, out_0, out
                     start=True, stop=True)
             diff = sb("diff%d" % c, [P, PACK, CHUNK], F32)
             nc.vector.tensor_tensor(diff[:], a[:], y_sb[:, :, cols], ALU.subtract)
-            th = sb("th%d" % c, [P, CHUNK, PACK], F32)
-            nc.scalar.activation(th[:], diff[:].rearrange("p t i -> p i t"), ACT.Tanh)
-            nc.gpsimd.tensor_tensor(
-                g_bf[:, cols, :], th[:], wt_wide[:], ALU.mult)
+            if c < CHUNKS - 1:
+                th = sb("th%d" % c, [P, CHUNK, PACK], F32)
+                nc.scalar.activation(th[:], diff[:].rearrange("p t i -> p i t"), ACT.Tanh)
+                nc.gpsimd.tensor_tensor(g_bf[:, cols, :], th[:], wt_wide[:], ALU.mult)
+            else:
+                th = sb("th%d" % c, [P, PACK, CHUNK], F32)
+                nc.scalar.activation(th[:], diff[:], ACT.Tanh)
+                for t in range(PACK):
+                    nc.scalar.activation(g_bf[:, cols, t], th[:, t, :], ACT.Copy, scale=wt_sb[:, t:t + 1])
         nc.vector.quantize_mx(
             out=g_codes.bitcast(E5M2), scales=g_scales[:],
             in_=g_bf[:].rearrange("p i t -> p (i t)"))
 
-        xm_bf = sb("xm_bf", [P, D, PACK], BF16, tag="diff%d" % (CHUNKS - 1))
-        nc.scalar.activation(
-            xm_bf[:].rearrange("p (c i) t -> p c t i", i=4),
-            xm_raw[:].rearrange("p t (c i) -> p c t i", i=4), ACT.Copy)
-        xm_scales = sb("xm_scales", [P, D], U8)
-        nc.vector.quantize_mx(
-            out=xm_codes.bitcast(E4M3), scales=xm_scales[:],
-            in_=xm_bf[:].rearrange("p d t -> p (d t)"))
-
-        dw = []
-        for k in range(BLOCKS):
-            rows = slice(k * P, (k + 1) * P)
-            bank = psum.tile([P, N], F32, name="dw%d" % k)
-            nc.tensor.matmul_mx(
-                out=bank[:],
-                lhsT=xm_codes[:, rows].bitcast(E4M3), lhsT_scale=xm_scales[:, rows],
-                rhs=g_codes.bitcast(E5M2), rhs_scale=g_scales[:],
-                start=True, stop=True)
-            dw.append(bank)
-
-        nv = sb("nv", [P, BLOCKS, N], F32)
+        nv = [sb("nv%d" % k, [P, N], F32) for k in range(BLOCKS)]
         nm = sb("nm", [P, BLOCKS, N], F32)
         sq = sb("sq", [P, BLOCKS, N], F32)
         dw_part = sb("dw_part", [P, BLOCKS, N], F32, tag="x_raw")
-        v_picked = sb("v_picked", [P, BLOCKS, N], F32, tag="y_sb")
+        root = sb("root", [P, BLOCKS, N], F32)
+
+        def gradient(h, cast_tag, codes):
+            xm_bf = sb("xm_bf%d" % h, [P, D // 2, PACK], BF16, tag=cast_tag)
+            nc.scalar.activation(
+                xm_bf[:].rearrange("p (c i) t -> p c t i", i=4),
+                xm_raw[h][:].rearrange("p t (c i) -> p c t i", i=4), ACT.Copy)
+            scales = sb("xm_scales%d" % h, [P, D // 2], U8)
+            nc.vector.quantize_mx(
+                out=codes.bitcast(E4M3), scales=scales[:], in_=xm_bf[:].rearrange("p d t -> p (d t)"))
+            banks = []
+            for b in range(2):
+                rows = slice(b * P, (b + 1) * P)
+                bank = psum.tile([P, N], F32, name="dw%d" % (2 * h + b))
+                nc.tensor.matmul_mx(
+                    out=bank[:],
+                    lhsT=codes[:, rows].bitcast(E4M3), lhsT_scale=scales[:, rows],
+                    rhs=g_codes.bitcast(E5M2), rhs_scale=g_scales[:],
+                    start=True, stop=True)
+                banks.append(bank)
+            return banks
+
+        dw = gradient(0, "diff%d" % (CHUNKS - 1), dw_codes[:, N:N + D // 2])
+
+        v_first = sb("v_first", [P, N], F32, tag="x_bf")
+        v_rest = sb("v_rest", [P, BLOCKS - 1, N], F32, tag="y_sb")
+        v_picked = [v_first[:]] + [v_rest[:, k, :] for k in range(BLOCKS - 1)]
         v_kept = sb("v_kept", [P, BLOCKS, N], F32, tag="w_first")
         m_first = sb("m_first", [P, N], F32)
         m_rest = sb("m_rest", [P, BLOCKS - 1, N], F32, tag="diff%d" % (CHUNKS - 1))
         m_picked = [m_first[:]] + [m_rest[:, k, :] for k in range(BLOCKS - 1)]
         m_kept = [sb("m_kept%d" % k, [P, N], F32, tag="th%d" % k) for k in range(BLOCKS)]
         for k in range(BLOCKS):
-            nc.vector.tensor_copy(v_picked[:, k, :], v_old[k][:].indirect(offsets[:]))
-            nc.scalar.activation(v_kept[:, k, :], v_picked[:, k, :], ACT.Copy, scale=RHO)
+            nc.vector.tensor_copy(v_picked[k], v_old[k][:].indirect(offsets[:]))
+            nc.scalar.activation(v_kept[:, k, :], v_picked[k], ACT.Copy, scale=RHO)
         for k in range(BLOCKS):
             nc.vector.tensor_copy(m_picked[k], m_old[k][:].indirect(offsets[:]))
-        for k in range(BLOCKS):
-            nc.scalar.activation(sq[:, k, :], dw[k][:], ACT.Square, scale=math.sqrt(1.0 - RHO))
-            nc.gpsimd.tensor_tensor(nv[:, k, :], v_kept[:, k, :], sq[:, k, :], ALU.add)
-        for k in range(BLOCKS):
-            nc.scalar.activation(m_kept[k][:], m_picked[k], ACT.Copy, scale=BETA)
-            nc.scalar.activation(dw_part[:, k, :], dw[k][:], ACT.Copy, scale=1.0 - BETA)
-            nc.gpsimd.tensor_tensor(nm[:, k, :], dw_part[:, k, :], m_kept[k][:], ALU.add)
+
+        def scatter_and_store(window, new, out, k):
+            nc.vector.tensor_copy(window[k][:].indirect(offsets[:]), new)
+            nc.sync.dma_start(out[k * P:(k + 1) * P, :], window[k][:])
+
+        for h in range(2):
+            blocks = (2 * h, 2 * h + 1)
+            for k in blocks:
+                nc.scalar.activation(sq[:, k, :], dw[k][:], ACT.Square, scale=math.sqrt(1.0 - RHO))
+                nc.gpsimd.tensor_tensor(nv[k][:], v_kept[:, k, :], sq[:, k, :], ALU.add)
+            for k in blocks:
+                nc.scalar.activation(m_kept[k][:], m_picked[k], ACT.Copy, scale=BETA)
+                nc.scalar.activation(dw_part[:, k, :], dw[k][:], ACT.Copy, scale=1.0 - BETA)
+                nc.gpsimd.tensor_tensor(nm[:, k, :], dw_part[:, k, :], m_kept[k][:], ALU.add)
+            for k in blocks:
+                nc.scalar.activation(root[:, k, :], nv[k][:], ACT.Sqrt)
+            for k in blocks:
+                scatter_and_store(v_new, nv[k][:], out_2, k)
+            if h == 0:
+                late_codes = sb("late_codes", [P, D // 2], U32, tag="nv0")
+                dw.extend(gradient(1, None, late_codes[:]))
+            for k in blocks:
+                scatter_and_store(m_new, nm[:, k, :], out_1, k)
+
         flat = "p k i -> p (k i)"
-        root = sb("root", [P, BLOCKS * N], F32, tag="xm_raw")
         log_den = sb("log_den", [P, BLOCKS * N], F32, tag="y_sb")
         rate = sb("rate", [P, BLOCKS * N], F32, tag="sq")
-        minus_rate = sb("minus_rate", [P, BLOCKS, N], F32, tag="xm_raw")
+        minus_rate = sb("minus_rate", [P, BLOCKS, N], F32, tag="root")
         nw = sb("nw", [P, BLOCKS, N], F32, tag="x_raw")
-        nc.scalar.activation(root[:], nv[:].rearrange(flat), ACT.Sqrt)
-        nc.scalar.activation(log_den[:], root[:], ACT.Ln, bias=eps_col[:], scale=1.0 / LR)
+        nc.scalar.activation(log_den[:], root[:].rearrange(flat), ACT.Ln, bias=eps_col[:], scale=1.0 / LR)
         nc.scalar.activation(rate[:], log_den[:], ACT.Exp, scale=-1.0)
         nc.scalar.activation(minus_rate[:].rearrange(flat), rate[:], ACT.Copy, scale=-1.0)
         for k in range(BLOCKS):
             nc.gpsimd.tensor_tensor(nw[:, k, :], nm[:, k, :], minus_rate[:, k, :], ALU.mult)
-        for tiles, new, out in ((v_new, nv, out_2), (m_new, nm, out_1), (step, nw, out_0)):
-            for k in range(BLOCKS):
-                nc.vector.tensor_copy(tiles[k][:].indirect(offsets[:]), new[:, k, :])
-                nc.sync.dma_start(out[k * P:(k + 1) * P, :], tiles[k][:])
+            scatter_and_store(step, nw[:, k, :], out_0, k)

@@ -24,6 +24,7 @@ CHUNK = 128
 CHUNKS = N // CHUNK
 HALF = T // 2
 FIRST_CUT = 384
+SECOND_CUT = 128
 
 
 def tile_attend_glch_adam_kernel(tc, xT, wT, y, wt, xm, mT, vT, offs, out_0, out_1, out_2):
@@ -43,15 +44,21 @@ def tile_attend_glch_adam_kernel(tc, xT, wT, y, wt, xm, mT, vT, offs, out_0, out
         w_second = [sb("w_second%d" % h, [P, 2, HALF], F32) for h in range(2)]
         for h in range(2):
             nc.sync.dma_start(w_second[h][:], w_rows[1][:, :, h * HALF:(h + 1) * HALF])
-        x_raw = sb("x_raw", [P, PACK, R], F32)
-        nc.sync.dma_start(x_raw[:], xT[0].rearrange("(p j) r -> p j r", j=PACK))
+        x_rows = xT[0].rearrange("(p j) r -> p j r", j=PACK)
+        x_raw = [sb("x_raw%d" % h, [P, PACK, R // 2], F32) for h in range(2)]
+        for h in range(2):
+            nc.sync.dma_start(x_raw[h][:], x_rows[:, :, h * (R // 2):(h + 1) * (R // 2)])
         wt_sb = sb("wt_sb", [P, PACK], F32)
         nc.sync.dma_start(wt_sb[:], wt[0].rearrange("(p t) o -> p (t o)", t=PACK))
-        y_sb = sb("y_sb", [P, PACK, N], F32)
-        xm_rows = xm[0].rearrange("(p t) d -> p t d", t=PACK)
-        xm_raw = [sb("xm_raw%d" % h, [P, PACK, D // 2], F32) for h in range(2)]
         m_old = [sb("m_old%d" % k, [P, T], F32) for k in range(BLOCKS)]
         v_old = [sb("v_old%d" % k, [P, T], F32) for k in range(BLOCKS)]
+        nc.sync.dma_start(v_old[0][:], vT[0:P, :])
+        y_rows = y[0].rearrange("(p t) i -> p t i", t=PACK)
+        y_sb = [sb("y_sb%d" % h, [P, PACK, N // 2], F32) for h in range(2)]
+        for h in range(2):
+            nc.sync.dma_start(y_sb[h][:], y_rows[:, :, h * (N // 2):(h + 1) * (N // 2)])
+        xm_rows = xm[0].rearrange("(p t) d -> p t d", t=PACK)
+        xm_raw = [sb("xm_raw%d" % h, [P, PACK, D // 2], F32) for h in range(2)]
         m_new = [sb("m_new%d" % k, [P, T], F32) for k in range(BLOCKS)]
         v_new = [sb("v_new%d" % k, [P, T], F32) for k in range(BLOCKS)]
         step = [sb("step%d" % k, [P, T], F32) for k in range(BLOCKS)]
@@ -59,19 +66,26 @@ def tile_attend_glch_adam_kernel(tc, xT, wT, y, wt, xm, mT, vT, offs, out_0, out
         def load_block(tiles, table, k):
             nc.sync.dma_start(tiles[k][:], table[k * P:(k + 1) * P, :])
 
-        load_block(v_old, vT, 0)
-        nc.sync.dma_start(y_sb[:], y[0].rearrange("(p t) i -> p t i", t=PACK))
-        nc.sync.dma_start(xm_raw[0][:], xm_rows[:, :, 0:D // 2])
-        for k in range(1, BLOCKS):
-            load_block(v_old, vT, k)
-        for k in range(BLOCKS):
-            load_block(m_old, mT, k)
+        def load_xm(h):
+            nc.sync.dma_start(xm_raw[h][:], xm_rows[:, :, h * (D // 2):(h + 1) * (D // 2)])
+
+        load_block(v_old, vT, 1)
+        load_block(v_old, vT, 2)
+        load_block(v_old, vT, 3)
+        load_xm(0)
+        load_block(m_old, mT, 0)
+        load_block(m_old, mT, 1)
+        load_block(m_old, mT, 2)
+        load_block(m_old, mT, 3)
         load_block(v_new, vT, 0)
-        nc.sync.dma_start(xm_raw[1][:], xm_rows[:, :, D // 2:D])
         load_block(v_new, vT, 1)
-        for tiles, table, blocks in ((m_new, mT, (0, 1)), (v_new, vT, (2, 3)), (m_new, mT, (2, 3))):
-            for k in blocks:
-                load_block(tiles, table, k)
+        load_xm(1)
+        load_block(m_new, mT, 0)
+        load_block(m_new, mT, 1)
+        load_block(v_new, vT, 2)
+        load_block(v_new, vT, 3)
+        load_block(m_new, mT, 2)
+        load_block(m_new, mT, 3)
 
         one = sb("one", [P, 1], F32)
         nc.vector.memset(one[:], 1.0)
@@ -79,8 +93,6 @@ def tile_attend_glch_adam_kernel(tc, xT, wT, y, wt, xm, mT, vT, offs, out_0, out
         nc.scalar.activation(eps_col[:], one[:], ACT.Copy, scale=EPS / LR)
         for k in range(BLOCKS):
             (nc.vector if k % 2 else nc.gpsimd).memset(step[k][:], 0.0)
-        wt_wide = sb("wt_wide", [P, CHUNK, PACK], F32)
-        nc.scalar.activation(wt_wide[:], wt_sb[:].unsqueeze(1).to_broadcast([P, CHUNK, PACK]), ACT.Copy)
 
         w_pairs = [sb("w_pairs%d" % u, [P, T], U32) for u in range(2)]
         w_picked = sb("w_picked", [P, N, 2], U32)
@@ -94,24 +106,23 @@ def tile_attend_glch_adam_kernel(tc, xT, wT, y, wt, xm, mT, vT, offs, out_0, out
         nc.vector.tensor_copy(*pair_views(0, FIRST_CUT, w_first[:, :, FIRST_CUT:T]))
         nc.vector.tensor_copy(w_picked[:, :, 0], w_pairs[0][:].indirect(offsets[:]))
         nc.scalar.activation(*pair_views(1, 0, w_second[0][:]), ACT.Copy)
-        nc.scalar.activation(*pair_views(1, HALF, w_second[1][:, :, 0:HALF // 2]), ACT.Copy)
-        nc.vector.tensor_copy(*pair_views(1, HALF + HALF // 2, w_second[1][:, :, HALF // 2:HALF]))
+        nc.scalar.activation(*pair_views(1, HALF, w_second[1][:, :, 0:SECOND_CUT]), ACT.Copy)
+        nc.vector.tensor_copy(*pair_views(1, HALF + SECOND_CUT, w_second[1][:, :, SECOND_CUT:HALF]))
         nc.vector.tensor_copy(w_picked[:, :, 1], w_pairs[1][:].indirect(offsets[:]))
-        w_codes = sb("w_codes", [P, N], U32)
-        w_scales = sb("w_scales", [P, N], U8)
-        nc.vector.quantize_mx(
-            out=w_codes[:].bitcast(E4M3), scales=w_scales[:],
-            in_=w_picked[:].rearrange("p i u -> p (i u)").bitcast(BF16))
 
         x_bf = sb("x_bf", [P, PACK, P, PACK], BF16)
         for h in range(2):
-            ms = slice(h * (P // 2), (h + 1) * (P // 2))
-            dst = x_bf[:, :, ms, :].rearrange("p t m j -> p m j t")
-            src = x_raw[:].rearrange("p j (m t) -> p m j t", t=PACK)[:, ms, :, :]
+            dst = x_bf[:, :, h * (P // 2):(h + 1) * (P // 2), :].rearrange("p t m j -> p m j t")
+            src = x_raw[h][:].rearrange("p j (m t) -> p m j t", t=PACK)
             if h == 0:
                 nc.scalar.activation(dst, src, ACT.Copy)
             else:
                 nc.vector.tensor_copy(dst, src)
+        w_codes = sb("w_codes", [P, N], U32, tag="x_raw1")
+        w_scales = sb("w_scales", [P, N], U8)
+        nc.vector.quantize_mx(
+            out=w_codes[:].bitcast(E4M3), scales=w_scales[:],
+            in_=w_picked[:].rearrange("p i u -> p (i u)").bitcast(BF16))
         x_codes = sb("x_codes", [P, R], U32)
         x_scales = sb("x_scales", [P, R], U8)
         for h in range(2):
@@ -119,9 +130,10 @@ def tile_attend_glch_adam_kernel(tc, xT, wT, y, wt, xm, mT, vT, offs, out_0, out
             nc.vector.quantize_mx(
                 out=x_codes[:, rows].bitcast(E4M3), scales=x_scales[:, rows],
                 in_=x_bf[:, 2 * h:2 * h + 2, :, :].rearrange("p t m j -> p (t m j)"))
+        wt_wide = sb("wt_wide", [P, CHUNK, PACK], F32)
+        nc.scalar.activation(wt_wide[:], wt_sb[:].unsqueeze(1).to_broadcast([P, CHUNK, PACK]), ACT.Copy)
 
-        dw_codes = sb("dw_codes", [P, N + D // 2], U32, tag="m_old0")
-        g_codes = dw_codes[:, 0:N]
+        g_codes = sb("g_codes", [P, N], U32, tag="m_old0")
         g_scales = sb("g_scales", [P, N], U8)
         g_bf = sb("g_bf", [P, N, PACK], BF16)
         for c in range(CHUNKS):
@@ -135,34 +147,28 @@ def tile_attend_glch_adam_kernel(tc, xT, wT, y, wt, xm, mT, vT, offs, out_0, out
                     rhs=w_codes[:, cols].bitcast(E4M3), rhs_scale=w_scales[:, cols],
                     start=True, stop=True)
             diff = sb("diff%d" % c, [P, PACK, CHUNK], F32)
-            nc.vector.tensor_tensor(diff[:], a[:], y_sb[:, :, cols], ALU.subtract)
-            if c < CHUNKS - 1:
-                th = sb("th%d" % c, [P, CHUNK, PACK], F32)
-                nc.scalar.activation(th[:], diff[:].rearrange("p t i -> p i t"), ACT.Tanh)
-                nc.gpsimd.tensor_tensor(g_bf[:, cols, :], th[:], wt_wide[:], ALU.mult)
-            else:
-                th = sb("th%d" % c, [P, PACK, CHUNK], F32)
-                nc.scalar.activation(th[:], diff[:], ACT.Tanh)
-                for t in range(PACK):
-                    nc.scalar.activation(g_bf[:, cols, t], th[:, t, :], ACT.Copy, scale=wt_sb[:, t:t + 1])
+            nc.vector.tensor_tensor(
+                diff[:], a[:], y_sb[c // 2][:, :, (c % 2) * CHUNK:(c % 2 + 1) * CHUNK], ALU.subtract)
+            th = sb("th%d" % c, [P, CHUNK, PACK], F32)
+            nc.scalar.activation(th[:], diff[:].rearrange("p t i -> p i t"), ACT.Tanh)
+            nc.gpsimd.tensor_tensor(g_bf[:, cols, :], th[:], wt_wide[:], ALU.mult)
         nc.vector.quantize_mx(
-            out=g_codes.bitcast(E5M2), scales=g_scales[:],
+            out=g_codes[:].bitcast(E5M2), scales=g_scales[:],
             in_=g_bf[:].rearrange("p i t -> p (i t)"))
 
         nv = [sb("nv%d" % k, [P, N], F32) for k in range(BLOCKS)]
-        nm = sb("nm", [P, BLOCKS, N], F32)
-        sq = sb("sq", [P, BLOCKS, N], F32)
-        dw_part = sb("dw_part", [P, BLOCKS, N], F32, tag="x_raw")
+        nm = [sb("nm%d" % k, [P, N], F32) for k in range(BLOCKS)]
         root = sb("root", [P, BLOCKS, N], F32)
 
-        def gradient(h, cast_tag, codes):
-            xm_bf = sb("xm_bf%d" % h, [P, D // 2, PACK], BF16, tag=cast_tag)
+        def gradient(h, tag):
+            xm_bf = sb("xm_bf%d" % h, [P, D // 2, PACK], BF16)
             nc.scalar.activation(
                 xm_bf[:].rearrange("p (c i) t -> p c t i", i=4),
                 xm_raw[h][:].rearrange("p t (c i) -> p c t i", i=4), ACT.Copy)
+            codes = sb("xm_codes%d" % h, [P, D // 2], U32, tag=tag)
             scales = sb("xm_scales%d" % h, [P, D // 2], U8)
             nc.vector.quantize_mx(
-                out=codes.bitcast(E4M3), scales=scales[:], in_=xm_bf[:].rearrange("p d t -> p (d t)"))
+                out=codes[:].bitcast(E4M3), scales=scales[:], in_=xm_bf[:].rearrange("p d t -> p (d t)"))
             banks = []
             for b in range(2):
                 rows = slice(b * P, (b + 1) * P)
@@ -170,26 +176,20 @@ def tile_attend_glch_adam_kernel(tc, xT, wT, y, wt, xm, mT, vT, offs, out_0, out
                 nc.tensor.matmul_mx(
                     out=bank[:],
                     lhsT=codes[:, rows].bitcast(E4M3), lhsT_scale=scales[:, rows],
-                    rhs=g_codes.bitcast(E5M2), rhs_scale=g_scales[:],
+                    rhs=g_codes[:].bitcast(E5M2), rhs_scale=g_scales[:],
                     start=True, stop=True)
                 banks.append(bank)
             return banks
 
-        dw = gradient(0, "diff%d" % (CHUNKS - 1), dw_codes[:, N:N + D // 2])
+        dw = gradient(0, "v_old3")
 
-        v_first = sb("v_first", [P, N], F32, tag="x_bf")
-        v_rest = sb("v_rest", [P, BLOCKS - 1, N], F32, tag="y_sb")
-        v_picked = [v_first[:]] + [v_rest[:, k, :] for k in range(BLOCKS - 1)]
-        v_kept = sb("v_kept", [P, BLOCKS, N], F32, tag="w_first")
-        m_first = sb("m_first", [P, N], F32)
-        m_rest = sb("m_rest", [P, BLOCKS - 1, N], F32, tag="diff%d" % (CHUNKS - 1))
-        m_picked = [m_first[:]] + [m_rest[:, k, :] for k in range(BLOCKS - 1)]
-        m_kept = [sb("m_kept%d" % k, [P, N], F32, tag="th%d" % k) for k in range(BLOCKS)]
+        v_kept = [sb("v_kept%d" % k, [P, N], F32) for k in range(BLOCKS)]
+        m_late = sb("m_late", [P, BLOCKS - 1, N], F32, tag="g_bf")
+        m_kept = [sb("m_kept0", [P, N], F32)[:]] + [m_late[:, k, :] for k in range(BLOCKS - 1)]
         for k in range(BLOCKS):
-            nc.vector.tensor_copy(v_picked[k], v_old[k][:].indirect(offsets[:]))
-            nc.scalar.activation(v_kept[:, k, :], v_picked[k], ACT.Copy, scale=RHO)
+            nc.vector.tensor_copy(v_kept[k][:], v_old[k][:].indirect(offsets[:]))
         for k in range(BLOCKS):
-            nc.vector.tensor_copy(m_picked[k], m_old[k][:].indirect(offsets[:]))
+            nc.vector.tensor_copy(m_kept[k], m_old[k][:].indirect(offsets[:]))
 
         def scatter_and_store(window, new, out, k):
             nc.vector.tensor_copy(window[k][:].indirect(offsets[:]), new)
@@ -198,30 +198,26 @@ def tile_attend_glch_adam_kernel(tc, xT, wT, y, wt, xm, mT, vT, offs, out_0, out
         for h in range(2):
             blocks = (2 * h, 2 * h + 1)
             for k in blocks:
-                nc.scalar.activation(sq[:, k, :], dw[k][:], ACT.Square, scale=math.sqrt(1.0 - RHO))
-                nc.gpsimd.tensor_tensor(nv[k][:], v_kept[:, k, :], sq[:, k, :], ALU.add)
+                nc.scalar.activation(v_kept[k][:], v_kept[k][:], ACT.Copy, scale=RHO)
+                nc.scalar.activation(nv[k][:], dw[k][:], ACT.Square, scale=math.sqrt(1.0 - RHO))
+                nc.gpsimd.tensor_tensor(nv[k][:], v_kept[k][:], nv[k][:], ALU.add)
             for k in blocks:
-                nc.scalar.activation(m_kept[k][:], m_picked[k], ACT.Copy, scale=BETA)
-                nc.scalar.activation(dw_part[:, k, :], dw[k][:], ACT.Copy, scale=1.0 - BETA)
-                nc.gpsimd.tensor_tensor(nm[:, k, :], dw_part[:, k, :], m_kept[k][:], ALU.add)
+                nc.scalar.activation(m_kept[k], m_kept[k], ACT.Copy, scale=BETA)
+                nc.scalar.activation(nm[k][:], dw[k][:], ACT.Copy, scale=1.0 - BETA)
+                nc.gpsimd.tensor_tensor(nm[k][:], nm[k][:], m_kept[k], ALU.add)
             for k in blocks:
                 nc.scalar.activation(root[:, k, :], nv[k][:], ACT.Sqrt)
             for k in blocks:
                 scatter_and_store(v_new, nv[k][:], out_2, k)
             if h == 0:
-                late_codes = sb("late_codes", [P, D // 2], U32, tag="nv0")
-                dw.extend(gradient(1, None, late_codes[:]))
+                dw.extend(gradient(1, "nv1"))
             for k in blocks:
-                scatter_and_store(m_new, nm[:, k, :], out_1, k)
+                scatter_and_store(m_new, nm[k][:], out_1, k)
 
-        flat = "p k i -> p (k i)"
-        log_den = sb("log_den", [P, BLOCKS * N], F32, tag="y_sb")
-        rate = sb("rate", [P, BLOCKS * N], F32, tag="sq")
-        minus_rate = sb("minus_rate", [P, BLOCKS, N], F32, tag="root")
-        nw = sb("nw", [P, BLOCKS, N], F32, tag="x_raw")
-        nc.scalar.activation(log_den[:], root[:].rearrange(flat), ACT.Ln, bias=eps_col[:], scale=1.0 / LR)
-        nc.scalar.activation(rate[:], log_den[:], ACT.Exp, scale=-1.0)
-        nc.scalar.activation(minus_rate[:].rearrange(flat), rate[:], ACT.Copy, scale=-1.0)
+        flat = root[:].rearrange("p k i -> p (k i)")
+        nc.scalar.activation(flat, flat, ACT.Ln, bias=eps_col[:], scale=1.0 / LR)
         for k in range(BLOCKS):
-            nc.gpsimd.tensor_tensor(nw[:, k, :], nm[:, k, :], minus_rate[:, k, :], ALU.mult)
-            scatter_and_store(step, nw[:, k, :], out_0, k)
+            nc.scalar.activation(root[:, k, :], root[:, k, :], ACT.Exp, scale=-1.0)
+            nc.scalar.activation(v_kept[k][:], root[:, k, :], ACT.Copy, scale=-1.0)
+            nc.gpsimd.tensor_tensor(m_kept[k], nm[k][:], v_kept[k][:], ALU.mult)
+            scatter_and_store(step, m_kept[k], out_0, k)

@@ -25,6 +25,7 @@ CHUNKS = N // CHUNK
 HALF = T // 2
 FIRST_CUT = 384
 SECOND_CUT = 128
+X_CUT = 36
 
 
 def tile_attend_glch_adam_kernel(tc, xT, wT, y, wt, xm, mT, vT, offs, out_0, out_1, out_2):
@@ -44,15 +45,16 @@ def tile_attend_glch_adam_kernel(tc, xT, wT, y, wt, xm, mT, vT, offs, out_0, out
         w_second = [sb("w_second%d" % h, [P, 2, HALF], F32) for h in range(2)]
         for h in range(2):
             nc.sync.dma_start(w_second[h][:], w_rows[1][:, :, h * HALF:(h + 1) * HALF])
+        m_old = [sb("m_old%d" % k, [P, T], F32) for k in range(BLOCKS)]
+        v_old = [sb("v_old%d" % k, [P, T], F32) for k in range(BLOCKS)]
+        nc.sync.dma_start(v_old[0][:], vT[0:P, :])
         x_rows = xT[0].rearrange("(p j) r -> p j r", j=PACK)
         x_raw = [sb("x_raw%d" % h, [P, PACK, R // 2], F32) for h in range(2)]
         for h in range(2):
             nc.sync.dma_start(x_raw[h][:], x_rows[:, :, h * (R // 2):(h + 1) * (R // 2)])
         wt_sb = sb("wt_sb", [P, PACK], F32)
         nc.sync.dma_start(wt_sb[:], wt[0].rearrange("(p t) o -> p (t o)", t=PACK))
-        m_old = [sb("m_old%d" % k, [P, T], F32) for k in range(BLOCKS)]
-        v_old = [sb("v_old%d" % k, [P, T], F32) for k in range(BLOCKS)]
-        nc.sync.dma_start(v_old[0][:], vT[0:P, :])
+        nc.sync.dma_start(v_old[1][:], vT[P:2 * P, :])
         y_rows = y[0].rearrange("(p t) i -> p t i", t=PACK)
         y_sb = [sb("y_sb%d" % h, [P, PACK, N // 2], F32) for h in range(2)]
         for h in range(2):
@@ -69,11 +71,10 @@ def tile_attend_glch_adam_kernel(tc, xT, wT, y, wt, xm, mT, vT, offs, out_0, out
         def load_xm(h):
             nc.sync.dma_start(xm_raw[h][:], xm_rows[:, :, h * (D // 2):(h + 1) * (D // 2)])
 
-        load_block(v_old, vT, 1)
         load_block(v_old, vT, 2)
         load_block(v_old, vT, 3)
-        load_xm(0)
         load_block(m_old, mT, 0)
+        load_xm(0)
         load_block(m_old, mT, 1)
         load_block(m_old, mT, 2)
         load_block(m_old, mT, 3)
@@ -111,14 +112,14 @@ def tile_attend_glch_adam_kernel(tc, xT, wT, y, wt, xm, mT, vT, offs, out_0, out
         nc.vector.tensor_copy(w_picked[:, :, 1], w_pairs[1][:].indirect(offsets[:]))
 
         x_bf = sb("x_bf", [P, PACK, P, PACK], BF16)
-        for h in range(2):
-            dst = x_bf[:, :, h * (P // 2):(h + 1) * (P // 2), :].rearrange("p t m j -> p m j t")
-            src = x_raw[h][:].rearrange("p j (m t) -> p m j t", t=PACK)
-            if h == 0:
-                nc.scalar.activation(dst, src, ACT.Copy)
-            else:
-                nc.vector.tensor_copy(dst, src)
-        w_codes = sb("w_codes", [P, N], U32, tag="x_raw1")
+        def x_views(h, lo, hi):
+            dst = x_bf[:, :, h * (P // 2) + lo:h * (P // 2) + hi, :].rearrange("p t m j -> p m j t")
+            return dst, x_raw[h][:].rearrange("p j (m t) -> p m j t", t=PACK)[:, lo:hi, :, :]
+
+        nc.scalar.activation(*x_views(0, 0, P // 2), ACT.Copy)
+        nc.scalar.activation(*x_views(1, 0, X_CUT), ACT.Copy)
+        nc.vector.tensor_copy(*x_views(1, X_CUT, P // 2))
+        w_codes = sb("w_codes", [P, N], U32)
         w_scales = sb("w_scales", [P, N], U8)
         nc.vector.quantize_mx(
             out=w_codes[:].bitcast(E4M3), scales=w_scales[:],
@@ -149,9 +150,15 @@ def tile_attend_glch_adam_kernel(tc, xT, wT, y, wt, xm, mT, vT, offs, out_0, out
             diff = sb("diff%d" % c, [P, PACK, CHUNK], F32)
             nc.vector.tensor_tensor(
                 diff[:], a[:], y_sb[c // 2][:, :, (c % 2) * CHUNK:(c % 2 + 1) * CHUNK], ALU.subtract)
-            th = sb("th%d" % c, [P, CHUNK, PACK], F32)
-            nc.scalar.activation(th[:], diff[:].rearrange("p t i -> p i t"), ACT.Tanh)
-            nc.gpsimd.tensor_tensor(g_bf[:, cols, :], th[:], wt_wide[:], ALU.mult)
+            if c < CHUNKS - 1:
+                th = sb("th%d" % c, [P, CHUNK, PACK], F32)
+                nc.scalar.activation(th[:], diff[:].rearrange("p t i -> p i t"), ACT.Tanh)
+                nc.gpsimd.tensor_tensor(g_bf[:, cols, :], th[:], wt_wide[:], ALU.mult)
+            else:
+                th = sb("th%d" % c, [P, PACK, CHUNK], F32)
+                nc.scalar.activation(th[:], diff[:], ACT.Tanh)
+                for t in range(PACK):
+                    nc.scalar.activation(g_bf[:, cols, t], th[:, t, :], ACT.Copy, scale=wt_sb[:, t:t + 1])
         nc.vector.quantize_mx(
             out=g_codes[:].bitcast(E5M2), scales=g_scales[:],
             in_=g_bf[:].rearrange("p i t -> p (i t)"))
@@ -181,15 +188,19 @@ def tile_attend_glch_adam_kernel(tc, xT, wT, y, wt, xm, mT, vT, offs, out_0, out
                 banks.append(bank)
             return banks
 
-        dw = gradient(0, "v_old3")
+        dw = gradient(0, "g_bf")
 
-        v_kept = [sb("v_kept%d" % k, [P, N], F32) for k in range(BLOCKS)]
-        m_late = sb("m_late", [P, BLOCKS - 1, N], F32, tag="g_bf")
-        m_kept = [sb("m_kept0", [P, N], F32)[:]] + [m_late[:, k, :] for k in range(BLOCKS - 1)]
+        v_picked = [sb("v_picked%d" % k, [P, N], F32, tag="x_bf" if k == 1 else None) for k in range(BLOCKS)]
+        v_pairs = [sb("v_pair%d" % h, [P, 2, N], F32, tag=("xm_raw0", "m_old2")[h]) for h in range(2)]
+        v_kept = [v_pairs[k // 2][:, k % 2, :] for k in range(BLOCKS)]
+        m_all = sb("m_all", [P, BLOCKS, N], F32, tag="m_old3")
+        m_kept = [m_all[:, k, :] for k in range(BLOCKS)]
+        m_late = sb("m_late", [P, BLOCKS - 1, N], F32, tag="xm_bf0")
+        m_picked = [sb("m_first", [P, N], F32)[:]] + [m_late[:, k, :] for k in range(BLOCKS - 1)]
         for k in range(BLOCKS):
-            nc.vector.tensor_copy(v_kept[k][:], v_old[k][:].indirect(offsets[:]))
+            nc.vector.tensor_copy(v_picked[k][:], v_old[k][:].indirect(offsets[:]))
         for k in range(BLOCKS):
-            nc.vector.tensor_copy(m_kept[k], m_old[k][:].indirect(offsets[:]))
+            nc.vector.tensor_copy(m_picked[k], m_old[k][:].indirect(offsets[:]))
 
         def scatter_and_store(window, new, out, k):
             nc.vector.tensor_copy(window[k][:].indirect(offsets[:]), new)
@@ -198,11 +209,11 @@ def tile_attend_glch_adam_kernel(tc, xT, wT, y, wt, xm, mT, vT, offs, out_0, out
         for h in range(2):
             blocks = (2 * h, 2 * h + 1)
             for k in blocks:
-                nc.scalar.activation(v_kept[k][:], v_kept[k][:], ACT.Copy, scale=RHO)
+                nc.scalar.activation(v_kept[k], v_picked[k][:], ACT.Copy, scale=RHO)
                 nc.scalar.activation(nv[k][:], dw[k][:], ACT.Square, scale=math.sqrt(1.0 - RHO))
-                nc.gpsimd.tensor_tensor(nv[k][:], v_kept[k][:], nv[k][:], ALU.add)
+                nc.gpsimd.tensor_tensor(nv[k][:], v_kept[k], nv[k][:], ALU.add)
             for k in blocks:
-                nc.scalar.activation(m_kept[k], m_kept[k], ACT.Copy, scale=BETA)
+                nc.scalar.activation(m_kept[k], m_picked[k], ACT.Copy, scale=BETA)
                 nc.scalar.activation(nm[k][:], dw[k][:], ACT.Copy, scale=1.0 - BETA)
                 nc.gpsimd.tensor_tensor(nm[k][:], nm[k][:], m_kept[k], ALU.add)
             for k in blocks:
@@ -218,6 +229,6 @@ def tile_attend_glch_adam_kernel(tc, xT, wT, y, wt, xm, mT, vT, offs, out_0, out
         nc.scalar.activation(flat, flat, ACT.Ln, bias=eps_col[:], scale=1.0 / LR)
         for k in range(BLOCKS):
             nc.scalar.activation(root[:, k, :], root[:, k, :], ACT.Exp, scale=-1.0)
-            nc.scalar.activation(v_kept[k][:], root[:, k, :], ACT.Copy, scale=-1.0)
-            nc.gpsimd.tensor_tensor(m_kept[k], nm[k][:], v_kept[k][:], ALU.mult)
+            nc.scalar.activation(v_kept[k], root[:, k, :], ACT.Copy, scale=-1.0)
+            nc.gpsimd.tensor_tensor(m_kept[k], nm[k][:], v_kept[k], ALU.mult)
             scatter_and_store(step, m_kept[k], out_0, k)

@@ -23,9 +23,8 @@ BLOCKS = D // P
 CHUNK = 128
 CHUNKS = N // CHUNK
 HALF = T // 2
-FIRST_CUT = 384
 SECOND_CUT = 128
-X_CUT = 36
+X_CUT = 28
 
 
 def tile_attend_glch_adam_kernel(tc, xT, wT, y, wt, xm, mT, vT, offs, out_0, out_1, out_2):
@@ -38,16 +37,17 @@ def tile_attend_glch_adam_kernel(tc, xT, wT, y, wt, xm, mT, vT, offs, out_0, out
             return keep.tile(shape, dtype, name=name, tag=tag or name, align_bytes=64)
 
         w_rows = wT.rearrange("(p u e) t -> u p e t", u=2, e=2)
-        w_first = sb("w_first", [P, 2, T], F32)
-        nc.sync.dma_start(w_first[:], w_rows[0])
+        w_first = [sb("w_first%d" % h, [P, 2, HALF], F32) for h in range(2)]
+        nc.sync.dma_start(w_first[0][:], w_rows[0][:, :, 0:HALF])
         offsets = keep.tile([P, N // 16], U16, name="offsets")
         nc.sync.dma_start(offsets[:], offs)
-        w_second = [sb("w_second%d" % h, [P, 2, HALF], F32) for h in range(2)]
-        for h in range(2):
-            nc.sync.dma_start(w_second[h][:], w_rows[1][:, :, h * HALF:(h + 1) * HALF])
+        nc.sync.dma_start(w_first[1][:], w_rows[0][:, :, HALF:T])
         m_old = [sb("m_old%d" % k, [P, T], F32) for k in range(BLOCKS)]
         v_old = [sb("v_old%d" % k, [P, T], F32) for k in range(BLOCKS)]
         nc.sync.dma_start(v_old[0][:], vT[0:P, :])
+        w_second = [sb("w_second%d" % h, [P, 2, HALF], F32) for h in range(2)]
+        for h in range(2):
+            nc.sync.dma_start(w_second[h][:], w_rows[1][:, :, h * HALF:(h + 1) * HALF])
         x_rows = xT[0].rearrange("(p j) r -> p j r", j=PACK)
         x_raw = [sb("x_raw%d" % h, [P, PACK, R // 2], F32) for h in range(2)]
         for h in range(2):
@@ -103,8 +103,9 @@ def tile_attend_glch_adam_kernel(tc, xT, wT, y, wt, xm, mT, vT, offs, out_0, out
             dst = w_pairs[u][:, lo:lo + width].bitcast(BF16).rearrange("p (c i e) -> p c e i", i=4, e=2)
             return dst, src.rearrange("p e (c i) -> p c e i", i=4)
 
-        nc.scalar.activation(*pair_views(0, 0, w_first[:, :, 0:FIRST_CUT]), ACT.Copy)
-        nc.vector.tensor_copy(*pair_views(0, FIRST_CUT, w_first[:, :, FIRST_CUT:T]))
+        nc.scalar.activation(*pair_views(0, 0, w_first[0][:]), ACT.Copy)
+        nc.scalar.activation(*pair_views(0, HALF, w_first[1][:, :, 0:SECOND_CUT]), ACT.Copy)
+        nc.vector.tensor_copy(*pair_views(0, HALF + SECOND_CUT, w_first[1][:, :, SECOND_CUT:HALF]))
         nc.vector.tensor_copy(w_picked[:, :, 0], w_pairs[0][:].indirect(offsets[:]))
         nc.scalar.activation(*pair_views(1, 0, w_second[0][:]), ACT.Copy)
         nc.scalar.activation(*pair_views(1, HALF, w_second[1][:, :, 0:SECOND_CUT]), ACT.Copy)
@@ -230,5 +231,5 @@ def tile_attend_glch_adam_kernel(tc, xT, wT, y, wt, xm, mT, vT, offs, out_0, out
         for k in range(BLOCKS):
             nc.scalar.activation(root[:, k, :], root[:, k, :], ACT.Exp, scale=-1.0)
             nc.scalar.activation(v_kept[k], root[:, k, :], ACT.Copy, scale=-1.0)
-            nc.gpsimd.tensor_tensor(m_kept[k], nm[k][:], v_kept[k], ALU.mult)
-            scatter_and_store(step, m_kept[k], out_0, k)
+            nc.vector.tensor_tensor(step[k][:].indirect(offsets[:]), nm[k][:], v_kept[k], ALU.mult)
+            nc.sync.dma_start(out_0[k * P:(k + 1) * P, :], step[k][:])

@@ -2,6 +2,7 @@ import math
 from contextlib import ExitStack
 
 import concourse.mybir as mybir
+from concourse.masks import make_identity
 
 N, T, D, R = 512, 1024, 512, 512
 LR, BETA, RHO, EPS = 0.1, 0.5, 0.9, 0.001
@@ -24,7 +25,7 @@ CHUNK = 128
 CHUNKS = N // CHUNK
 HALF = T // 2
 SECOND_CUT = 128
-X_CUT = 28
+X_CUT = 12
 
 
 def tile_attend_glch_adam_kernel(tc, xT, wT, y, wt, xm, mT, vT, offs, out_0, out_1, out_2):
@@ -79,11 +80,11 @@ def tile_attend_glch_adam_kernel(tc, xT, wT, y, wt, xm, mT, vT, offs, out_0, out
         load_block(m_old, mT, 2)
         load_block(m_old, mT, 3)
         load_block(v_new, vT, 0)
-        load_block(v_new, vT, 1)
         load_xm(1)
+        load_block(v_new, vT, 2)
+        load_block(v_new, vT, 1)
         load_block(m_new, mT, 0)
         load_block(m_new, mT, 1)
-        load_block(v_new, vT, 2)
         load_block(v_new, vT, 3)
         load_block(m_new, mT, 2)
         load_block(m_new, mT, 3)
@@ -94,6 +95,9 @@ def tile_attend_glch_adam_kernel(tc, xT, wT, y, wt, xm, mT, vT, offs, out_0, out
         nc.scalar.activation(eps_col[:], one[:], ACT.Copy, scale=EPS / LR)
         for k in range(BLOCKS):
             (nc.vector if k % 2 else nc.gpsimd).memset(step[k][:], 0.0)
+
+        ident = sb("ident", [P, P], F32)
+        make_identity(nc, ident[:])
 
         w_pairs = [sb("w_pairs%d" % u, [P, T], U32) for u in range(2)]
         w_picked = sb("w_picked", [P, N, 2], U32)
@@ -120,7 +124,7 @@ def tile_attend_glch_adam_kernel(tc, xT, wT, y, wt, xm, mT, vT, offs, out_0, out
         nc.scalar.activation(*x_views(0, 0, P // 2), ACT.Copy)
         nc.scalar.activation(*x_views(1, 0, X_CUT), ACT.Copy)
         nc.vector.tensor_copy(*x_views(1, X_CUT, P // 2))
-        w_codes = sb("w_codes", [P, N], U32)
+        w_codes = sb("w_codes", [P, N], U32, tag="x_raw1")
         w_scales = sb("w_scales", [P, N], U8)
         nc.vector.quantize_mx(
             out=w_codes[:].bitcast(E4M3), scales=w_scales[:],
@@ -192,10 +196,8 @@ def tile_attend_glch_adam_kernel(tc, xT, wT, y, wt, xm, mT, vT, offs, out_0, out
         dw = gradient(0, "g_bf")
 
         v_picked = [sb("v_picked%d" % k, [P, N], F32, tag="x_bf" if k == 1 else None) for k in range(BLOCKS)]
-        v_pairs = [sb("v_pair%d" % h, [P, 2, N], F32, tag=("xm_raw0", "m_old2")[h]) for h in range(2)]
-        v_kept = [v_pairs[k // 2][:, k % 2, :] for k in range(BLOCKS)]
-        m_all = sb("m_all", [P, BLOCKS, N], F32, tag="m_old3")
-        m_kept = [m_all[:, k, :] for k in range(BLOCKS)]
+        v_kept = sb("v_kept", [P, 2, N], F32, tag="xm_raw0")
+        minus_nm = sb("minus_nm", [P, BLOCKS, N], F32)
         m_late = sb("m_late", [P, BLOCKS - 1, N], F32, tag="xm_bf0")
         m_picked = [sb("m_first", [P, N], F32)[:]] + [m_late[:, k, :] for k in range(BLOCKS - 1)]
         for k in range(BLOCKS):
@@ -207,22 +209,41 @@ def tile_attend_glch_adam_kernel(tc, xT, wT, y, wt, xm, mT, vT, offs, out_0, out
             nc.vector.tensor_copy(window[k][:].indirect(offsets[:]), new)
             nc.sync.dma_start(out[k * P:(k + 1) * P, :], window[k][:])
 
+        def add_on_tensor(name, first, second, scale, which):
+            turned = psum.tile([P, PACK, P], F32, name=name + "_turned", tag="a%d" % which)
+            for j in range(PACK):
+                cols = slice(j * P, (j + 1) * P)
+                nc.tensor.matmul(turned[:, j, :], first[:, cols], ident[:], start=True, stop=False, is_transpose=True)
+                nc.tensor.matmul(turned[:, j, :], second[:, cols], ident[:], start=False, stop=True, is_transpose=True)
+            staged = sb(name + "_staged", [P, PACK, P], F32, tag="th%d" % which)
+            nc.scalar.activation(staged[:], turned[:], ACT.Copy, scale=scale)
+            total = psum.tile([P, N], F32, name=name + "_total", tag="a%d" % (2 + which))
+            for j in range(PACK):
+                nc.tensor.transpose(total[:, j * P:(j + 1) * P], staged[:, j, :], ident[:])
+            return total
+
         for h in range(2):
             blocks = (2 * h, 2 * h + 1)
             for k in blocks:
-                nc.scalar.activation(v_kept[k], v_picked[k][:], ACT.Copy, scale=RHO)
-                nc.scalar.activation(nv[k][:], dw[k][:], ACT.Square, scale=math.sqrt(1.0 - RHO))
-                nc.gpsimd.tensor_tensor(nv[k][:], v_kept[k], nv[k][:], ALU.add)
+                if h == 0:
+                    nc.scalar.activation(v_kept[:, k, :], v_picked[k][:], ACT.Copy, scale=RHO)
+                    nc.scalar.activation(nv[k][:], dw[k][:], ACT.Square, scale=math.sqrt(1.0 - RHO))
+                    nc.gpsimd.tensor_tensor(nv[k][:], v_kept[:, k, :], nv[k][:], ALU.add)
+                else:
+                    nc.scalar.activation(nv[k][:], dw[k][:], ACT.Square, scale=math.sqrt((1.0 - RHO) / RHO))
+                    total = add_on_tensor("nv%d" % k, v_picked[k][:], nv[k][:], RHO, k % 2)
+                    nc.scalar.activation(nv[k][:], total[:], ACT.Copy)
+            if h == 0:
+                dw.extend(gradient(1, None))
             for k in blocks:
-                nc.scalar.activation(m_kept[k], m_picked[k], ACT.Copy, scale=BETA)
-                nc.scalar.activation(nm[k][:], dw[k][:], ACT.Copy, scale=1.0 - BETA)
-                nc.gpsimd.tensor_tensor(nm[k][:], nm[k][:], m_kept[k], ALU.add)
+                nc.scalar.activation(nm[k][:], dw[k][:], ACT.Copy, scale=(1.0 - BETA) / BETA)
+                total = add_on_tensor("nm%d" % k, m_picked[k], nm[k][:], BETA, k % 2)
+                nc.scalar.activation(nm[k][:], total[:], ACT.Copy)
+                nc.scalar.activation(minus_nm[:, k, :], total[:], ACT.Copy, scale=-1.0)
             for k in blocks:
                 nc.scalar.activation(root[:, k, :], nv[k][:], ACT.Sqrt)
             for k in blocks:
                 scatter_and_store(v_new, nv[k][:], out_2, k)
-            if h == 0:
-                dw.extend(gradient(1, "nv1"))
             for k in blocks:
                 scatter_and_store(m_new, nm[k][:], out_1, k)
 
@@ -230,6 +251,5 @@ def tile_attend_glch_adam_kernel(tc, xT, wT, y, wt, xm, mT, vT, offs, out_0, out
         nc.scalar.activation(flat, flat, ACT.Ln, bias=eps_col[:], scale=1.0 / LR)
         for k in range(BLOCKS):
             nc.scalar.activation(root[:, k, :], root[:, k, :], ACT.Exp, scale=-1.0)
-            nc.scalar.activation(v_kept[k], root[:, k, :], ACT.Copy, scale=-1.0)
-            nc.vector.tensor_tensor(step[k][:].indirect(offsets[:]), nm[k][:], v_kept[k], ALU.mult)
+            nc.vector.tensor_tensor(step[k][:].indirect(offsets[:]), minus_nm[:, k, :], root[:, k, :], ALU.mult)
             nc.sync.dma_start(out_0[k * P:(k + 1) * P, :], step[k][:])

@@ -75,15 +75,15 @@ def tile_attend_glch_adam_kernel(tc, xT, wT, y, wt, xm, mT, vT, offs, out_0, out
         load_block(v_old, vT, 2)
         load_block(v_old, vT, 3)
         load_block(m_old, mT, 0)
-        load_xm(0)
         load_block(m_old, mT, 1)
+        load_xm(0)
+        load_xm(1)
         load_block(m_old, mT, 2)
         load_block(m_old, mT, 3)
         load_block(v_new, vT, 0)
-        load_xm(1)
-        load_block(v_new, vT, 2)
         load_block(v_new, vT, 1)
         load_block(m_new, mT, 0)
+        load_block(v_new, vT, 2)
         load_block(m_new, mT, 1)
         load_block(v_new, vT, 3)
         load_block(m_new, mT, 2)
@@ -139,9 +139,10 @@ def tile_attend_glch_adam_kernel(tc, xT, wT, y, wt, xm, mT, vT, offs, out_0, out
         wt_wide = sb("wt_wide", [P, CHUNK, PACK], F32)
         nc.scalar.activation(wt_wide[:], wt_sb[:].unsqueeze(1).to_broadcast([P, CHUNK, PACK]), ACT.Copy)
 
-        g_codes = sb("g_codes", [P, N], U32, tag="m_old0")
+        g_codes = sb("g_codes", [P, N], U32, tag="m_old1")
         g_scales = sb("g_scales", [P, N], U8)
         g_bf = sb("g_bf", [P, N, PACK], BF16)
+        diffs = [sb("diff%d" % c, [P, PACK, CHUNK], F32) for c in range(CHUNKS)]
         for c in range(CHUNKS):
             cols = slice(c * CHUNK, (c + 1) * CHUNK)
             a = psum.tile([P, PACK, CHUNK], F32, name="a%d" % c)
@@ -152,11 +153,18 @@ def tile_attend_glch_adam_kernel(tc, xT, wT, y, wt, xm, mT, vT, offs, out_0, out
                     lhsT=x_codes[:, rows].bitcast(E4M3), lhsT_scale=x_scales[:, rows],
                     rhs=w_codes[:, cols].bitcast(E4M3), rhs_scale=w_scales[:, cols],
                     start=True, stop=True)
-            diff = sb("diff%d" % c, [P, PACK, CHUNK], F32)
-            nc.vector.tensor_tensor(
-                diff[:], a[:], y_sb[c // 2][:, :, (c % 2) * CHUNK:(c % 2 + 1) * CHUNK], ALU.subtract)
+            diff = diffs[c]
+            y_part = y_sb[c // 2][:, :, (c % 2) * CHUNK:(c % 2 + 1) * CHUNK]
+            if c == 0:
+                nc.scalar.activation(diff[:], a[:], ACT.Copy)
+                nc.gpsimd.tensor_tensor(diff[:], diff[:], y_part, ALU.subtract)
+            else:
+                nc.vector.tensor_tensor(diff[:], a[:], y_part, ALU.subtract)
+        for c in (1, 0, 2, 3):
+            cols = slice(c * CHUNK, (c + 1) * CHUNK)
+            diff = diffs[c]
             if c < CHUNKS - 1:
-                th = sb("th%d" % c, [P, CHUNK, PACK], F32)
+                th = sb("th%d" % c, [P, CHUNK, PACK], F32, tag="diff1" if c == 0 else None)
                 nc.scalar.activation(th[:], diff[:].rearrange("p t i -> p i t"), ACT.Tanh)
                 nc.gpsimd.tensor_tensor(g_bf[:, cols, :], th[:], wt_wide[:], ALU.mult)
             else:
@@ -173,7 +181,7 @@ def tile_attend_glch_adam_kernel(tc, xT, wT, y, wt, xm, mT, vT, offs, out_0, out
         root = sb("root", [P, BLOCKS, N], F32)
 
         def gradient(h, tag):
-            xm_bf = sb("xm_bf%d" % h, [P, D // 2, PACK], BF16)
+            xm_bf = sb("xm_bf%d" % h, [P, D // 2, PACK], BF16, tag=(None, "m_old3")[h])
             nc.scalar.activation(
                 xm_bf[:].rearrange("p (c i) t -> p c t i", i=4),
                 xm_raw[h][:].rearrange("p t (c i) -> p c t i", i=4), ACT.Copy)
@@ -193,20 +201,23 @@ def tile_attend_glch_adam_kernel(tc, xT, wT, y, wt, xm, mT, vT, offs, out_0, out
                 banks.append(bank)
             return banks
 
-        dw = gradient(0, "g_bf")
+        dw = gradient(0, None)
 
         v_picked = [sb("v_picked%d" % k, [P, N], F32, tag="x_bf" if k == 1 else None) for k in range(BLOCKS)]
-        v_kept = sb("v_kept", [P, 2, N], F32, tag="xm_raw0")
+        v_early = sb("v_early", [P, 2, N], F32, tag="xm_raw0")
+        late = sb("late", [P, 2 + BLOCKS, N], F32, tag="xm_raw1")
+        v_kept = [v_early[:, 0, :], v_early[:, 1, :], late[:, 0, :], late[:, 1, :]]
+        m_kept = [late[:, 2 + k, :] for k in range(BLOCKS)]
         minus_nm = sb("minus_nm", [P, BLOCKS, N], F32)
-        m_late = sb("m_late", [P, BLOCKS - 1, N], F32, tag="xm_bf0")
-        m_picked = [sb("m_first", [P, N], F32)[:]] + [m_late[:, k, :] for k in range(BLOCKS - 1)]
+        m_pairs = [sb("m_pair%d" % h, [P, 2, N], F32, tag=None) for h in range(2)]
+        m_picked = [m_pairs[k // 2][:, k % 2, :] for k in range(BLOCKS)]
         for k in range(BLOCKS):
             nc.vector.tensor_copy(v_picked[k][:], v_old[k][:].indirect(offsets[:]))
         for k in range(BLOCKS):
             nc.vector.tensor_copy(m_picked[k], m_old[k][:].indirect(offsets[:]))
 
-        def scatter_and_store(window, new, out, k):
-            nc.vector.tensor_copy(window[k][:].indirect(offsets[:]), new)
+        def scatter_and_store(window, first, second, op, out, k):
+            nc.vector.tensor_tensor(window[k][:].indirect(offsets[:]), first, second, op)
             nc.sync.dma_start(out[k * P:(k + 1) * P, :], window[k][:])
 
         def add_on_tensor(name, first, second, scale, which):
@@ -222,34 +233,37 @@ def tile_attend_glch_adam_kernel(tc, xT, wT, y, wt, xm, mT, vT, offs, out_0, out
                 nc.tensor.transpose(total[:, j * P:(j + 1) * P], staged[:, j, :], ident[:])
             return total
 
+        def root_of_nv(k):
+            total = add_on_tensor("nv%d" % k, v_kept[k], nv[k][:], 1.0, k % 2)
+            nc.scalar.activation(root[:, k, :], total[:], ACT.Sqrt)
+
+        def negated_nm(k):
+            total = add_on_tensor("nm%d" % k, m_kept[k], nm[k][:], -1.0, k % 2)
+            nc.scalar.activation(minus_nm[:, k, :], total[:], ACT.Copy)
+
         for h in range(2):
             blocks = (2 * h, 2 * h + 1)
             for k in blocks:
-                if h == 0:
-                    nc.scalar.activation(v_kept[:, k, :], v_picked[k][:], ACT.Copy, scale=RHO)
-                    nc.scalar.activation(nv[k][:], dw[k][:], ACT.Square, scale=math.sqrt(1.0 - RHO))
-                    nc.gpsimd.tensor_tensor(nv[k][:], v_kept[:, k, :], nv[k][:], ALU.add)
-                else:
-                    nc.scalar.activation(nv[k][:], dw[k][:], ACT.Square, scale=math.sqrt((1.0 - RHO) / RHO))
-                    total = add_on_tensor("nv%d" % k, v_picked[k][:], nv[k][:], RHO, k % 2)
-                    nc.scalar.activation(nv[k][:], total[:], ACT.Copy)
+                nc.scalar.activation(v_kept[k], v_picked[k][:], ACT.Copy, scale=RHO)
+                nc.scalar.activation(nv[k][:], dw[k][:], ACT.Square, scale=math.sqrt(1.0 - RHO))
+                scatter_and_store(v_new, v_kept[k], nv[k][:], ALU.add, out_2, k)
             if h == 0:
                 dw.extend(gradient(1, None))
             for k in blocks:
-                nc.scalar.activation(nm[k][:], dw[k][:], ACT.Copy, scale=(1.0 - BETA) / BETA)
-                total = add_on_tensor("nm%d" % k, m_picked[k], nm[k][:], BETA, k % 2)
-                nc.scalar.activation(nm[k][:], total[:], ACT.Copy)
-                nc.scalar.activation(minus_nm[:, k, :], total[:], ACT.Copy, scale=-1.0)
+                root_of_nv(k)
             for k in blocks:
-                nc.scalar.activation(root[:, k, :], nv[k][:], ACT.Sqrt)
-            for k in blocks:
-                scatter_and_store(v_new, nv[k][:], out_2, k)
-            for k in blocks:
-                scatter_and_store(m_new, nm[k][:], out_1, k)
+                nc.scalar.activation(m_kept[k], m_picked[k], ACT.Copy, scale=BETA)
+                nc.scalar.activation(nm[k][:], dw[k][:], ACT.Copy, scale=1.0 - BETA)
+                scatter_and_store(m_new, m_kept[k], nm[k][:], ALU.add, out_1, k)
+            if h == 0:
+                for k in blocks:
+                    negated_nm(k)
 
         flat = root[:].rearrange("p k i -> p (k i)")
         nc.scalar.activation(flat, flat, ACT.Ln, bias=eps_col[:], scale=1.0 / LR)
         for k in range(BLOCKS):
             nc.scalar.activation(root[:, k, :], root[:, k, :], ACT.Exp, scale=-1.0)
-            nc.vector.tensor_tensor(step[k][:].indirect(offsets[:]), minus_nm[:, k, :], root[:, k, :], ALU.mult)
-            nc.sync.dma_start(out_0[k * P:(k + 1) * P, :], step[k][:])
+        for k in range(BLOCKS):
+            if k >= 2:
+                negated_nm(k)
+            scatter_and_store(step, minus_nm[:, k, :], root[:, k, :], ALU.mult, out_0, k)

@@ -77,10 +77,10 @@ def tile_attend_glch_adam_kernel(tc, xT, wT, y, wt, xm, mT, vT, offs, out_0, out
         load_block(m_old, mT, 0)
         load_block(m_old, mT, 1)
         load_xm(0)
-        load_xm(1)
         load_block(m_old, mT, 2)
         load_block(m_old, mT, 3)
         load_block(v_new, vT, 0)
+        load_xm(1)
         load_block(v_new, vT, 1)
         load_block(m_new, mT, 0)
         load_block(v_new, vT, 2)
@@ -181,7 +181,7 @@ def tile_attend_glch_adam_kernel(tc, xT, wT, y, wt, xm, mT, vT, offs, out_0, out
         root = sb("root", [P, BLOCKS, N], F32)
 
         def gradient(h, tag):
-            xm_bf = sb("xm_bf%d" % h, [P, D // 2, PACK], BF16, tag=(None, "m_old3")[h])
+            xm_bf = sb("xm_bf%d" % h, [P, D // 2, PACK], BF16)
             nc.scalar.activation(
                 xm_bf[:].rearrange("p (c i) t -> p c t i", i=4),
                 xm_raw[h][:].rearrange("p t (c i) -> p c t i", i=4), ACT.Copy)
@@ -203,14 +203,14 @@ def tile_attend_glch_adam_kernel(tc, xT, wT, y, wt, xm, mT, vT, offs, out_0, out
 
         dw = gradient(0, None)
 
-        v_picked = [sb("v_picked%d" % k, [P, N], F32, tag="x_bf" if k == 1 else None) for k in range(BLOCKS)]
-        v_early = sb("v_early", [P, 2, N], F32, tag="xm_raw0")
+        v_picked = [sb("v_picked%d" % k, [P, N], F32, tag=None) for k in range(BLOCKS)]
+        after_cast = sb("after_cast", [P, 4, N], F32, tag="xm_raw0")
         late = sb("late", [P, 2 + BLOCKS, N], F32, tag="xm_raw1")
-        v_kept = [v_early[:, 0, :], v_early[:, 1, :], late[:, 0, :], late[:, 1, :]]
+        v_kept = [after_cast[:, 0, :], after_cast[:, 1, :], late[:, 0, :], late[:, 1, :]]
         m_kept = [late[:, 2 + k, :] for k in range(BLOCKS)]
         minus_nm = sb("minus_nm", [P, BLOCKS, N], F32)
-        m_pairs = [sb("m_pair%d" % h, [P, 2, N], F32, tag=None) for h in range(2)]
-        m_picked = [m_pairs[k // 2][:, k % 2, :] for k in range(BLOCKS)]
+        m_early = sb("m_early", [P, 2, N], F32)
+        m_picked = [m_early[:, 0, :], m_early[:, 1, :], after_cast[:, 2, :], after_cast[:, 3, :]]
         for k in range(BLOCKS):
             nc.vector.tensor_copy(v_picked[k][:], v_old[k][:].indirect(offsets[:]))
         for k in range(BLOCKS):

@@ -79,13 +79,12 @@ def tile_attend_glch_adam_kernel(tc, xT, wT, y, wt, xm, mT, vT, offs, out_0, out
         load_xm(0)
         load_block(m_old, mT, 2)
         load_block(m_old, mT, 3)
-        load_block(v_new, vT, 0)
         load_xm(1)
         load_block(v_new, vT, 1)
-        load_block(m_new, mT, 0)
         load_block(v_new, vT, 2)
-        load_block(m_new, mT, 1)
         load_block(v_new, vT, 3)
+        load_block(m_new, mT, 0)
+        load_block(m_new, mT, 1)
         load_block(m_new, mT, 2)
         load_block(m_new, mT, 3)
 
@@ -96,6 +95,8 @@ def tile_attend_glch_adam_kernel(tc, xT, wT, y, wt, xm, mT, vT, offs, out_0, out
         for k in range(BLOCKS):
             (nc.vector if k % 2 else nc.gpsimd).memset(step[k][:], 0.0)
 
+        minus_one = sb("minus_one", [P, N], F32)
+        nc.gpsimd.memset(minus_one[:], -1.0)
         ident = sb("ident", [P, P], F32)
         make_identity(nc, ident[:])
 
@@ -115,6 +116,8 @@ def tile_attend_glch_adam_kernel(tc, xT, wT, y, wt, xm, mT, vT, offs, out_0, out
         nc.scalar.activation(*pair_views(1, HALF, w_second[1][:, :, 0:SECOND_CUT]), ACT.Copy)
         nc.vector.tensor_copy(*pair_views(1, HALF + SECOND_CUT, w_second[1][:, :, SECOND_CUT:HALF]))
         nc.vector.tensor_copy(w_picked[:, :, 1], w_pairs[1][:].indirect(offsets[:]))
+
+        nc.scalar.activation(v_new[0][:], v_old[0][:], ACT.Copy)
 
         x_bf = sb("x_bf", [P, PACK, P, PACK], BF16)
         def x_views(h, lo, hi):
@@ -145,7 +148,7 @@ def tile_attend_glch_adam_kernel(tc, xT, wT, y, wt, xm, mT, vT, offs, out_0, out
         diffs = [sb("diff%d" % c, [P, PACK, CHUNK], F32) for c in range(CHUNKS)]
         for c in range(CHUNKS):
             cols = slice(c * CHUNK, (c + 1) * CHUNK)
-            a = psum.tile([P, PACK, CHUNK], F32, name="a%d" % c)
+            a = psum.tile([P, PACK, CHUNK], F32, name="a%d" % c)[:]
             for t in range(PACK):
                 rows = slice(t * P, (t + 1) * P)
                 nc.tensor.matmul_mx(
@@ -156,10 +159,10 @@ def tile_attend_glch_adam_kernel(tc, xT, wT, y, wt, xm, mT, vT, offs, out_0, out
             diff = diffs[c]
             y_part = y_sb[c // 2][:, :, (c % 2) * CHUNK:(c % 2 + 1) * CHUNK]
             if c == 0:
-                nc.scalar.activation(diff[:], a[:], ACT.Copy)
+                nc.scalar.activation(diff[:], a, ACT.Copy)
                 nc.gpsimd.tensor_tensor(diff[:], diff[:], y_part, ALU.subtract)
             else:
-                nc.vector.tensor_tensor(diff[:], a[:], y_part, ALU.subtract)
+                nc.vector.tensor_tensor(diff[:], a, y_part, ALU.subtract)
         for c in (1, 0, 2, 3):
             cols = slice(c * CHUNK, (c + 1) * CHUNK)
             diff = diffs[c]
@@ -176,8 +179,7 @@ def tile_attend_glch_adam_kernel(tc, xT, wT, y, wt, xm, mT, vT, offs, out_0, out
             out=g_codes[:].bitcast(E5M2), scales=g_scales[:],
             in_=g_bf[:].rearrange("p i t -> p (i t)"))
 
-        nv = [sb("nv%d" % k, [P, N], F32) for k in range(BLOCKS)]
-        nm = [sb("nm%d" % k, [P, N], F32) for k in range(BLOCKS)]
+        dw_sb = [sb("dw_sb%d" % k, [P, N], F32) for k in range(BLOCKS)]
         root = sb("root", [P, BLOCKS, N], F32)
 
         def gradient(h, tag):
@@ -205,9 +207,9 @@ def tile_attend_glch_adam_kernel(tc, xT, wT, y, wt, xm, mT, vT, offs, out_0, out
 
         v_picked = [sb("v_picked%d" % k, [P, N], F32, tag=None) for k in range(BLOCKS)]
         after_cast = sb("after_cast", [P, 4, N], F32, tag="xm_raw0")
-        late = sb("late", [P, 2 + BLOCKS, N], F32, tag="xm_raw1")
+        late = sb("late", [P, 3, N], F32, tag="xm_raw1")
+        nv = [late[:, 2, :] if k == 1 else sb("nv%d" % k, [P, N], F32)[:] for k in range(BLOCKS)]
         v_kept = [after_cast[:, 0, :], after_cast[:, 1, :], late[:, 0, :], late[:, 1, :]]
-        m_kept = [late[:, 2 + k, :] for k in range(BLOCKS)]
         minus_nm = sb("minus_nm", [P, BLOCKS, N], F32)
         m_early = sb("m_early", [P, 2, N], F32)
         m_picked = [m_early[:, 0, :], m_early[:, 1, :], after_cast[:, 2, :], after_cast[:, 3, :]]
@@ -220,50 +222,44 @@ def tile_attend_glch_adam_kernel(tc, xT, wT, y, wt, xm, mT, vT, offs, out_0, out
             nc.vector.tensor_tensor(window[k][:].indirect(offsets[:]), first, second, op)
             nc.sync.dma_start(out[k * P:(k + 1) * P, :], window[k][:])
 
-        def add_on_tensor(name, first, second, scale, which):
-            turned = psum.tile([P, PACK, P], F32, name=name + "_turned", tag="a%d" % which)
+        def add_turned(turned, first, second):
             for j in range(PACK):
                 cols = slice(j * P, (j + 1) * P)
-                nc.tensor.matmul(turned[:, j, :], first[:, cols], ident[:], start=True, stop=False, is_transpose=True)
-                nc.tensor.matmul(turned[:, j, :], second[:, cols], ident[:], start=False, stop=True, is_transpose=True)
-            staged = sb(name + "_staged", [P, PACK, P], F32, tag="th%d" % which)
-            nc.scalar.activation(staged[:], turned[:], ACT.Copy, scale=scale)
-            total = psum.tile([P, N], F32, name=name + "_total", tag="a%d" % (2 + which))
+                nc.tensor.matmul(turned[:, cols], first[:, cols], ident[:], start=True, stop=False, is_transpose=True)
+                nc.tensor.matmul(turned[:, cols], second[:, cols], ident[:], start=False, stop=True, is_transpose=True)
+
+        def turn_back(total, staged):
             for j in range(PACK):
-                nc.tensor.transpose(total[:, j * P:(j + 1) * P], staged[:, j, :], ident[:])
-            return total
+                cols = slice(j * P, (j + 1) * P)
+                nc.tensor.transpose(total[:, cols], staged[:, cols], ident[:])
 
-        def root_of_nv(k):
-            total = add_on_tensor("nv%d" % k, v_kept[k], nv[k][:], 1.0, k % 2)
-            nc.scalar.activation(root[:, k, :], total[:], ACT.Sqrt)
-
-        def negated_nm(k):
-            total = add_on_tensor("nm%d" % k, m_kept[k], nm[k][:], -1.0, k % 2)
-            nc.scalar.activation(minus_nm[:, k, :], total[:], ACT.Copy)
-
-        for h in range(2):
-            blocks = (2 * h, 2 * h + 1)
-            for k in blocks:
-                nc.scalar.activation(v_kept[k], v_picked[k][:], ACT.Copy, scale=RHO)
-                nc.scalar.activation(nv[k][:], dw[k][:], ACT.Square, scale=math.sqrt(1.0 - RHO))
-                scatter_and_store(v_new, v_kept[k], nv[k][:], ALU.add, out_2, k)
-            if h == 0:
+        for k in range(BLOCKS):
+            if k == 1:
                 dw.extend(gradient(1, None))
-            for k in blocks:
-                root_of_nv(k)
-            for k in blocks:
-                nc.scalar.activation(m_kept[k], m_picked[k], ACT.Copy, scale=BETA)
-                nc.scalar.activation(nm[k][:], dw[k][:], ACT.Copy, scale=1.0 - BETA)
-                scatter_and_store(m_new, m_kept[k], nm[k][:], ALU.add, out_1, k)
-            if h == 0:
-                for k in blocks:
-                    negated_nm(k)
+            nc.scalar.activation(v_kept[k], v_picked[k][:], ACT.Copy, scale=RHO)
+            nc.scalar.activation(nv[k], dw[k][:], ACT.Square, scale=math.sqrt(1.0 - RHO))
+            scatter_and_store(v_new, v_kept[k], nv[k], ALU.add, out_2, k)
+        for k in range(BLOCKS):
+            nc.scalar.activation(dw_sb[k][:], dw[k][:], ACT.Copy)
+            turned = psum.tile([P, N], F32, name="nm_turned%d" % k, tag="dw%d" % k)
+            add_turned(turned, m_picked[k], dw_sb[k])
+            staged = sb("nm_staged%d" % k, [P, N], F32, tag="diff%d" % k)
+            nc.scalar.activation(staged[:], turned[:], ACT.Copy, scale=-BETA)
+            total = psum.tile([P, N], F32, name="nm_total%d" % k, tag="dw%d" % k)
+            turn_back(total, staged)
+            nc.scalar.activation(minus_nm[:, k, :], total[:], ACT.Copy)
+            scatter_and_store(m_new, minus_nm[:, k, :], minus_one[:], ALU.mult, out_1, k)
 
+        root_turned = sb("root_turned", [P, BLOCKS, N], F32)
+        for k in range(BLOCKS):
+            turned = psum.tile([P, N], F32, name="nv_turned%d" % k, tag="a%d" % k)
+            add_turned(turned, v_kept[k], nv[k])
+            nc.scalar.activation(root_turned[:, k, :], turned[:], ACT.Sqrt)
+        for k in range(BLOCKS):
+            back = psum.tile([P, N], F32, name="root_back%d" % k, tag="a%d" % (BLOCKS - 1 - k))
+            turn_back(back, root_turned[:, k, :])
+            nc.scalar.activation(root[:, k, :], back[:], ACT.Ln, bias=eps_col[:], scale=1.0 / LR)
         flat = root[:].rearrange("p k i -> p (k i)")
-        nc.scalar.activation(flat, flat, ACT.Ln, bias=eps_col[:], scale=1.0 / LR)
+        nc.scalar.activation(flat, flat, ACT.Exp, scale=-1.0)
         for k in range(BLOCKS):
-            nc.scalar.activation(root[:, k, :], root[:, k, :], ACT.Exp, scale=-1.0)
-        for k in range(BLOCKS):
-            if k >= 2:
-                negated_nm(k)
             scatter_and_store(step, minus_nm[:, k, :], root[:, k, :], ALU.mult, out_0, k)

@@ -24,8 +24,8 @@ BLOCKS = D // P
 CHUNK = 128
 CHUNKS = N // CHUNK
 HALF = T // 2
-SECOND_CUT = 128
-X_CUT = 12
+W_CUTS = (192, 224)
+X_CUT = 40
 
 
 def tile_attend_glch_adam_kernel(tc, xT, wT, y, wt, xm, mT, vT, offs, out_0, out_1, out_2):
@@ -95,8 +95,6 @@ def tile_attend_glch_adam_kernel(tc, xT, wT, y, wt, xm, mT, vT, offs, out_0, out
         for k in range(BLOCKS):
             (nc.vector if k % 2 else nc.gpsimd).memset(step[k][:], 0.0)
 
-        minus_one = sb("minus_one", [P, N], F32)
-        nc.gpsimd.memset(minus_one[:], -1.0)
         ident = sb("ident", [P, P], F32)
         make_identity(nc, ident[:])
 
@@ -109,12 +107,12 @@ def tile_attend_glch_adam_kernel(tc, xT, wT, y, wt, xm, mT, vT, offs, out_0, out
             return dst, src.rearrange("p e (c i) -> p c e i", i=4)
 
         nc.scalar.activation(*pair_views(0, 0, w_first[0][:]), ACT.Copy)
-        nc.scalar.activation(*pair_views(0, HALF, w_first[1][:, :, 0:SECOND_CUT]), ACT.Copy)
-        nc.vector.tensor_copy(*pair_views(0, HALF + SECOND_CUT, w_first[1][:, :, SECOND_CUT:HALF]))
+        nc.scalar.activation(*pair_views(0, HALF, w_first[1][:, :, 0:W_CUTS[0]]), ACT.Copy)
+        nc.vector.tensor_copy(*pair_views(0, HALF + W_CUTS[0], w_first[1][:, :, W_CUTS[0]:HALF]))
         nc.vector.tensor_copy(w_picked[:, :, 0], w_pairs[0][:].indirect(offsets[:]))
         nc.scalar.activation(*pair_views(1, 0, w_second[0][:]), ACT.Copy)
-        nc.scalar.activation(*pair_views(1, HALF, w_second[1][:, :, 0:SECOND_CUT]), ACT.Copy)
-        nc.vector.tensor_copy(*pair_views(1, HALF + SECOND_CUT, w_second[1][:, :, SECOND_CUT:HALF]))
+        nc.scalar.activation(*pair_views(1, HALF, w_second[1][:, :, 0:W_CUTS[1]]), ACT.Copy)
+        nc.vector.tensor_copy(*pair_views(1, HALF + W_CUTS[1], w_second[1][:, :, W_CUTS[1]:HALF]))
         nc.vector.tensor_copy(w_picked[:, :, 1], w_pairs[1][:].indirect(offsets[:]))
 
         nc.scalar.activation(v_new[0][:], v_old[0][:], ACT.Copy)
@@ -127,7 +125,7 @@ def tile_attend_glch_adam_kernel(tc, xT, wT, y, wt, xm, mT, vT, offs, out_0, out
         nc.scalar.activation(*x_views(0, 0, P // 2), ACT.Copy)
         nc.scalar.activation(*x_views(1, 0, X_CUT), ACT.Copy)
         nc.vector.tensor_copy(*x_views(1, X_CUT, P // 2))
-        w_codes = sb("w_codes", [P, N], U32, tag="x_raw1")
+        w_codes = sb("w_codes", [P, N], U32, tag="x_raw0")
         w_scales = sb("w_scales", [P, N], U8)
         nc.vector.quantize_mx(
             out=w_codes[:].bitcast(E4M3), scales=w_scales[:],
@@ -247,8 +245,11 @@ def tile_attend_glch_adam_kernel(tc, xT, wT, y, wt, xm, mT, vT, offs, out_0, out
             nc.scalar.activation(staged[:], turned[:], ACT.Copy, scale=-BETA)
             total = psum.tile([P, N], F32, name="nm_total%d" % k, tag="dw%d" % k)
             turn_back(total, staged)
+            nm = sb("nm%d" % k, [P, N], F32)
+            nc.scalar.activation(nm[:], total[:], ACT.Copy, scale=-1.0)
+            nc.vector.tensor_copy(m_new[k][:].indirect(offsets[:]), nm[:])
+            nc.sync.dma_start(out_1[k * P:(k + 1) * P, :], m_new[k][:])
             nc.scalar.activation(minus_nm[:, k, :], total[:], ACT.Copy)
-            scatter_and_store(m_new, minus_nm[:, k, :], minus_one[:], ALU.mult, out_1, k)
 
         root_turned = sb("root_turned", [P, BLOCKS, N], F32)
         for k in range(BLOCKS):
@@ -259,7 +260,8 @@ def tile_attend_glch_adam_kernel(tc, xT, wT, y, wt, xm, mT, vT, offs, out_0, out
             back = psum.tile([P, N], F32, name="root_back%d" % k, tag="a%d" % (BLOCKS - 1 - k))
             turn_back(back, root_turned[:, k, :])
             nc.scalar.activation(root[:, k, :], back[:], ACT.Ln, bias=eps_col[:], scale=1.0 / LR)
-        flat = root[:].rearrange("p k i -> p (k i)")
-        nc.scalar.activation(flat, flat, ACT.Exp, scale=-1.0)
+        for h in range(2):
+            flat = root[:, 2 * h:2 * h + 2, :].rearrange("p k i -> p (k i)")
+            nc.scalar.activation(flat, flat, ACT.Exp, scale=-1.0)
         for k in range(BLOCKS):
             scatter_and_store(step, minus_nm[:, k, :], root[:, k, :], ALU.mult, out_0, k)

@@ -2,7 +2,6 @@ import math
 from contextlib import ExitStack
 
 import concourse.mybir as mybir
-from concourse.masks import make_identity
 
 N, T, D, R = 512, 1024, 512, 512
 LR, BETA, RHO, EPS = 0.1, 0.5, 0.9, 0.001
@@ -20,12 +19,12 @@ ALU = mybir.AluOpType
 
 P = 128
 PACK = 4
-BLOCKS = D // P
+BANDS = D // P
 CHUNK = 128
 CHUNKS = N // CHUNK
-HALF = T // 2
-W_CUTS = (192, 224)
-X_CUT = 40
+X_CUT = 24
+TINY = 1e-30
+RATE = LR * BETA
 
 
 def tile_attend_glch_adam_kernel(tc, xT, wT, y, wt, xm, mT, vT, offs, out_0, out_1, out_2):
@@ -37,87 +36,94 @@ def tile_attend_glch_adam_kernel(tc, xT, wT, y, wt, xm, mT, vT, offs, out_0, out
         def sb(name, shape, dtype, tag=None):
             return keep.tile(shape, dtype, name=name, tag=tag or name, align_bytes=64)
 
-        w_rows = wT.rearrange("(p u e) t -> u p e t", u=2, e=2)
-        w_first = [sb("w_first%d" % h, [P, 2, HALF], F32) for h in range(2)]
-        nc.sync.dma_start(w_first[0][:], w_rows[0][:, :, 0:HALF])
+        def bands(name, width):
+            return [sb("%s%d" % (name, k), [P, width], F32) for k in range(BANDS)]
+
+        w_rows = wT.rearrange("(p j) t -> j p t", j=PACK)
+        w_raw = bands("w_raw", T)
+        nc.sync.dma_start(w_raw[0][:], w_rows[0])
         offsets = keep.tile([P, N // 16], U16, name="offsets")
         nc.sync.dma_start(offsets[:], offs)
-        nc.sync.dma_start(w_first[1][:], w_rows[0][:, :, HALF:T])
-        m_old = [sb("m_old%d" % k, [P, T], F32) for k in range(BLOCKS)]
-        v_old = [sb("v_old%d" % k, [P, T], F32) for k in range(BLOCKS)]
-        nc.sync.dma_start(v_old[0][:], vT[0:P, :])
-        w_second = [sb("w_second%d" % h, [P, 2, HALF], F32) for h in range(2)]
-        for h in range(2):
-            nc.sync.dma_start(w_second[h][:], w_rows[1][:, :, h * HALF:(h + 1) * HALF])
+        for j in range(1, PACK):
+            nc.sync.dma_start(w_raw[j][:], w_rows[j])
         x_rows = xT[0].rearrange("(p j) r -> p j r", j=PACK)
         x_raw = [sb("x_raw%d" % h, [P, PACK, R // 2], F32) for h in range(2)]
         for h in range(2):
             nc.sync.dma_start(x_raw[h][:], x_rows[:, :, h * (R // 2):(h + 1) * (R // 2)])
         wt_sb = sb("wt_sb", [P, PACK], F32)
         nc.sync.dma_start(wt_sb[:], wt[0].rearrange("(p t) o -> p (t o)", t=PACK))
-        nc.sync.dma_start(v_old[1][:], vT[P:2 * P, :])
         y_rows = y[0].rearrange("(p t) i -> p t i", t=PACK)
         y_sb = [sb("y_sb%d" % h, [P, PACK, N // 2], F32) for h in range(2)]
         for h in range(2):
             nc.sync.dma_start(y_sb[h][:], y_rows[:, :, h * (N // 2):(h + 1) * (N // 2)])
         xm_rows = xm[0].rearrange("(p t) d -> p t d", t=PACK)
         xm_raw = [sb("xm_raw%d" % h, [P, PACK, D // 2], F32) for h in range(2)]
-        m_new = [sb("m_new%d" % k, [P, T], F32) for k in range(BLOCKS)]
-        v_new = [sb("v_new%d" % k, [P, T], F32) for k in range(BLOCKS)]
-        step = [sb("step%d" % k, [P, T], F32) for k in range(BLOCKS)]
+        m_new, v_new, step = [bands(name, T) for name in ("m_new", "v_new", "step")]
+        m_pairs = [sb("m_pair%d" % h, [P, 2 * T], F32) for h in range(2)]
+        v_pair = sb("v_pair", [P, 2 * T], F32)
+        v_alone = [sb("v_alone%d" % k, [P, T], F32) for k in range(2)]
+        m_old = [m_pairs[0][:, T:], m_pairs[0][:, :T], m_pairs[1][:, :T], m_pairs[1][:, T:]]
+        v_old = [v_alone[0][:], v_alone[1][:], v_pair[:, T:], v_pair[:, :T]]
 
-        def load_block(tiles, table, k):
-            nc.sync.dma_start(tiles[k][:], table[k * P:(k + 1) * P, :])
+        def load_band(tiles, table, k):
+            nc.sync.dma_start(tiles[k][:, :], table[k * P:(k + 1) * P, :])
 
         def load_xm(h):
             nc.sync.dma_start(xm_raw[h][:], xm_rows[:, :, h * (D // 2):(h + 1) * (D // 2)])
 
-        load_block(v_old, vT, 2)
-        load_block(v_old, vT, 3)
-        load_block(m_old, mT, 0)
-        load_block(m_old, mT, 1)
         load_xm(0)
-        load_block(m_old, mT, 2)
-        load_block(m_old, mT, 3)
+        load_band(v_old, vT, 0)
+        load_band(v_old, vT, 1)
         load_xm(1)
-        load_block(v_new, vT, 1)
-        load_block(v_new, vT, 2)
-        load_block(v_new, vT, 3)
-        load_block(m_new, mT, 0)
-        load_block(m_new, mT, 1)
-        load_block(m_new, mT, 2)
-        load_block(m_new, mT, 3)
+        load_band(m_old, mT, 0)
+        load_band(m_new, mT, 0)
+        load_band(v_old, vT, 2)
+        load_band(v_old, vT, 3)
+        load_band(m_old, mT, 3)
+        load_band(v_new, vT, 2)
+        load_band(m_new, mT, 3)
+        load_band(m_old, mT, 1)
+        load_band(m_old, mT, 2)
+        for k in (0, 1, 3):
+            load_band(v_new, vT, k)
+        nc.sync.dma_start(m_new[2][:, :T // 2], mT[2 * P:3 * P, :T // 2])
+        load_band(m_new, mT, 1)
+        nc.sync.dma_start(m_new[2][:, T // 2:], mT[2 * P:3 * P, T // 2:])
 
         one = sb("one", [P, 1], F32)
         nc.vector.memset(one[:], 1.0)
+        tiny_col = sb("tiny_col", [P, 1], F32)
+        nc.scalar.activation(tiny_col[:], one[:], ACT.Copy, scale=TINY)
         eps_col = sb("eps_col", [P, 1], F32)
-        nc.scalar.activation(eps_col[:], one[:], ACT.Copy, scale=EPS / LR)
-        for k in range(BLOCKS):
-            (nc.vector if k % 2 else nc.gpsimd).memset(step[k][:], 0.0)
+        nc.scalar.activation(eps_col[:], one[:], ACT.Copy, scale=(EPS / RATE) ** 2)
+        for k in range(BANDS):
+            nc.gpsimd.memset(step[k][:], 0.0)
 
-        ident = sb("ident", [P, P], F32)
-        make_identity(nc, ident[:])
+        def slots(lo, hi):
+            return offsets[:, lo // 16:hi // 16]
 
-        w_pairs = [sb("w_pairs%d" % u, [P, T], U32) for u in range(2)]
-        w_picked = sb("w_picked", [P, N, 2], U32)
+        def gather(on_scalar, dst, window, lo=0, hi=N, scale=1.0):
+            if on_scalar:
+                nc.scalar.activation(dst[:, lo:hi], window[:, :].indirect(slots(lo, hi)), ACT.Copy, scale=scale)
+            else:
+                nc.vector.tensor_copy(dst[:, lo:hi], window[:, :].indirect(slots(lo, hi)))
 
-        def pair_views(u, lo, src):
-            width = src.shape[2]
-            dst = w_pairs[u][:, lo:lo + width].bitcast(BF16).rearrange("p (c i e) -> p c e i", i=4, e=2)
-            return dst, src.rearrange("p e (c i) -> p c e i", i=4)
-
-        nc.scalar.activation(*pair_views(0, 0, w_first[0][:]), ACT.Copy)
-        nc.scalar.activation(*pair_views(0, HALF, w_first[1][:, :, 0:W_CUTS[0]]), ACT.Copy)
-        nc.vector.tensor_copy(*pair_views(0, HALF + W_CUTS[0], w_first[1][:, :, W_CUTS[0]:HALF]))
-        nc.vector.tensor_copy(w_picked[:, :, 0], w_pairs[0][:].indirect(offsets[:]))
-        nc.scalar.activation(*pair_views(1, 0, w_second[0][:]), ACT.Copy)
-        nc.scalar.activation(*pair_views(1, HALF, w_second[1][:, :, 0:W_CUTS[1]]), ACT.Copy)
-        nc.vector.tensor_copy(*pair_views(1, HALF + W_CUTS[1], w_second[1][:, :, W_CUTS[1]:HALF]))
-        nc.vector.tensor_copy(w_picked[:, :, 1], w_pairs[1][:].indirect(offsets[:]))
-
-        nc.scalar.activation(v_new[0][:], v_old[0][:], ACT.Copy)
+        w_planes = sb("w_planes", [P, PACK, N], BF16)
+        gather(False, w_planes[:, 0, :], w_raw[0])
+        gather(True, w_planes[:, 1, :], w_raw[1])
+        gather(False, w_planes[:, 2, :], w_raw[2])
+        gather(True, w_planes[:, 3, :], w_raw[3], 0, N // 2)
+        gather(False, w_planes[:, 3, :], w_raw[3], N // 2, N)
+        w_bf = sb("w_bf", [P, N, PACK], BF16)
+        nc.vector.tensor_copy(
+            w_bf[:].rearrange("p (c i) t -> p c t i", i=4), w_planes[:].rearrange("p t (c i) -> p c t i", i=4))
+        w_codes = sb("w_codes", [P, N], U32)
+        w_scales = sb("w_scales", [P, N], U8)
+        nc.vector.quantize_mx(
+            out=w_codes[:].bitcast(E4M3), scales=w_scales[:], in_=w_bf[:].rearrange("p i t -> p (i t)"))
 
         x_bf = sb("x_bf", [P, PACK, P, PACK], BF16)
+
         def x_views(h, lo, hi):
             dst = x_bf[:, :, h * (P // 2) + lo:h * (P // 2) + hi, :].rearrange("p t m j -> p m j t")
             return dst, x_raw[h][:].rearrange("p j (m t) -> p m j t", t=PACK)[:, lo:hi, :, :]
@@ -125,11 +131,6 @@ def tile_attend_glch_adam_kernel(tc, xT, wT, y, wt, xm, mT, vT, offs, out_0, out
         nc.scalar.activation(*x_views(0, 0, P // 2), ACT.Copy)
         nc.scalar.activation(*x_views(1, 0, X_CUT), ACT.Copy)
         nc.vector.tensor_copy(*x_views(1, X_CUT, P // 2))
-        w_codes = sb("w_codes", [P, N], U32, tag="x_raw0")
-        w_scales = sb("w_scales", [P, N], U8)
-        nc.vector.quantize_mx(
-            out=w_codes[:].bitcast(E4M3), scales=w_scales[:],
-            in_=w_picked[:].rearrange("p i u -> p (i u)").bitcast(BF16))
         x_codes = sb("x_codes", [P, R], U32)
         x_scales = sb("x_scales", [P, R], U8)
         for h in range(2):
@@ -137,10 +138,8 @@ def tile_attend_glch_adam_kernel(tc, xT, wT, y, wt, xm, mT, vT, offs, out_0, out
             nc.vector.quantize_mx(
                 out=x_codes[:, rows].bitcast(E4M3), scales=x_scales[:, rows],
                 in_=x_bf[:, 2 * h:2 * h + 2, :, :].rearrange("p t m j -> p (t m j)"))
-        wt_wide = sb("wt_wide", [P, CHUNK, PACK], F32)
-        nc.scalar.activation(wt_wide[:], wt_sb[:].unsqueeze(1).to_broadcast([P, CHUNK, PACK]), ACT.Copy)
 
-        g_codes = sb("g_codes", [P, N], U32, tag="m_old1")
+        g_codes = sb("g_codes", [P, N], U32)
         g_scales = sb("g_scales", [P, N], U8)
         g_bf = sb("g_bf", [P, N, PACK], BF16)
         diffs = [sb("diff%d" % c, [P, PACK, CHUNK], F32) for c in range(CHUNKS)]
@@ -154,114 +153,113 @@ def tile_attend_glch_adam_kernel(tc, xT, wT, y, wt, xm, mT, vT, offs, out_0, out
                     lhsT=x_codes[:, rows].bitcast(E4M3), lhsT_scale=x_scales[:, rows],
                     rhs=w_codes[:, cols].bitcast(E4M3), rhs_scale=w_scales[:, cols],
                     start=True, stop=True)
-            diff = diffs[c]
             y_part = y_sb[c // 2][:, :, (c % 2) * CHUNK:(c % 2 + 1) * CHUNK]
-            if c == 0:
-                nc.scalar.activation(diff[:], a, ACT.Copy)
-                nc.gpsimd.tensor_tensor(diff[:], diff[:], y_part, ALU.subtract)
-            else:
-                nc.vector.tensor_tensor(diff[:], a, y_part, ALU.subtract)
-        for c in (1, 0, 2, 3):
+            nc.vector.tensor_tensor(diffs[c][:], a, y_part, ALU.subtract)
+        for c in range(CHUNKS):
             cols = slice(c * CHUNK, (c + 1) * CHUNK)
             diff = diffs[c]
-            if c < CHUNKS - 1:
-                th = sb("th%d" % c, [P, CHUNK, PACK], F32, tag="diff1" if c == 0 else None)
+            if c == 0:
+                th = sb("th0", [P, CHUNK, PACK], F32)
                 nc.scalar.activation(th[:], diff[:].rearrange("p t i -> p i t"), ACT.Tanh)
-                nc.gpsimd.tensor_tensor(g_bf[:, cols, :], th[:], wt_wide[:], ALU.mult)
+                nc.gpsimd.tensor_tensor(
+                    g_bf[:, cols, :], th[:], wt_sb[:].unsqueeze(1).to_broadcast([P, CHUNK, PACK]), ALU.mult)
             else:
-                th = sb("th%d" % c, [P, PACK, CHUNK], F32)
-                nc.scalar.activation(th[:], diff[:], ACT.Tanh)
-                for t in range(PACK):
-                    nc.scalar.activation(g_bf[:, cols, t], th[:, t, :], ACT.Copy, scale=wt_sb[:, t:t + 1])
-        nc.vector.quantize_mx(
-            out=g_codes[:].bitcast(E5M2), scales=g_scales[:],
-            in_=g_bf[:].rearrange("p i t -> p (i t)"))
+                nc.scalar.activation(diff[:], diff[:], ACT.Tanh)
+                nc.vector.tensor_tensor(
+                    g_bf[:, cols, :].rearrange("p (c i) t -> p c t i", i=4),
+                    diff[:].rearrange("p t (c i) -> p c t i", i=4),
+                    wt_sb[:].unsqueeze(1).unsqueeze(3).to_broadcast([P, CHUNK // 4, PACK, 4]), ALU.mult)
 
-        dw_sb = [sb("dw_sb%d" % k, [P, N], F32) for k in range(BLOCKS)]
-        root = sb("root", [P, BLOCKS, N], F32)
+        xm_codes = [sb("xm_codes%d" % k, [P, P], U32) for k in range(BANDS)]
+        xm_scales = [sb("xm_scales%d" % k, [P, P], U8) for k in range(BANDS)]
 
-        def gradient(h, tag):
-            xm_bf = sb("xm_bf%d" % h, [P, D // 2, PACK], BF16)
-            nc.scalar.activation(
-                xm_bf[:].rearrange("p (c i) t -> p c t i", i=4),
-                xm_raw[h][:].rearrange("p t (c i) -> p c t i", i=4), ACT.Copy)
-            codes = sb("xm_codes%d" % h, [P, D // 2], U32, tag=tag)
-            scales = sb("xm_scales%d" % h, [P, D // 2], U8)
+        def quantise_xm(k):
+            xm_bf = sb("xm_bf%d" % k, [P, P, PACK], BF16)
+            dst = xm_bf[:].rearrange("p (c i) t -> p c t i", i=4)
+            raw = xm_raw[k // 2][:, :, (k % 2) * P:(k % 2 + 1) * P]
+            src = raw.rearrange("p t (c i) -> p c t i", i=4)
+            if k < 2:
+                nc.scalar.activation(dst, src, ACT.Copy)
+            else:
+                nc.gpsimd.tensor_copy(xm_bf[:], raw.rearrange("p t d -> p d t"))
             nc.vector.quantize_mx(
-                out=codes[:].bitcast(E4M3), scales=scales[:], in_=xm_bf[:].rearrange("p d t -> p (d t)"))
-            banks = []
-            for b in range(2):
-                rows = slice(b * P, (b + 1) * P)
-                bank = psum.tile([P, N], F32, name="dw%d" % (2 * h + b))
-                nc.tensor.matmul_mx(
-                    out=bank[:],
-                    lhsT=codes[:, rows].bitcast(E4M3), lhsT_scale=scales[:, rows],
-                    rhs=g_codes[:].bitcast(E5M2), rhs_scale=g_scales[:],
-                    start=True, stop=True)
-                banks.append(bank)
-            return banks
+                out=xm_codes[k][:].bitcast(E4M3), scales=xm_scales[k][:], in_=xm_bf[:].rearrange("p d t -> p (d t)"))
 
-        dw = gradient(0, None)
+        quantise_xm(0)
+        nc.vector.quantize_mx(
+            out=g_codes[:].bitcast(E5M2), scales=g_scales[:], in_=g_bf[:].rearrange("p i t -> p (i t)"))
 
-        v_picked = [sb("v_picked%d" % k, [P, N], F32, tag=None) for k in range(BLOCKS)]
-        after_cast = sb("after_cast", [P, 4, N], F32, tag="xm_raw0")
-        late = sb("late", [P, 3, N], F32, tag="xm_raw1")
-        nv = [late[:, 2, :] if k == 1 else sb("nv%d" % k, [P, N], F32)[:] for k in range(BLOCKS)]
-        v_kept = [after_cast[:, 0, :], after_cast[:, 1, :], late[:, 0, :], late[:, 1, :]]
-        minus_nm = sb("minus_nm", [P, BLOCKS, N], F32)
-        m_early = sb("m_early", [P, 2, N], F32)
-        m_picked = [m_early[:, 0, :], m_early[:, 1, :], after_cast[:, 2, :], after_cast[:, 3, :]]
-        for k in range(BLOCKS):
-            nc.vector.tensor_copy(v_picked[k][:], v_old[k][:].indirect(offsets[:]))
-        for k in range(BLOCKS):
-            nc.vector.tensor_copy(m_picked[k], m_old[k][:].indirect(offsets[:]))
+        def scatter_and_store(on_scalar, window, values, out, k, scale=1.0):
+            if on_scalar:
+                for lo in (0, N // 2):
+                    nc.scalar.activation(
+                        window[k][:].indirect(slots(lo, lo + N // 2)), values[:, lo:lo + N // 2], ACT.Copy, scale=scale)
+                nc.scalar.dma_start(out[k * P:(k + 1) * P, :], window[k][:])
+            else:
+                nc.vector.tensor_copy(window[k][:].indirect(offsets[:]), values[:])
+                nc.sync.dma_start(out[k * P:(k + 1) * P, :], window[k][:])
 
-        def scatter_and_store(window, first, second, op, out, k):
-            nc.vector.tensor_tensor(window[k][:].indirect(offsets[:]), first, second, op)
-            nc.sync.dma_start(out[k * P:(k + 1) * P, :], window[k][:])
+        def gather_scaled(dst, pair, scale):
+            nc.vector.tensor_scalar(dst[:], pair[:].indirect(offsets[:]), scale, 0.0, ALU.mult, ALU.add)
 
-        def add_turned(turned, first, second):
-            for j in range(PACK):
-                cols = slice(j * P, (j + 1) * P)
-                nc.tensor.matmul(turned[:, cols], first[:, cols], ident[:], start=True, stop=False, is_transpose=True)
-                nc.tensor.matmul(turned[:, cols], second[:, cols], ident[:], start=False, stop=True, is_transpose=True)
+        m_picked, nm = [bands(name, N) for name in ("m_picked", "nm")]
+        v_picked_pairs = [sb("v_picked%d" % h, [P, 2 * N], F32) for h in range(2)]
+        nv_pairs = [sb("nv%d" % h, [P, 2 * N], F32) for h in range(2)]
+        v_picked = [v_picked_pairs[k // 2][:, (k % 2) * N:(k % 2 + 1) * N] for k in range(BANDS)]
+        nv = [nv_pairs[k // 2][:, (k % 2) * N:(k % 2 + 1) * N] for k in range(BANDS)]
+        ratio = v_picked[2:] + v_picked[:2]
+        dw = []
+        for k in range(BANDS):
+            if k > 0:
+                quantise_xm(k)
+            bank = psum.tile([P, N], F32, name="dw%d" % k)
+            nc.tensor.matmul_mx(
+                out=bank[:], lhsT=xm_codes[k][:].bitcast(E4M3), lhsT_scale=xm_scales[k][:],
+                rhs=g_codes[:].bitcast(E5M2), rhs_scale=g_scales[:], start=True, stop=True)
+            dw.append(bank)
+        unit = [1.0, 1.0, RHO, 1.0]
+        product = [ratio[0], ratio[1], ratio[2], nm[1]]
 
-        def turn_back(total, staged):
-            for j in range(PACK):
-                cols = slice(j * P, (j + 1) * P)
-                nc.tensor.transpose(total[:, cols], staged[:, cols], ident[:])
+        def new_m(k):
+            if k in (0, 3):
+                gather(False, m_picked[k], m_old[k])
+                nc.vector.scalar_tensor_tensor(nm[k][:], dw[k][:], -1.0, m_picked[k][:], ALU.mult, ALU.subtract)
+            else:
+                gather_scaled(m_picked[k], m_pairs[k // 2], BETA)
+                nc.vector.scalar_tensor_tensor(nm[k][:], dw[k][:], 1.0 - BETA, m_picked[k][:], ALU.mult, ALU.add)
 
-        for k in range(BLOCKS):
-            if k == 1:
-                dw.extend(gradient(1, None))
-            nc.scalar.activation(v_kept[k], v_picked[k][:], ACT.Copy, scale=RHO)
-            nc.scalar.activation(nv[k], dw[k][:], ACT.Square, scale=math.sqrt(1.0 - RHO))
-            scatter_and_store(v_new, v_kept[k], nv[k], ALU.add, out_2, k)
-        for k in range(BLOCKS):
-            nc.scalar.activation(dw_sb[k][:], dw[k][:], ACT.Copy)
-            turned = psum.tile([P, N], F32, name="nm_turned%d" % k, tag="dw%d" % k)
-            add_turned(turned, m_picked[k], dw_sb[k])
-            staged = sb("nm_staged%d" % k, [P, N], F32, tag="diff%d" % k)
-            nc.scalar.activation(staged[:], turned[:], ACT.Copy, scale=-BETA)
-            total = psum.tile([P, N], F32, name="nm_total%d" % k, tag="dw%d" % k)
-            turn_back(total, staged)
-            nm = sb("nm%d" % k, [P, N], F32)
-            nc.scalar.activation(nm[:], total[:], ACT.Copy, scale=-1.0)
-            nc.vector.tensor_copy(m_new[k][:].indirect(offsets[:]), nm[:])
-            nc.sync.dma_start(out_1[k * P:(k + 1) * P, :], m_new[k][:])
-            nc.scalar.activation(minus_nm[:, k, :], total[:], ACT.Copy)
+        def second_root(k):
+            nc.scalar.activation(
+                ratio[k][:], ratio[k][:], ACT.Abs_reciprocal_sqrt, bias=eps_col[:], scale=unit[k] / RATE ** 2)
 
-        root_turned = sb("root_turned", [P, BLOCKS, N], F32)
-        for k in range(BLOCKS):
-            turned = psum.tile([P, N], F32, name="nv_turned%d" % k, tag="a%d" % k)
-            add_turned(turned, v_kept[k], nv[k])
-            nc.scalar.activation(root_turned[:, k, :], turned[:], ACT.Sqrt)
-        for k in range(BLOCKS):
-            back = psum.tile([P, N], F32, name="root_back%d" % k, tag="a%d" % (BLOCKS - 1 - k))
-            turn_back(back, root_turned[:, k, :])
-            nc.scalar.activation(root[:, k, :], back[:], ACT.Ln, bias=eps_col[:], scale=1.0 / LR)
-        for h in range(2):
-            flat = root[:, 2 * h:2 * h + 2, :].rearrange("p k i -> p (k i)")
-            nc.scalar.activation(flat, flat, ACT.Exp, scale=-1.0)
-        for k in range(BLOCKS):
-            scatter_and_store(step, minus_nm[:, k, :], root[:, k, :], ALU.mult, out_0, k)
+        for k in range(BANDS):
+            if k < 2:
+                gather(True, v_picked[k], v_old[k], scale=RHO)
+            elif k == 2:
+                gather(False, v_picked[k], v_old[k])
+            else:
+                gather_scaled(v_picked[k], v_pair, RHO)
+            nc.scalar.activation(nv[k][:], dw[k][:], ACT.Square, scale=math.sqrt((1.0 - RHO) / unit[k]))
+            nc.gpsimd.tensor_tensor(nv[k][:], nv[k][:], v_picked[k][:], ALU.add)
+        for k in (0, 3, 1, 2):
+            new_m(k)
+        scatter_and_store(True, m_new, nm[0], out_1, 0, scale=-BETA)
+        for k in range(BANDS):
+            if k % 2 == 0:
+                nc.scalar.activation(
+                    v_picked_pairs[1 - k // 2][:], nv_pairs[k // 2][:], ACT.Abs_reciprocal_sqrt, bias=tiny_col[:])
+            nc.gpsimd.tensor_scalar(ratio[k][:], ratio[k][:], 2.0 * EPS / math.sqrt(unit[k]), 1.0, ALU.mult, ALU.add)
+            nc.gpsimd.tensor_tensor(ratio[k][:], ratio[k][:], nv[k][:], ALU.mult)
+        scatter_and_store(True, v_new, nv[2], out_2, 2, scale=RHO)
+        second_root(0)
+        second_root(1)
+        scatter_and_store(True, m_new, nm[3], out_1, 3, scale=-BETA)
+        second_root(2)
+        second_root(3)
+        for k in (0, 1, 3):
+            scatter_and_store(False, v_new, nv[k], out_2, k)
+        for k in (1, 2):
+            scatter_and_store(False, m_new, nm[k], out_1, k)
+        for k in range(BANDS):
+            nc.gpsimd.tensor_tensor(product[k][:], ratio[k][:], nm[k][:], ALU.mult)
+            scatter_and_store(k < 3, step, product[k], out_0, k, scale=1.0 if k == 0 else -1.0 / BETA)

@@ -2,6 +2,7 @@ import math
 from contextlib import ExitStack
 
 import concourse.mybir as mybir
+from concourse.masks import make_identity
 
 N, T, D, R = 512, 1024, 512, 512
 LR, BETA, RHO, EPS = 0.1, 0.5, 0.9, 0.001
@@ -22,7 +23,10 @@ PACK = 4
 BANDS = D // P
 CHUNK = 128
 CHUNKS = N // CHUNK
-X_CUT = 24
+X_CUT = 28
+G_CUT = 96
+I_CUT = 96
+W_CUT = 192
 TINY = 1e-30
 RATE = LR * BETA
 
@@ -44,47 +48,50 @@ def tile_attend_glch_adam_kernel(tc, xT, wT, y, wt, xm, mT, vT, offs, out_0, out
         nc.sync.dma_start(w_raw[0][:], w_rows[0])
         offsets = keep.tile([P, N // 16], U16, name="offsets")
         nc.sync.dma_start(offsets[:], offs)
-        for j in range(1, PACK):
+        nc.sync.dma_start(w_raw[1][:], w_rows[1])
+        wt_row = sb("wt_row", [P, R], F32)
+        nc.gpsimd.memset(wt_row[:], 0.0)
+        nc.sync.dma_start(wt_row[0:1, :], wt[0].rearrange("r o -> o r"))
+        for j in range(2, PACK):
             nc.sync.dma_start(w_raw[j][:], w_rows[j])
         x_rows = xT[0].rearrange("(p j) r -> p j r", j=PACK)
         x_raw = [sb("x_raw%d" % h, [P, PACK, R // 2], F32) for h in range(2)]
         for h in range(2):
             nc.sync.dma_start(x_raw[h][:], x_rows[:, :, h * (R // 2):(h + 1) * (R // 2)])
-        wt_sb = sb("wt_sb", [P, PACK], F32)
-        nc.sync.dma_start(wt_sb[:], wt[0].rearrange("(p t) o -> p (t o)", t=PACK))
         y_rows = y[0].rearrange("(p t) i -> p t i", t=PACK)
         y_sb = [sb("y_sb%d" % h, [P, PACK, N // 2], F32) for h in range(2)]
-        for h in range(2):
-            nc.sync.dma_start(y_sb[h][:], y_rows[:, :, h * (N // 2):(h + 1) * (N // 2)])
         xm_rows = xm[0].rearrange("(p t) d -> p t d", t=PACK)
         xm_raw = [sb("xm_raw%d" % h, [P, PACK, D // 2], F32) for h in range(2)]
         m_new, v_new, step = [bands(name, T) for name in ("m_new", "v_new", "step")]
         m_pairs = [sb("m_pair%d" % h, [P, 2 * T], F32) for h in range(2)]
-        v_pair = sb("v_pair", [P, 2 * T], F32)
-        v_alone = [sb("v_alone%d" % k, [P, T], F32) for k in range(2)]
+        v_pairs = [sb("v_pair%d" % h, [P, 2 * T], F32) for h in range(2)]
         m_old = [m_pairs[0][:, T:], m_pairs[0][:, :T], m_pairs[1][:, :T], m_pairs[1][:, T:]]
-        v_old = [v_alone[0][:], v_alone[1][:], v_pair[:, T:], v_pair[:, :T]]
+        v_old = [v_pairs[0][:, T:], v_pairs[0][:, :T], v_pairs[1][:, :T], v_pairs[1][:, T:]]
 
         def load_band(tiles, table, k):
             nc.sync.dma_start(tiles[k][:, :], table[k * P:(k + 1) * P, :])
+
+        def load_pair(tile, table):
+            nc.sync.dma_start(
+                tile[:].rearrange("p (b t) -> p b t", b=2), table[2 * P:, :].rearrange("(b p) t -> p b t", b=2))
 
         def load_xm(h):
             nc.sync.dma_start(xm_raw[h][:], xm_rows[:, :, h * (D // 2):(h + 1) * (D // 2)])
 
         load_xm(0)
-        load_band(v_old, vT, 0)
-        load_band(v_old, vT, 1)
+        for h in range(2):
+            nc.sync.dma_start(y_sb[h][:], y_rows[:, :, h * (N // 2):(h + 1) * (N // 2)])
         load_xm(1)
         load_band(m_old, mT, 0)
+        load_band(v_old, vT, 0)
+        load_band(v_old, vT, 1)
+        load_pair(v_pairs[1], vT)
         load_band(m_new, mT, 0)
-        load_band(v_old, vT, 2)
-        load_band(v_old, vT, 3)
-        load_band(m_old, mT, 3)
-        load_band(v_new, vT, 2)
-        load_band(m_new, mT, 3)
+        load_pair(m_pairs[1], mT)
+        load_band(v_new, vT, 3)
         load_band(m_old, mT, 1)
-        load_band(m_old, mT, 2)
-        for k in (0, 1, 3):
+        load_band(m_new, mT, 3)
+        for k in (0, 1, 2):
             load_band(v_new, vT, k)
         nc.sync.dma_start(m_new[2][:, :T // 2], mT[2 * P:3 * P, :T // 2])
         load_band(m_new, mT, 1)
@@ -96,8 +103,15 @@ def tile_attend_glch_adam_kernel(tc, xT, wT, y, wt, xm, mT, vT, offs, out_0, out
         nc.scalar.activation(tiny_col[:], one[:], ACT.Copy, scale=TINY)
         eps_col = sb("eps_col", [P, 1], F32)
         nc.scalar.activation(eps_col[:], one[:], ACT.Copy, scale=(EPS / RATE) ** 2)
+        ident = sb("ident", [P, P], F32)
+        make_identity(nc, ident[:])
         for k in range(BANDS):
             nc.gpsimd.memset(step[k][:], 0.0)
+        wt_bank = psum.tile([P, PACK, P], F32, name="wt_bank", tag="dw3")
+        for t in range(PACK):
+            nc.tensor.transpose(wt_bank[:, t, :], wt_row[:, t:R:PACK], ident[:])
+        wt_wide = sb("wt_wide", [P, CHUNK, PACK], F32)
+        nc.scalar.activation(wt_wide[:], wt_bank[:].rearrange("p t n -> p n t")[:, 0:1, :].to_broadcast([P, CHUNK, PACK]), ACT.Copy)
 
         def slots(lo, hi):
             return offsets[:, lo // 16:hi // 16]
@@ -112,15 +126,24 @@ def tile_attend_glch_adam_kernel(tc, xT, wT, y, wt, xm, mT, vT, offs, out_0, out
         gather(False, w_planes[:, 0, :], w_raw[0])
         gather(True, w_planes[:, 1, :], w_raw[1])
         gather(False, w_planes[:, 2, :], w_raw[2])
-        gather(True, w_planes[:, 3, :], w_raw[3], 0, N // 2)
-        gather(False, w_planes[:, 3, :], w_raw[3], N // 2, N)
+        gather(True, w_planes[:, 3, :], w_raw[3], 0, W_CUT)
+        gather(False, w_planes[:, 3, :], w_raw[3], W_CUT, N)
         w_bf = sb("w_bf", [P, N, PACK], BF16)
-        nc.vector.tensor_copy(
-            w_bf[:].rearrange("p (c i) t -> p c t i", i=4), w_planes[:].rearrange("p t (c i) -> p c t i", i=4))
+        halves = [slice(h * (N // 2), (h + 1) * (N // 2)) for h in range(2)]
+
+        def w_views(lo, hi):
+            return (w_bf[:, lo:hi, :].rearrange("p (c i) t -> p c t i", i=4),
+                    w_planes[:, :, lo:hi].rearrange("p t (c i) -> p c t i", i=4))
+
+        nc.scalar.activation(*w_views(0, I_CUT), ACT.Copy)
+        for lo, hi in ((I_CUT, W_CUT), (W_CUT, N // 2), (N // 2, N)):
+            nc.vector.tensor_copy(*w_views(lo, hi))
         w_codes = sb("w_codes", [P, N], U32)
         w_scales = sb("w_scales", [P, N], U8)
-        nc.vector.quantize_mx(
-            out=w_codes[:].bitcast(E4M3), scales=w_scales[:], in_=w_bf[:].rearrange("p i t -> p (i t)"))
+        for cols in halves:
+            nc.vector.quantize_mx(
+                out=w_codes[:, cols].bitcast(E4M3), scales=w_scales[:, cols],
+                in_=w_bf[:, cols, :].rearrange("p i t -> p (i t)"))
 
         x_bf = sb("x_bf", [P, PACK, P, PACK], BF16)
 
@@ -133,15 +156,13 @@ def tile_attend_glch_adam_kernel(tc, xT, wT, y, wt, xm, mT, vT, offs, out_0, out
         nc.vector.tensor_copy(*x_views(1, X_CUT, P // 2))
         x_codes = sb("x_codes", [P, R], U32)
         x_scales = sb("x_scales", [P, R], U8)
-        for h in range(2):
-            rows = slice(h * 2 * P, (h + 1) * 2 * P)
-            nc.vector.quantize_mx(
-                out=x_codes[:, rows].bitcast(E4M3), scales=x_scales[:, rows],
-                in_=x_bf[:, 2 * h:2 * h + 2, :, :].rearrange("p t m j -> p (t m j)"))
+        nc.vector.quantize_mx(
+            out=x_codes[:].bitcast(E4M3), scales=x_scales[:], in_=x_bf[:].rearrange("p t m j -> p (t m j)"))
 
         g_codes = sb("g_codes", [P, N], U32)
         g_scales = sb("g_scales", [P, N], U8)
         g_bf = sb("g_bf", [P, N, PACK], BF16)
+        m_picked = bands("m_picked", N)
         diffs = [sb("diff%d" % c, [P, PACK, CHUNK], F32) for c in range(CHUNKS)]
         for c in range(CHUNKS):
             cols = slice(c * CHUNK, (c + 1) * CHUNK)
@@ -158,34 +179,38 @@ def tile_attend_glch_adam_kernel(tc, xT, wT, y, wt, xm, mT, vT, offs, out_0, out
         for c in range(CHUNKS):
             cols = slice(c * CHUNK, (c + 1) * CHUNK)
             diff = diffs[c]
-            if c == 0:
-                th = sb("th0", [P, CHUNK, PACK], F32)
+            if c < 2:
+                th = sb("th%d" % c, [P, CHUNK, PACK], F32)
                 nc.scalar.activation(th[:], diff[:].rearrange("p t i -> p i t"), ACT.Tanh)
-                nc.gpsimd.tensor_tensor(
-                    g_bf[:, cols, :], th[:], wt_sb[:].unsqueeze(1).to_broadcast([P, CHUNK, PACK]), ALU.mult)
+                width = CHUNK if c == 0 else G_CUT
+                lo = c * CHUNK
+                nc.gpsimd.tensor_tensor(g_bf[:, lo:lo + width, :], th[:, :width, :], wt_wide[:, :width, :], ALU.mult)
+                if width < CHUNK:
+                    nc.vector.tensor_tensor(
+                        g_bf[:, lo + width:lo + CHUNK, :], th[:, width:, :],
+                        wt_bank[:].rearrange("p t n -> p n t")[:, 0:1, :].to_broadcast([P, CHUNK - width, PACK]), ALU.mult)
             else:
-                nc.scalar.activation(diff[:], diff[:], ACT.Tanh)
+                th = diff[:] if c == 2 else m_picked[0][:].rearrange("p (t i) -> p t i", t=PACK)
+                nc.scalar.activation(th, diff[:], ACT.Tanh)
                 nc.vector.tensor_tensor(
                     g_bf[:, cols, :].rearrange("p (c i) t -> p c t i", i=4),
-                    diff[:].rearrange("p t (c i) -> p c t i", i=4),
-                    wt_sb[:].unsqueeze(1).unsqueeze(3).to_broadcast([P, CHUNK // 4, PACK, 4]), ALU.mult)
+                    th.rearrange("p t (c i) -> p c t i", i=4),
+                    wt_bank[:, :, 0:1].unsqueeze(1).to_broadcast([P, CHUNK // 4, PACK, 4]), ALU.mult)
 
-        xm_codes = [sb("xm_codes%d" % k, [P, P], U32) for k in range(BANDS)]
-        xm_scales = [sb("xm_scales%d" % k, [P, P], U8) for k in range(BANDS)]
-
-        def quantise_xm(k):
-            xm_bf = sb("xm_bf%d" % k, [P, P, PACK], BF16)
-            dst = xm_bf[:].rearrange("p (c i) t -> p c t i", i=4)
-            raw = xm_raw[k // 2][:, :, (k % 2) * P:(k % 2 + 1) * P]
-            src = raw.rearrange("p t (c i) -> p c t i", i=4)
-            if k < 2:
-                nc.scalar.activation(dst, src, ACT.Copy)
-            else:
-                nc.gpsimd.tensor_copy(xm_bf[:], raw.rearrange("p t d -> p d t"))
+        xm_codes = [sb("xm_codes%d" % h, [P, 2 * P], U32, tag="y_sb1" if h == 0 else None) for h in range(2)]
+        xm_scales = [sb("xm_scales%d" % h, [P, 2 * P], U8) for h in range(2)]
+        for h in range(2):
+            xm_bf = sb("xm_bf%d" % h, [P, 2 * P, PACK], BF16, tag="diff3" if h == 1 else None)
+            cut = 2 * P if h == 0 else P
+            nc.scalar.activation(
+                xm_bf[:, :cut, :].rearrange("p (c i) t -> p c t i", i=4),
+                xm_raw[h][:, :, :cut].rearrange("p t (c i) -> p c t i", i=4), ACT.Copy)
+            if cut < 2 * P:
+                nc.vector.tensor_copy(
+                    xm_bf[:, cut:, :].rearrange("p (c i) t -> p c t i", i=4),
+                    xm_raw[h][:, :, cut:].rearrange("p t (c i) -> p c t i", i=4))
             nc.vector.quantize_mx(
-                out=xm_codes[k][:].bitcast(E4M3), scales=xm_scales[k][:], in_=xm_bf[:].rearrange("p d t -> p (d t)"))
-
-        quantise_xm(0)
+                out=xm_codes[h][:].bitcast(E4M3), scales=xm_scales[h][:], in_=xm_bf[:].rearrange("p d t -> p (d t)"))
         nc.vector.quantize_mx(
             out=g_codes[:].bitcast(E5M2), scales=g_scales[:], in_=g_bf[:].rearrange("p i t -> p (i t)"))
 
@@ -202,47 +227,55 @@ def tile_attend_glch_adam_kernel(tc, xT, wT, y, wt, xm, mT, vT, offs, out_0, out
         def gather_scaled(dst, pair, scale):
             nc.vector.tensor_scalar(dst[:], pair[:].indirect(offsets[:]), scale, 0.0, ALU.mult, ALU.add)
 
-        m_picked, nm = [bands(name, N) for name in ("m_picked", "nm")]
-        v_picked_pairs = [sb("v_picked%d" % h, [P, 2 * N], F32) for h in range(2)]
+        nm = bands("nm", N)
+        v_picked_pairs = [sb("v_picked%d" % h, [P, 2 * N], F32, tag="g_bf" if h == 0 else None) for h in range(2)]
         nv_pairs = [sb("nv%d" % h, [P, 2 * N], F32) for h in range(2)]
         v_picked = [v_picked_pairs[k // 2][:, (k % 2) * N:(k % 2 + 1) * N] for k in range(BANDS)]
         nv = [nv_pairs[k // 2][:, (k % 2) * N:(k % 2 + 1) * N] for k in range(BANDS)]
         ratio = v_picked[2:] + v_picked[:2]
         dw = []
         for k in range(BANDS):
-            if k > 0:
-                quantise_xm(k)
+            rows = slice((k % 2) * P, (k % 2 + 1) * P)
             bank = psum.tile([P, N], F32, name="dw%d" % k)
             nc.tensor.matmul_mx(
-                out=bank[:], lhsT=xm_codes[k][:].bitcast(E4M3), lhsT_scale=xm_scales[k][:],
+                out=bank[:], lhsT=xm_codes[k // 2][:, rows].bitcast(E4M3), lhsT_scale=xm_scales[k // 2][:, rows],
                 rhs=g_codes[:].bitcast(E5M2), rhs_scale=g_scales[:], start=True, stop=True)
             dw.append(bank)
-        unit = [1.0, 1.0, RHO, 1.0]
+        unit = [1.0, 1.0, 1.0, RHO]
         product = [ratio[0], ratio[1], ratio[2], nm[1]]
+
+        def pick_m(k):
+            if k in (0, 3):
+                gather(k == 0, m_picked[k], m_old[k])
+            else:
+                gather_scaled(m_picked[k], m_pairs[k // 2], BETA)
 
         def new_m(k):
             if k in (0, 3):
-                gather(False, m_picked[k], m_old[k])
                 nc.vector.scalar_tensor_tensor(nm[k][:], dw[k][:], -1.0, m_picked[k][:], ALU.mult, ALU.subtract)
             else:
-                gather_scaled(m_picked[k], m_pairs[k // 2], BETA)
                 nc.vector.scalar_tensor_tensor(nm[k][:], dw[k][:], 1.0 - BETA, m_picked[k][:], ALU.mult, ALU.add)
 
         def second_root(k):
             nc.scalar.activation(
                 ratio[k][:], ratio[k][:], ACT.Abs_reciprocal_sqrt, bias=eps_col[:], scale=unit[k] / RATE ** 2)
 
-        for k in range(BANDS):
-            if k < 2:
-                gather(True, v_picked[k], v_old[k], scale=RHO)
-            elif k == 2:
-                gather(False, v_picked[k], v_old[k])
+        pick_m(0)
+        for k in (0, 1, 3, 2):
+            if k in (0, 3):
+                gather(k == 0, v_picked[k], v_old[k], scale=RHO)
             else:
-                gather_scaled(v_picked[k], v_pair, RHO)
+                gather_scaled(v_picked[k], v_pairs[k // 2], RHO)
             nc.scalar.activation(nv[k][:], dw[k][:], ACT.Square, scale=math.sqrt((1.0 - RHO) / unit[k]))
             nc.gpsimd.tensor_tensor(nv[k][:], nv[k][:], v_picked[k][:], ALU.add)
-        for k in (0, 3, 1, 2):
-            new_m(k)
+            if k == 1:
+                new_m(0)
+        pick_m(3)
+        pick_m(2)
+        new_m(3)
+        pick_m(1)
+        new_m(2)
+        new_m(1)
         scatter_and_store(True, m_new, nm[0], out_1, 0, scale=-BETA)
         for k in range(BANDS):
             if k % 2 == 0:
@@ -250,13 +283,13 @@ def tile_attend_glch_adam_kernel(tc, xT, wT, y, wt, xm, mT, vT, offs, out_0, out
                     v_picked_pairs[1 - k // 2][:], nv_pairs[k // 2][:], ACT.Abs_reciprocal_sqrt, bias=tiny_col[:])
             nc.gpsimd.tensor_scalar(ratio[k][:], ratio[k][:], 2.0 * EPS / math.sqrt(unit[k]), 1.0, ALU.mult, ALU.add)
             nc.gpsimd.tensor_tensor(ratio[k][:], ratio[k][:], nv[k][:], ALU.mult)
-        scatter_and_store(True, v_new, nv[2], out_2, 2, scale=RHO)
+        scatter_and_store(True, v_new, nv[3], out_2, 3, scale=RHO)
         second_root(0)
         second_root(1)
         scatter_and_store(True, m_new, nm[3], out_1, 3, scale=-BETA)
         second_root(2)
         second_root(3)
-        for k in (0, 1, 3):
+        for k in (0, 1, 2):
             scatter_and_store(False, v_new, nv[k], out_2, k)
         for k in (1, 2):
             scatter_and_store(False, m_new, nm[k], out_1, k)

@@ -23,9 +23,10 @@ PACK = 4
 BANDS = D // P
 CHUNK = 128
 CHUNKS = N // CHUNK
-X_CUT = 28
+X_CUT = 20
 G_CUT = 96
-I_CUT = 96
+V_CUT = 384
+I_CUT = 128
 W_CUT = 192
 TINY = 1e-30
 RATE = LR * BETA
@@ -162,7 +163,6 @@ def tile_attend_glch_adam_kernel(tc, xT, wT, y, wt, xm, mT, vT, offs, out_0, out
         g_codes = sb("g_codes", [P, N], U32)
         g_scales = sb("g_scales", [P, N], U8)
         g_bf = sb("g_bf", [P, N, PACK], BF16)
-        m_picked = bands("m_picked", N)
         diffs = [sb("diff%d" % c, [P, PACK, CHUNK], F32) for c in range(CHUNKS)]
         for c in range(CHUNKS):
             cols = slice(c * CHUNK, (c + 1) * CHUNK)
@@ -190,7 +190,7 @@ def tile_attend_glch_adam_kernel(tc, xT, wT, y, wt, xm, mT, vT, offs, out_0, out
                         g_bf[:, lo + width:lo + CHUNK, :], th[:, width:, :],
                         wt_bank[:].rearrange("p t n -> p n t")[:, 0:1, :].to_broadcast([P, CHUNK - width, PACK]), ALU.mult)
             else:
-                th = diff[:] if c == 2 else m_picked[0][:].rearrange("p (t i) -> p t i", t=PACK)
+                th = diff[:]
                 nc.scalar.activation(th, diff[:], ACT.Tanh)
                 nc.vector.tensor_tensor(
                     g_bf[:, cols, :].rearrange("p (c i) t -> p c t i", i=4),
@@ -199,20 +199,22 @@ def tile_attend_glch_adam_kernel(tc, xT, wT, y, wt, xm, mT, vT, offs, out_0, out
 
         xm_codes = [sb("xm_codes%d" % h, [P, 2 * P], U32, tag="y_sb1" if h == 0 else None) for h in range(2)]
         xm_scales = [sb("xm_scales%d" % h, [P, 2 * P], U8) for h in range(2)]
-        for h in range(2):
+
+        def quantise_xm(h):
             xm_bf = sb("xm_bf%d" % h, [P, 2 * P, PACK], BF16, tag="diff3" if h == 1 else None)
-            cut = 2 * P if h == 0 else P
-            nc.scalar.activation(
-                xm_bf[:, :cut, :].rearrange("p (c i) t -> p c t i", i=4),
-                xm_raw[h][:, :, :cut].rearrange("p t (c i) -> p c t i", i=4), ACT.Copy)
-            if cut < 2 * P:
-                nc.vector.tensor_copy(
-                    xm_bf[:, cut:, :].rearrange("p (c i) t -> p c t i", i=4),
-                    xm_raw[h][:, :, cut:].rearrange("p t (c i) -> p c t i", i=4))
+            dst = xm_bf[:].rearrange("p (c i) t -> p c t i", i=4)
+            src = xm_raw[h][:].rearrange("p t (c i) -> p c t i", i=4)
+            if h == 0:
+                nc.scalar.activation(dst, src, ACT.Copy)
+            else:
+                nc.vector.tensor_copy(dst, src)
             nc.vector.quantize_mx(
                 out=xm_codes[h][:].bitcast(E4M3), scales=xm_scales[h][:], in_=xm_bf[:].rearrange("p d t -> p (d t)"))
+
+        quantise_xm(0)
         nc.vector.quantize_mx(
             out=g_codes[:].bitcast(E5M2), scales=g_scales[:], in_=g_bf[:].rearrange("p i t -> p (i t)"))
+        quantise_xm(1)
 
         def scatter_and_store(on_scalar, window, values, out, k, scale=1.0):
             if on_scalar:
@@ -227,8 +229,8 @@ def tile_attend_glch_adam_kernel(tc, xT, wT, y, wt, xm, mT, vT, offs, out_0, out
         def gather_scaled(dst, pair, scale):
             nc.vector.tensor_scalar(dst[:], pair[:].indirect(offsets[:]), scale, 0.0, ALU.mult, ALU.add)
 
-        nm = bands("nm", N)
-        v_picked_pairs = [sb("v_picked%d" % h, [P, 2 * N], F32, tag="g_bf" if h == 0 else None) for h in range(2)]
+        m_picked, nm = bands("m_picked", N), bands("nm", N)
+        v_picked_pairs = [sb("v_picked%d" % h, [P, 2 * N], F32) for h in range(2)]
         nv_pairs = [sb("nv%d" % h, [P, 2 * N], F32) for h in range(2)]
         v_picked = [v_picked_pairs[k // 2][:, (k % 2) * N:(k % 2 + 1) * N] for k in range(BANDS)]
         nv = [nv_pairs[k // 2][:, (k % 2) * N:(k % 2 + 1) * N] for k in range(BANDS)]
@@ -289,7 +291,10 @@ def tile_attend_glch_adam_kernel(tc, xT, wT, y, wt, xm, mT, vT, offs, out_0, out
         scatter_and_store(True, m_new, nm[3], out_1, 3, scale=-BETA)
         second_root(2)
         second_root(3)
-        for k in (0, 1, 2):
+        nc.vector.tensor_copy(v_new[0][:].indirect(slots(0, V_CUT)), nv[0][:, :V_CUT])
+        nc.scalar.activation(v_new[0][:].indirect(slots(V_CUT, N)), nv[0][:, V_CUT:], ACT.Copy)
+        nc.scalar.dma_start(out_2[0:P, :], v_new[0][:])
+        for k in (1, 2):
             scatter_and_store(False, v_new, nv[k], out_2, k)
         for k in (1, 2):
             scatter_and_store(False, m_new, nm[k], out_1, k)

@@ -25,10 +25,9 @@ CHUNK = 128
 CHUNKS = N // CHUNK
 X_CUT = 20
 G_CUT = 96
-V_CUT = 384
 I_CUT = 128
 W_CUT = 192
-TINY = 1e-30
+TINY = 2.0 ** -80
 RATE = LR * BETA
 
 
@@ -291,10 +290,7 @@ def tile_attend_glch_adam_kernel(tc, xT, wT, y, wt, xm, mT, vT, offs, out_0, out
         scatter_and_store(True, m_new, nm[3], out_1, 3, scale=-BETA)
         second_root(2)
         second_root(3)
-        nc.vector.tensor_copy(v_new[0][:].indirect(slots(0, V_CUT)), nv[0][:, :V_CUT])
-        nc.scalar.activation(v_new[0][:].indirect(slots(V_CUT, N)), nv[0][:, V_CUT:], ACT.Copy)
-        nc.scalar.dma_start(out_2[0:P, :], v_new[0][:])
-        for k in (1, 2):
+        for k in (0, 1, 2):
             scatter_and_store(False, v_new, nv[k], out_2, k)
         for k in (1, 2):
             scatter_and_store(False, m_new, nm[k], out_1, k)

@@ -23,10 +23,14 @@ PACK = 4
 BANDS = D // P
 CHUNK = 128
 CHUNKS = N // CHUNK
-X_CUT = 20
-G_CUT = 96
-I_CUT = 128
-W_CUT = 192
+RUN = 4
+LIST_ROWS = 16
+
+W_GATHER_ON_SCALAR = 192
+W_WEAVE_ON_SCALAR = 128
+X_CAST_ON_SCALAR = 20
+G_WEIGH_ON_GPSIMD = 96
+
 TINY = 2.0 ** -80
 RATE = LR * BETA
 
@@ -40,13 +44,19 @@ def tile_attend_glch_adam_kernel(tc, xT, wT, y, wt, xm, mT, vT, offs, out_0, out
         def sb(name, shape, dtype, tag=None):
             return keep.tile(shape, dtype, name=name, tag=tag or name, align_bytes=64)
 
-        def bands(name, width):
+        def four(name, width):
             return [sb("%s%d" % (name, k), [P, width], F32) for k in range(BANDS)]
 
+        def woven(tile):
+            return tile.rearrange("p (c i) t -> p c t i", i=RUN)
+
+        def by_places(tile):
+            return tile.rearrange("p t (c i) -> p c t i", i=RUN)
+
         w_rows = wT.rearrange("(p j) t -> j p t", j=PACK)
-        w_raw = bands("w_raw", T)
+        w_raw = four("w_raw", T)
         nc.sync.dma_start(w_raw[0][:], w_rows[0])
-        offsets = keep.tile([P, N // 16], U16, name="offsets")
+        offsets = keep.tile([P, N // LIST_ROWS], U16, name="offsets")
         nc.sync.dma_start(offsets[:], offs)
         nc.sync.dma_start(w_raw[1][:], w_rows[1])
         wt_row = sb("wt_row", [P, R], F32)
@@ -62,7 +72,7 @@ def tile_attend_glch_adam_kernel(tc, xT, wT, y, wt, xm, mT, vT, offs, out_0, out
         y_sb = [sb("y_sb%d" % h, [P, PACK, N // 2], F32) for h in range(2)]
         xm_rows = xm[0].rearrange("(p t) d -> p t d", t=PACK)
         xm_raw = [sb("xm_raw%d" % h, [P, PACK, D // 2], F32) for h in range(2)]
-        m_new, v_new, step = [bands(name, T) for name in ("m_new", "v_new", "step")]
+        m_new, v_new, step = [four(name, T) for name in ("m_new", "v_new", "step")]
         m_pairs = [sb("m_pair%d" % h, [P, 2 * T], F32) for h in range(2)]
         v_pairs = [sb("v_pair%d" % h, [P, 2 * T], F32) for h in range(2)]
         m_old = [m_pairs[0][:, T:], m_pairs[0][:, :T], m_pairs[1][:, :T], m_pairs[1][:, T:]]
@@ -71,7 +81,7 @@ def tile_attend_glch_adam_kernel(tc, xT, wT, y, wt, xm, mT, vT, offs, out_0, out
         def load_band(tiles, table, k):
             nc.sync.dma_start(tiles[k][:, :], table[k * P:(k + 1) * P, :])
 
-        def load_pair(tile, table):
+        def load_bands_2_and_3(tile, table):
             nc.sync.dma_start(
                 tile[:].rearrange("p (b t) -> p b t", b=2), table[2 * P:, :].rearrange("(b p) t -> p b t", b=2))
 
@@ -85,9 +95,9 @@ def tile_attend_glch_adam_kernel(tc, xT, wT, y, wt, xm, mT, vT, offs, out_0, out
         load_band(m_old, mT, 0)
         load_band(v_old, vT, 0)
         load_band(v_old, vT, 1)
-        load_pair(v_pairs[1], vT)
+        load_bands_2_and_3(v_pairs[1], vT)
         load_band(m_new, mT, 0)
-        load_pair(m_pairs[1], mT)
+        load_bands_2_and_3(m_pairs[1], mT)
         load_band(v_new, vT, 3)
         load_band(m_old, mT, 1)
         load_band(m_new, mT, 3)
@@ -110,40 +120,40 @@ def tile_attend_glch_adam_kernel(tc, xT, wT, y, wt, xm, mT, vT, offs, out_0, out
         wt_bank = psum.tile([P, PACK, P], F32, name="wt_bank", tag="dw3")
         for t in range(PACK):
             nc.tensor.transpose(wt_bank[:, t, :], wt_row[:, t:R:PACK], ident[:])
+        wt_words = wt_bank[:].rearrange("p t n -> p n t")[:, 0:1, :]
         wt_wide = sb("wt_wide", [P, CHUNK, PACK], F32)
-        nc.scalar.activation(wt_wide[:], wt_bank[:].rearrange("p t n -> p n t")[:, 0:1, :].to_broadcast([P, CHUNK, PACK]), ACT.Copy)
+        nc.scalar.activation(wt_wide[:], wt_words.to_broadcast([P, CHUNK, PACK]), ACT.Copy)
 
         def slots(lo, hi):
-            return offsets[:, lo // 16:hi // 16]
+            return offsets[:, lo // LIST_ROWS:hi // LIST_ROWS]
 
-        def gather(on_scalar, dst, window, lo=0, hi=N, scale=1.0):
-            if on_scalar:
-                nc.scalar.activation(dst[:, lo:hi], window[:, :].indirect(slots(lo, hi)), ACT.Copy, scale=scale)
-            else:
-                nc.vector.tensor_copy(dst[:, lo:hi], window[:, :].indirect(slots(lo, hi)))
+        def gather_on_scalar(dst, window, lo=0, hi=N, scale=1.0):
+            nc.scalar.activation(dst[:, lo:hi], window[:, :].indirect(slots(lo, hi)), ACT.Copy, scale=scale)
 
-        w_planes = sb("w_planes", [P, PACK, N], BF16)
-        gather(False, w_planes[:, 0, :], w_raw[0])
-        gather(True, w_planes[:, 1, :], w_raw[1])
-        gather(False, w_planes[:, 2, :], w_raw[2])
-        gather(True, w_planes[:, 3, :], w_raw[3], 0, W_CUT)
-        gather(False, w_planes[:, 3, :], w_raw[3], W_CUT, N)
+        def gather_on_vector(dst, window, lo=0, hi=N):
+            nc.vector.tensor_copy(dst[:, lo:hi], window[:, :].indirect(slots(lo, hi)))
+
+        def gather_scaled_on_vector(dst, pair, scale):
+            nc.vector.tensor_scalar(dst[:], pair[:].indirect(offsets[:]), scale, 0.0, ALU.mult, ALU.add)
+
+        def quantise(codes, scales, fmt, src):
+            nc.vector.quantize_mx(out=codes.bitcast(fmt), scales=scales, in_=src)
+
+        w_places = sb("w_places", [P, PACK, N], BF16)
+        gather_on_vector(w_places[:, 0, :], w_raw[0])
+        gather_on_scalar(w_places[:, 1, :], w_raw[1])
+        gather_on_vector(w_places[:, 2, :], w_raw[2])
+        gather_on_scalar(w_places[:, 3, :], w_raw[3], 0, W_GATHER_ON_SCALAR)
+        gather_on_vector(w_places[:, 3, :], w_raw[3], W_GATHER_ON_SCALAR, N)
         w_bf = sb("w_bf", [P, N, PACK], BF16)
-        halves = [slice(h * (N // 2), (h + 1) * (N // 2)) for h in range(2)]
-
-        def w_views(lo, hi):
-            return (w_bf[:, lo:hi, :].rearrange("p (c i) t -> p c t i", i=4),
-                    w_planes[:, :, lo:hi].rearrange("p t (c i) -> p c t i", i=4))
-
-        nc.scalar.activation(*w_views(0, I_CUT), ACT.Copy)
-        for lo, hi in ((I_CUT, W_CUT), (W_CUT, N // 2), (N // 2, N)):
-            nc.vector.tensor_copy(*w_views(lo, hi))
+        nc.scalar.copy(woven(w_bf[:, :W_WEAVE_ON_SCALAR, :]), by_places(w_places[:, :, :W_WEAVE_ON_SCALAR]))
+        for lo, hi in ((W_WEAVE_ON_SCALAR, W_GATHER_ON_SCALAR), (W_GATHER_ON_SCALAR, N // 2), (N // 2, N)):
+            nc.vector.tensor_copy(woven(w_bf[:, lo:hi, :]), by_places(w_places[:, :, lo:hi]))
         w_codes = sb("w_codes", [P, N], U32)
         w_scales = sb("w_scales", [P, N], U8)
-        for cols in halves:
-            nc.vector.quantize_mx(
-                out=w_codes[:, cols].bitcast(E4M3), scales=w_scales[:, cols],
-                in_=w_bf[:, cols, :].rearrange("p i t -> p (i t)"))
+        for lo in (0, N // 2):
+            cols = slice(lo, lo + N // 2)
+            quantise(w_codes[:, cols], w_scales[:, cols], E4M3, w_bf[:, cols, :].rearrange("p i t -> p (i t)"))
 
         x_bf = sb("x_bf", [P, PACK, P, PACK], BF16)
 
@@ -152,12 +162,11 @@ def tile_attend_glch_adam_kernel(tc, xT, wT, y, wt, xm, mT, vT, offs, out_0, out
             return dst, x_raw[h][:].rearrange("p j (m t) -> p m j t", t=PACK)[:, lo:hi, :, :]
 
         nc.scalar.activation(*x_views(0, 0, P // 2), ACT.Copy)
-        nc.scalar.activation(*x_views(1, 0, X_CUT), ACT.Copy)
-        nc.vector.tensor_copy(*x_views(1, X_CUT, P // 2))
+        nc.scalar.activation(*x_views(1, 0, X_CAST_ON_SCALAR), ACT.Copy)
+        nc.vector.tensor_copy(*x_views(1, X_CAST_ON_SCALAR, P // 2))
         x_codes = sb("x_codes", [P, R], U32)
         x_scales = sb("x_scales", [P, R], U8)
-        nc.vector.quantize_mx(
-            out=x_codes[:].bitcast(E4M3), scales=x_scales[:], in_=x_bf[:].rearrange("p t m j -> p (t m j)"))
+        quantise(x_codes[:], x_scales[:], E4M3, x_bf[:].rearrange("p t m j -> p (t m j)"))
 
         g_codes = sb("g_codes", [P, N], U32)
         g_scales = sb("g_scales", [P, N], U8)
@@ -175,65 +184,40 @@ def tile_attend_glch_adam_kernel(tc, xT, wT, y, wt, xm, mT, vT, offs, out_0, out
                     start=True, stop=True)
             y_part = y_sb[c // 2][:, :, (c % 2) * CHUNK:(c % 2 + 1) * CHUNK]
             nc.vector.tensor_tensor(diffs[c][:], a, y_part, ALU.subtract)
-        for c in range(CHUNKS):
-            cols = slice(c * CHUNK, (c + 1) * CHUNK)
-            diff = diffs[c]
-            if c < 2:
-                th = sb("th%d" % c, [P, CHUNK, PACK], F32)
-                nc.scalar.activation(th[:], diff[:].rearrange("p t i -> p i t"), ACT.Tanh)
-                width = CHUNK if c == 0 else G_CUT
-                lo = c * CHUNK
-                nc.gpsimd.tensor_tensor(g_bf[:, lo:lo + width, :], th[:, :width, :], wt_wide[:, :width, :], ALU.mult)
-                if width < CHUNK:
-                    nc.vector.tensor_tensor(
-                        g_bf[:, lo + width:lo + CHUNK, :], th[:, width:, :],
-                        wt_bank[:].rearrange("p t n -> p n t")[:, 0:1, :].to_broadcast([P, CHUNK - width, PACK]), ALU.mult)
-            else:
-                th = diff[:]
-                nc.scalar.activation(th, diff[:], ACT.Tanh)
-                nc.vector.tensor_tensor(
-                    g_bf[:, cols, :].rearrange("p (c i) t -> p c t i", i=4),
-                    th.rearrange("p t (c i) -> p c t i", i=4),
-                    wt_bank[:, :, 0:1].unsqueeze(1).to_broadcast([P, CHUNK // 4, PACK, 4]), ALU.mult)
+        for c, width in ((0, CHUNK), (1, G_WEIGH_ON_GPSIMD)):
+            lo = c * CHUNK
+            th = sb("th%d" % c, [P, CHUNK, PACK], F32)
+            nc.scalar.activation(woven(th[:]), by_places(diffs[c][:]), ACT.Tanh)
+            nc.gpsimd.tensor_tensor(g_bf[:, lo:lo + width, :], th[:, :width, :], wt_wide[:, :width, :], ALU.mult)
+        nc.vector.tensor_tensor(
+            g_bf[:, lo + width:lo + CHUNK, :], th[:, width:, :], wt_words.to_broadcast([P, CHUNK - width, PACK]),
+            ALU.mult)
+        for c in (2, 3):
+            nc.scalar.activation(diffs[c][:], diffs[c][:], ACT.Tanh)
+            nc.vector.tensor_tensor(
+                woven(g_bf[:, c * CHUNK:(c + 1) * CHUNK, :]), by_places(diffs[c][:]),
+                wt_bank[:, :, 0:1].unsqueeze(1).to_broadcast([P, CHUNK // RUN, PACK, RUN]), ALU.mult)
 
-        xm_codes = [sb("xm_codes%d" % h, [P, 2 * P], U32, tag="y_sb1" if h == 0 else None) for h in range(2)]
+        xm_codes = [sb("xm_codes%d" % h, [P, 2 * P], U32) for h in range(2)]
         xm_scales = [sb("xm_scales%d" % h, [P, 2 * P], U8) for h in range(2)]
 
-        def quantise_xm(h):
-            xm_bf = sb("xm_bf%d" % h, [P, 2 * P, PACK], BF16, tag="diff3" if h == 1 else None)
-            dst = xm_bf[:].rearrange("p (c i) t -> p c t i", i=4)
-            src = xm_raw[h][:].rearrange("p t (c i) -> p c t i", i=4)
-            if h == 0:
-                nc.scalar.activation(dst, src, ACT.Copy)
-            else:
-                nc.vector.tensor_copy(dst, src)
-            nc.vector.quantize_mx(
-                out=xm_codes[h][:].bitcast(E4M3), scales=xm_scales[h][:], in_=xm_bf[:].rearrange("p d t -> p (d t)"))
+        def quantise_xm(h, xm_bf):
+            quantise(xm_codes[h][:], xm_scales[h][:], E4M3, xm_bf[:].rearrange("p d t -> p (d t)"))
 
-        quantise_xm(0)
-        nc.vector.quantize_mx(
-            out=g_codes[:].bitcast(E5M2), scales=g_scales[:], in_=g_bf[:].rearrange("p i t -> p (i t)"))
-        quantise_xm(1)
+        xm_early = sb("xm_bf0", [P, 2 * P, PACK], BF16)
+        nc.scalar.activation(woven(xm_early[:, :P, :]), by_places(xm_raw[0][:, :, :P]), ACT.Copy)
+        nc.vector.tensor_copy(woven(xm_early[:, P:, :]), by_places(xm_raw[0][:, :, P:]))
+        quantise_xm(0, xm_early)
+        quantise(g_codes[:], g_scales[:], E5M2, g_bf[:].rearrange("p i t -> p (i t)"))
+        xm_late = sb("xm_bf1", [P, 2 * P, PACK], BF16, tag="diff3")
+        nc.vector.tensor_copy(woven(xm_late[:]), by_places(xm_raw[1][:]))
+        quantise_xm(1, xm_late)
 
-        def scatter_and_store(on_scalar, window, values, out, k, scale=1.0):
-            if on_scalar:
-                for lo in (0, N // 2):
-                    nc.scalar.activation(
-                        window[k][:].indirect(slots(lo, lo + N // 2)), values[:, lo:lo + N // 2], ACT.Copy, scale=scale)
-                nc.scalar.dma_start(out[k * P:(k + 1) * P, :], window[k][:])
-            else:
-                nc.vector.tensor_copy(window[k][:].indirect(offsets[:]), values[:])
-                nc.sync.dma_start(out[k * P:(k + 1) * P, :], window[k][:])
-
-        def gather_scaled(dst, pair, scale):
-            nc.vector.tensor_scalar(dst[:], pair[:].indirect(offsets[:]), scale, 0.0, ALU.mult, ALU.add)
-
-        m_picked, nm = bands("m_picked", N), bands("nm", N)
+        m_picked, nm = four("m_picked", N), four("nm", N)
         v_picked_pairs = [sb("v_picked%d" % h, [P, 2 * N], F32) for h in range(2)]
         nv_pairs = [sb("nv%d" % h, [P, 2 * N], F32) for h in range(2)]
         v_picked = [v_picked_pairs[k // 2][:, (k % 2) * N:(k % 2 + 1) * N] for k in range(BANDS)]
         nv = [nv_pairs[k // 2][:, (k % 2) * N:(k % 2 + 1) * N] for k in range(BANDS)]
-        ratio = v_picked[2:] + v_picked[:2]
         dw = []
         for k in range(BANDS):
             rows = slice((k % 2) * P, (k % 2 + 1) * P)
@@ -242,58 +226,83 @@ def tile_attend_glch_adam_kernel(tc, xT, wT, y, wt, xm, mT, vT, offs, out_0, out
                 out=bank[:], lhsT=xm_codes[k // 2][:, rows].bitcast(E4M3), lhsT_scale=xm_scales[k // 2][:, rows],
                 rhs=g_codes[:].bitcast(E5M2), rhs_scale=g_scales[:], start=True, stop=True)
             dw.append(bank)
-        unit = [1.0, 1.0, 1.0, RHO]
-        product = [ratio[0], ratio[1], ratio[2], nm[1]]
 
-        def pick_m(k):
-            if k in (0, 3):
-                gather(k == 0, m_picked[k], m_old[k])
-            else:
-                gather_scaled(m_picked[k], m_pairs[k // 2], BETA)
+        nv_unit = [1.0, 1.0, 1.0, RHO]
+        root = v_picked[2:] + v_picked[:2]
+        step_picked = [root[0], root[1], root[2], nm[1]]
+
+        def scatter_on_scalar(window, values, scale):
+            for lo in (0, N // 2):
+                nc.scalar.activation(
+                    window[:].indirect(slots(lo, lo + N // 2)), values[:, lo:lo + N // 2], ACT.Copy, scale=scale)
+
+        def scatter_on_vector(window, values):
+            nc.vector.tensor_copy(window[:].indirect(offsets[:]), values[:])
+
+        def store(queue, out, windows, k):
+            queue.dma_start(out[k * P:(k + 1) * P, :], windows[k][:])
+
+        def new_v(k):
+            nc.scalar.activation(nv[k][:], dw[k][:], ACT.Square, scale=math.sqrt((1.0 - RHO) / nv_unit[k]))
+            nc.gpsimd.tensor_tensor(nv[k][:], nv[k][:], v_picked[k][:], ALU.add)
 
         def new_m(k):
-            if k in (0, 3):
-                nc.vector.scalar_tensor_tensor(nm[k][:], dw[k][:], -1.0, m_picked[k][:], ALU.mult, ALU.subtract)
-            else:
-                nc.vector.scalar_tensor_tensor(nm[k][:], dw[k][:], 1.0 - BETA, m_picked[k][:], ALU.mult, ALU.add)
+            nc.vector.scalar_tensor_tensor(nm[k][:], dw[k][:], 1.0 - BETA, m_picked[k][:], ALU.mult, ALU.add)
+
+        def new_m_over_minus_beta(k):
+            nc.vector.scalar_tensor_tensor(
+                nm[k][:], dw[k][:], -(1.0 - BETA) / BETA, m_picked[k][:], ALU.mult, ALU.subtract)
 
         def second_root(k):
             nc.scalar.activation(
-                ratio[k][:], ratio[k][:], ACT.Abs_reciprocal_sqrt, bias=eps_col[:], scale=unit[k] / RATE ** 2)
+                root[k][:], root[k][:], ACT.Abs_reciprocal_sqrt, bias=eps_col[:], scale=nv_unit[k] / RATE ** 2)
 
-        pick_m(0)
-        for k in (0, 1, 3, 2):
-            if k in (0, 3):
-                gather(k == 0, v_picked[k], v_old[k], scale=RHO)
-            else:
-                gather_scaled(v_picked[k], v_pairs[k // 2], RHO)
-            nc.scalar.activation(nv[k][:], dw[k][:], ACT.Square, scale=math.sqrt((1.0 - RHO) / unit[k]))
-            nc.gpsimd.tensor_tensor(nv[k][:], nv[k][:], v_picked[k][:], ALU.add)
-            if k == 1:
-                new_m(0)
-        pick_m(3)
-        pick_m(2)
-        new_m(3)
-        pick_m(1)
+        def new_step(k):
+            nc.gpsimd.tensor_tensor(step_picked[k][:], root[k][:], nm[k][:], ALU.mult)
+
+        gather_on_scalar(m_picked[0], m_old[0])
+        gather_on_scalar(v_picked[0], v_old[0], scale=RHO)
+        new_v(0)
+        gather_scaled_on_vector(v_picked[1], v_pairs[0], RHO)
+        new_v(1)
+        new_m_over_minus_beta(0)
+        gather_on_vector(v_picked[3], v_old[3])
+        new_v(3)
+        gather_scaled_on_vector(v_picked[2], v_pairs[1], RHO)
+        new_v(2)
+        gather_on_vector(m_picked[3], m_old[3])
+        gather_scaled_on_vector(m_picked[2], m_pairs[1], BETA)
+        new_m_over_minus_beta(3)
+        gather_scaled_on_vector(m_picked[1], m_pairs[0], BETA)
         new_m(2)
         new_m(1)
-        scatter_and_store(True, m_new, nm[0], out_1, 0, scale=-BETA)
-        for k in range(BANDS):
-            if k % 2 == 0:
-                nc.scalar.activation(
-                    v_picked_pairs[1 - k // 2][:], nv_pairs[k // 2][:], ACT.Abs_reciprocal_sqrt, bias=tiny_col[:])
-            nc.gpsimd.tensor_scalar(ratio[k][:], ratio[k][:], 2.0 * EPS / math.sqrt(unit[k]), 1.0, ALU.mult, ALU.add)
-            nc.gpsimd.tensor_tensor(ratio[k][:], ratio[k][:], nv[k][:], ALU.mult)
-        scatter_and_store(True, v_new, nv[3], out_2, 3, scale=RHO)
+        scatter_on_scalar(m_new[0], nm[0], -BETA)
+        store(nc.sync, out_1, m_new, 0)
+        for h in range(2):
+            nc.scalar.activation(
+                v_picked_pairs[1 - h][:], nv_pairs[h][:], ACT.Abs_reciprocal_sqrt, bias=tiny_col[:])
+            for k in (2 * h, 2 * h + 1):
+                nc.gpsimd.tensor_scalar(
+                    root[k][:], root[k][:], 2.0 * EPS / math.sqrt(nv_unit[k]), 1.0, ALU.mult, ALU.add)
+                nc.gpsimd.tensor_tensor(root[k][:], root[k][:], nv[k][:], ALU.mult)
+        scatter_on_scalar(v_new[3], nv[3], RHO)
+        store(nc.scalar, out_2, v_new, 3)
         second_root(0)
         second_root(1)
-        scatter_and_store(True, m_new, nm[3], out_1, 3, scale=-BETA)
+        scatter_on_scalar(m_new[3], nm[3], -BETA)
+        store(nc.scalar, out_1, m_new, 3)
         second_root(2)
         second_root(3)
         for k in (0, 1, 2):
-            scatter_and_store(False, v_new, nv[k], out_2, k)
+            scatter_on_vector(v_new[k], nv[k])
+            store(nc.sync, out_2, v_new, k)
         for k in (1, 2):
-            scatter_and_store(False, m_new, nm[k], out_1, k)
-        for k in range(BANDS):
-            nc.gpsimd.tensor_tensor(product[k][:], ratio[k][:], nm[k][:], ALU.mult)
-            scatter_and_store(k < 3, step, product[k], out_0, k, scale=1.0 if k == 0 else -1.0 / BETA)
+            scatter_on_vector(m_new[k], nm[k])
+            store(nc.sync, out_1, m_new, k)
+        for k, scale in ((0, 1.0), (1, -1.0 / BETA), (2, -1.0 / BETA)):
+            new_step(k)
+            scatter_on_scalar(step[k], step_picked[k], scale)
+            store(nc.scalar, out_0, step, k)
+        new_step(3)
+        scatter_on_vector(step[3], step_picked[3])
+        store(nc.sync, out_0, step, 3)

@@ -30,6 +30,7 @@ W_GATHER_ON_SCALAR = 192
 W_WEAVE_ON_SCALAR = 128
 X_CAST_ON_SCALAR = 20
 G_WEIGH_ON_GPSIMD = 96
+V_SCATTER_ON_VECTOR = 384
 
 TINY = 2.0 ** -80
 RATE = LR * BETA
@@ -277,7 +278,7 @@ def tile_attend_glch_adam_kernel(tc, xT, wT, y, wt, xm, mT, vT, offs, out_0, out
         new_m(2)
         new_m(1)
         scatter_on_scalar(m_new[0], nm[0], -BETA)
-        store(nc.sync, out_1, m_new, 0)
+        store(nc.scalar, out_1, m_new, 0)
         for h in range(2):
             nc.scalar.activation(
                 v_picked_pairs[1 - h][:], nv_pairs[h][:], ACT.Abs_reciprocal_sqrt, bias=tiny_col[:])
@@ -293,7 +294,11 @@ def tile_attend_glch_adam_kernel(tc, xT, wT, y, wt, xm, mT, vT, offs, out_0, out
         store(nc.scalar, out_1, m_new, 3)
         second_root(2)
         second_root(3)
-        for k in (0, 1, 2):
+        nc.vector.tensor_copy(v_new[0][:].indirect(slots(0, V_SCATTER_ON_VECTOR)), nv[0][:, :V_SCATTER_ON_VECTOR])
+        nc.scalar.activation(
+            v_new[0][:].indirect(slots(V_SCATTER_ON_VECTOR, N)), nv[0][:, V_SCATTER_ON_VECTOR:], ACT.Copy)
+        store(nc.scalar, out_2, v_new, 0)
+        for k in (1, 2):
             scatter_on_vector(v_new[k], nv[k])
             store(nc.sync, out_2, v_new, k)
         for k in (1, 2):

@@ -30,7 +30,9 @@ W_GATHER_ON_SCALAR = 192
 W_WEAVE_ON_SCALAR = 128
 X_CAST_ON_SCALAR = 20
 G_WEIGH_ON_GPSIMD = 96
-V_SCATTER_ON_VECTOR = 384
+
+HALF = N // 2
+LONG = 384
 
 TINY = 2.0 ** -80
 RATE = LR * BETA
@@ -74,17 +76,13 @@ def tile_attend_glch_adam_kernel(tc, xT, wT, y, wt, xm, mT, vT, offs, out_0, out
         xm_rows = xm[0].rearrange("(p t) d -> p t d", t=PACK)
         xm_raw = [sb("xm_raw%d" % h, [P, PACK, D // 2], F32) for h in range(2)]
         m_new, v_new, step = [four(name, T) for name in ("m_new", "v_new", "step")]
-        m_pairs = [sb("m_pair%d" % h, [P, 2 * T], F32) for h in range(2)]
+        m_pair = sb("m_pair", [P, 2 * T], F32)
+        m_old = [sb("m_old0", [P, T], F32), sb("m_old1", [P, T], F32), m_pair[:, :T], m_pair[:, T:]]
         v_pairs = [sb("v_pair%d" % h, [P, 2 * T], F32) for h in range(2)]
-        m_old = [m_pairs[0][:, T:], m_pairs[0][:, :T], m_pairs[1][:, :T], m_pairs[1][:, T:]]
-        v_old = [v_pairs[0][:, T:], v_pairs[0][:, :T], v_pairs[1][:, :T], v_pairs[1][:, T:]]
+        v_old = [v_pairs[0][:, T:], v_pairs[0][:, :T], v_pairs[1][:, T:], v_pairs[1][:, :T]]
 
         def load_band(tiles, table, k):
             nc.sync.dma_start(tiles[k][:, :], table[k * P:(k + 1) * P, :])
-
-        def load_bands_2_and_3(tile, table):
-            nc.sync.dma_start(
-                tile[:].rearrange("p (b t) -> p b t", b=2), table[2 * P:, :].rearrange("(b p) t -> p b t", b=2))
 
         def load_xm(h):
             nc.sync.dma_start(xm_raw[h][:], xm_rows[:, :, h * (D // 2):(h + 1) * (D // 2)])
@@ -92,28 +90,27 @@ def tile_attend_glch_adam_kernel(tc, xT, wT, y, wt, xm, mT, vT, offs, out_0, out
         load_xm(0)
         for h in range(2):
             nc.sync.dma_start(y_sb[h][:], y_rows[:, :, h * (N // 2):(h + 1) * (N // 2)])
-        load_xm(1)
-        load_band(m_old, mT, 0)
         load_band(v_old, vT, 0)
         load_band(v_old, vT, 1)
-        load_bands_2_and_3(v_pairs[1], vT)
+        load_xm(1)
+        load_band(v_old, vT, 2)
+        load_band(m_old, mT, 0)
+        load_band(v_old, vT, 3)
         load_band(m_new, mT, 0)
-        load_bands_2_and_3(m_pairs[1], mT)
-        load_band(v_new, vT, 3)
-        load_band(m_old, mT, 1)
-        load_band(m_new, mT, 3)
-        for k in (0, 1, 2):
-            load_band(v_new, vT, k)
-        nc.sync.dma_start(m_new[2][:, :T // 2], mT[2 * P:3 * P, :T // 2])
+        load_band(v_new, vT, 0)
         load_band(m_new, mT, 1)
-        nc.sync.dma_start(m_new[2][:, T // 2:], mT[2 * P:3 * P, T // 2:])
+        load_band(m_old, mT, 1)
+        for k in (1, 2, 3):
+            load_band(v_new, vT, k)
+        for k in (2, 3):
+            load_band(m_new, mT, k)
+        nc.sync.dma_start(
+            m_pair[:].rearrange("p (b t) -> p b t", b=2), mT[2 * P:, :].rearrange("(b p) t -> p b t", b=2))
 
         one = sb("one", [P, 1], F32)
         nc.vector.memset(one[:], 1.0)
         tiny_col = sb("tiny_col", [P, 1], F32)
         nc.scalar.activation(tiny_col[:], one[:], ACT.Copy, scale=TINY)
-        eps_col = sb("eps_col", [P, 1], F32)
-        nc.scalar.activation(eps_col[:], one[:], ACT.Copy, scale=(EPS / RATE) ** 2)
         ident = sb("ident", [P, P], F32)
         make_identity(nc, ident[:])
         for k in range(BANDS):
@@ -193,11 +190,15 @@ def tile_attend_glch_adam_kernel(tc, xT, wT, y, wt, xm, mT, vT, offs, out_0, out
         nc.vector.tensor_tensor(
             g_bf[:, lo + width:lo + CHUNK, :], th[:, width:, :], wt_words.to_broadcast([P, CHUNK - width, PACK]),
             ALU.mult)
+        ths = [sb("th%d" % c, [P, PACK, CHUNK], F32) for c in (2, 3)]
         for c in (2, 3):
-            nc.scalar.activation(diffs[c][:], diffs[c][:], ACT.Tanh)
+            nc.scalar.activation(ths[c - 2][:], diffs[c][:], ACT.Tanh)
             nc.vector.tensor_tensor(
-                woven(g_bf[:, c * CHUNK:(c + 1) * CHUNK, :]), by_places(diffs[c][:]),
+                woven(g_bf[:, c * CHUNK:(c + 1) * CHUNK, :]), by_places(ths[c - 2][:]),
                 wt_bank[:, :, 0:1].unsqueeze(1).to_broadcast([P, CHUNK // RUN, PACK, RUN]), ALU.mult)
+
+        eps_col = sb("eps_col", [P, 1], F32, tag="diff3")
+        nc.scalar.activation(eps_col[:], one[:], ACT.Abs_reciprocal_sqrt, scale=(RATE / EPS) ** 4)
 
         xm_codes = [sb("xm_codes%d" % h, [P, 2 * P], U32) for h in range(2)]
         xm_scales = [sb("xm_scales%d" % h, [P, 2 * P], U8) for h in range(2)]
@@ -210,15 +211,23 @@ def tile_attend_glch_adam_kernel(tc, xT, wT, y, wt, xm, mT, vT, offs, out_0, out
         nc.vector.tensor_copy(woven(xm_early[:, P:, :]), by_places(xm_raw[0][:, :, P:]))
         quantise_xm(0, xm_early)
         quantise(g_codes[:], g_scales[:], E5M2, g_bf[:].rearrange("p i t -> p (i t)"))
-        xm_late = sb("xm_bf1", [P, 2 * P, PACK], BF16, tag="diff3")
+        xm_late = sb("xm_bf1", [P, 2 * P, PACK], BF16)
         nc.vector.tensor_copy(woven(xm_late[:]), by_places(xm_raw[1][:]))
         quantise_xm(1, xm_late)
 
-        m_picked, nm = four("m_picked", N), four("nm", N)
-        v_picked_pairs = [sb("v_picked%d" % h, [P, 2 * N], F32) for h in range(2)]
-        nv_pairs = [sb("nv%d" % h, [P, 2 * N], F32) for h in range(2)]
-        v_picked = [v_picked_pairs[k // 2][:, (k % 2) * N:(k % 2 + 1) * N] for k in range(BANDS)]
-        nv = [nv_pairs[k // 2][:, (k % 2) * N:(k % 2 + 1) * N] for k in range(BANDS)]
+        def halves(pairs):
+            return [pairs[k // 2][:, (k % 2) * N:(k % 2 + 1) * N] for k in range(BANDS)]
+
+        def pair(name):
+            return sb(name, [P, 2 * N], F32)
+
+        nm = four("nm", N)
+        nv_pairs = [pair("nv0"), pair("nv1")]
+        divisor_pairs = [pair("divisor0"), pair("divisor1")]
+        inverse_pairs = [pair("inverse0"), divisor_pairs[0]]
+        nv, divisor, inverse = halves(nv_pairs), halves(divisor_pairs), halves(inverse_pairs)
+        v_picked = [sb("v_picked0", [P, N], F32, tag="diff2")] + [sb("v_picked%d" % k, [P, N], F32) for k in (1, 2, 3)]
+        m_picked = [sb("m_picked0", [P, N], F32), inverse[0], sb("m_picked2", [P, N], F32), sb("m_picked3", [P, N], F32)]
         dw = []
         for k in range(BANDS):
             rows = slice((k % 2) * P, (k % 2 + 1) * P)
@@ -228,86 +237,85 @@ def tile_attend_glch_adam_kernel(tc, xT, wT, y, wt, xm, mT, vT, offs, out_0, out
                 rhs=g_codes[:].bitcast(E5M2), rhs_scale=g_scales[:], start=True, stop=True)
             dw.append(bank)
 
-        nv_unit = [1.0, 1.0, 1.0, RHO]
-        root = v_picked[2:] + v_picked[:2]
-        step_picked = [root[0], root[1], root[2], nm[1]]
-
-        def scatter_on_scalar(window, values, scale):
-            for lo in (0, N // 2):
-                nc.scalar.activation(
-                    window[:].indirect(slots(lo, lo + N // 2)), values[:, lo:lo + N // 2], ACT.Copy, scale=scale)
+        def scatter_on_scalar(window, values, scale, lo, hi):
+            nc.scalar.activation(window[:].indirect(slots(lo, hi)), values[:, lo:hi], ACT.Copy, scale=scale)
 
         def scatter_on_vector(window, values):
             nc.vector.tensor_copy(window[:].indirect(offsets[:]), values[:])
 
-        def store(queue, out, windows, k):
-            queue.dma_start(out[k * P:(k + 1) * P, :], windows[k][:])
+        def square(k):
+            nc.scalar.activation(nv[k][:], dw[k][:], ACT.Square, scale=math.sqrt(1.0 - RHO))
 
         def new_v(k):
-            nc.scalar.activation(nv[k][:], dw[k][:], ACT.Square, scale=math.sqrt((1.0 - RHO) / nv_unit[k]))
             nc.gpsimd.tensor_tensor(nv[k][:], nv[k][:], v_picked[k][:], ALU.add)
 
         def new_m(k):
-            nc.vector.scalar_tensor_tensor(nm[k][:], dw[k][:], 1.0 - BETA, m_picked[k][:], ALU.mult, ALU.add)
-
-        def new_m_over_minus_beta(k):
             nc.vector.scalar_tensor_tensor(
                 nm[k][:], dw[k][:], -(1.0 - BETA) / BETA, m_picked[k][:], ALU.mult, ALU.subtract)
 
-        def second_root(k):
+        def first_roots(h, roots):
+            nc.scalar.activation(roots[:], nv_pairs[h][:], ACT.Abs_reciprocal_sqrt, bias=tiny_col[:])
+
+        def new_divisors(h, roots):
+            for k in (2 * h, 2 * h + 1):
+                root = roots[:, (k % 2) * N:(k % 2 + 1) * N]
+                nc.gpsimd.tensor_scalar(root, root, 2.0 * EPS, 1.0, ALU.mult, ALU.add)
+            for k in (2 * h, 2 * h + 1):
+                nc.gpsimd.tensor_tensor(divisor[k][:], roots[:, (k % 2) * N:(k % 2 + 1) * N], nv[k][:], ALU.mult)
+
+        def second_roots(h):
             nc.scalar.activation(
-                root[k][:], root[k][:], ACT.Abs_reciprocal_sqrt, bias=eps_col[:], scale=nv_unit[k] / RATE ** 2)
+                inverse_pairs[h][:], divisor_pairs[h][:], ACT.Abs_reciprocal_sqrt, bias=eps_col[:], scale=1.0 / RATE ** 2)
 
         def new_step(k):
-            nc.gpsimd.tensor_tensor(step_picked[k][:], root[k][:], nm[k][:], ALU.mult)
+            nc.gpsimd.tensor_tensor(inverse[k][:], inverse[k][:], nm[k][:], ALU.mult)
 
-        gather_on_scalar(m_picked[0], m_old[0])
         gather_on_scalar(v_picked[0], v_old[0], scale=RHO)
-        new_v(0)
         gather_scaled_on_vector(v_picked[1], v_pairs[0], RHO)
+        square(0)
+        square(1)
+        gather_on_scalar(v_picked[2], v_old[2], scale=RHO)
+        square(2)
+        square(3)
+        new_v(0)
         new_v(1)
-        new_m_over_minus_beta(0)
-        gather_on_vector(v_picked[3], v_old[3])
-        new_v(3)
-        gather_scaled_on_vector(v_picked[2], v_pairs[1], RHO)
         new_v(2)
-        gather_on_vector(m_picked[3], m_old[3])
-        gather_scaled_on_vector(m_picked[2], m_pairs[1], BETA)
-        new_m_over_minus_beta(3)
-        gather_scaled_on_vector(m_picked[1], m_pairs[0], BETA)
-        new_m(2)
+        gather_on_vector(m_picked[0], m_old[0])
+        new_m(0)
+        gather_scaled_on_vector(v_picked[3], v_pairs[1], RHO)
+        new_v(3)
+        roots = [sb("root0", [P, 2 * N], F32, tag="v_pair1"), pair("root1")]
+        first_roots(0, roots[0])
+        scatter_on_scalar(m_new[0], nm[0], -BETA, 0, HALF)
+        first_roots(1, roots[1])
+        scatter_on_scalar(m_new[0], nm[0], -BETA, HALF, N)
+        scatter_on_vector(v_new[0], nv[0])
+        new_divisors(0, roots[0])
+        new_divisors(1, roots[1])
+        gather_on_vector(m_picked[1], m_old[1])
         new_m(1)
-        scatter_on_scalar(m_new[0], nm[0], -BETA)
-        store(nc.scalar, out_1, m_new, 0)
-        for h in range(2):
-            nc.scalar.activation(
-                v_picked_pairs[1 - h][:], nv_pairs[h][:], ACT.Abs_reciprocal_sqrt, bias=tiny_col[:])
-            for k in (2 * h, 2 * h + 1):
-                nc.gpsimd.tensor_scalar(
-                    root[k][:], root[k][:], 2.0 * EPS / math.sqrt(nv_unit[k]), 1.0, ALU.mult, ALU.add)
-                nc.gpsimd.tensor_tensor(root[k][:], root[k][:], nv[k][:], ALU.mult)
-        scatter_on_scalar(v_new[3], nv[3], RHO)
-        store(nc.scalar, out_2, v_new, 3)
-        second_root(0)
-        second_root(1)
-        scatter_on_scalar(m_new[3], nm[3], -BETA)
-        store(nc.scalar, out_1, m_new, 3)
-        second_root(2)
-        second_root(3)
-        nc.vector.tensor_copy(v_new[0][:].indirect(slots(0, V_SCATTER_ON_VECTOR)), nv[0][:, :V_SCATTER_ON_VECTOR])
-        nc.scalar.activation(
-            v_new[0][:].indirect(slots(V_SCATTER_ON_VECTOR, N)), nv[0][:, V_SCATTER_ON_VECTOR:], ACT.Copy)
-        store(nc.scalar, out_2, v_new, 0)
-        for k in (1, 2):
+        scatter_on_scalar(m_new[1], nm[1], -BETA, 0, HALF)
+        second_roots(0)
+        scatter_on_scalar(m_new[1], nm[1], -BETA, HALF, N)
+        second_roots(1)
+        for k in (1, 2, 3):
             scatter_on_vector(v_new[k], nv[k])
-            store(nc.sync, out_2, v_new, k)
-        for k in (1, 2):
-            scatter_on_vector(m_new[k], nm[k])
-            store(nc.sync, out_1, m_new, k)
-        for k, scale in ((0, 1.0), (1, -1.0 / BETA), (2, -1.0 / BETA)):
-            new_step(k)
-            scatter_on_scalar(step[k], step_picked[k], scale)
-            store(nc.scalar, out_0, step, k)
-        new_step(3)
-        scatter_on_vector(step[3], step_picked[3])
-        store(nc.sync, out_0, step, 3)
+        new_step(0)
+        new_step(1)
+        for lo in (0, HALF):
+            for k in (0, 1):
+                scatter_on_scalar(step[k], inverse[k], 1.0, lo, lo + HALF)
+        for k in (2, 3):
+            gather_on_vector(m_picked[k], m_old[k])
+        for k in (2, 3):
+            new_m(k)
+        for k, lo, hi in ((2, 0, LONG), (3, 0, N - LONG), (2, LONG, N), (3, N - LONG, N)):
+            scatter_on_scalar(m_new[k], nm[k], -BETA, lo, hi)
+        for k in (2, 3):
+            nc.vector.tensor_tensor(step[k][:].indirect(offsets[:]), inverse[k][:], nm[k][:], ALU.mult)
+
+        for out, windows, k in (
+                (out_2, v_new, 0), (out_1, m_new, 0), (out_2, v_new, 1), (out_1, m_new, 1), (out_2, v_new, 2),
+                (out_0, step, 0), (out_2, v_new, 3), (out_0, step, 1), (out_0, step, 2), (out_1, m_new, 2),
+                (out_0, step, 3), (out_1, m_new, 3)):
+            nc.sync.dma_start(out[k * P:(k + 1) * P, :], windows[k][:])

@@ -91,21 +91,21 @@ def tile_attend_glch_adam_kernel(tc, xT, wT, y, wt, xm, mT, vT, offs, out_0, out
         for h in range(2):
             nc.sync.dma_start(y_sb[h][:], y_rows[:, :, h * (N // 2):(h + 1) * (N // 2)])
         load_band(v_old, vT, 0)
-        load_band(v_old, vT, 1)
         load_xm(1)
-        load_band(v_old, vT, 2)
+        for k in (1, 2, 3):
+            load_band(v_old, vT, k)
         load_band(m_old, mT, 0)
-        load_band(v_old, vT, 3)
         load_band(m_new, mT, 0)
         load_band(v_new, vT, 0)
         load_band(m_new, mT, 1)
         load_band(m_old, mT, 1)
-        for k in (1, 2, 3):
+        for k in (1, 2):
             load_band(v_new, vT, k)
         for k in (2, 3):
             load_band(m_new, mT, k)
         nc.sync.dma_start(
             m_pair[:].rearrange("p (b t) -> p b t", b=2), mT[2 * P:, :].rearrange("(b p) t -> p b t", b=2))
+        load_band(v_new, vT, 3)
 
         one = sb("one", [P, 1], F32)
         nc.vector.memset(one[:], 1.0)
@@ -211,7 +211,7 @@ def tile_attend_glch_adam_kernel(tc, xT, wT, y, wt, xm, mT, vT, offs, out_0, out
         nc.vector.tensor_copy(woven(xm_early[:, P:, :]), by_places(xm_raw[0][:, :, P:]))
         quantise_xm(0, xm_early)
         quantise(g_codes[:], g_scales[:], E5M2, g_bf[:].rearrange("p i t -> p (i t)"))
-        xm_late = sb("xm_bf1", [P, 2 * P, PACK], BF16)
+        xm_late = sb("xm_bf1", [P, 2 * P, PACK], BF16, tag="th3")
         nc.vector.tensor_copy(woven(xm_late[:]), by_places(xm_raw[1][:]))
         quantise_xm(1, xm_late)
 
@@ -225,7 +225,7 @@ def tile_attend_glch_adam_kernel(tc, xT, wT, y, wt, xm, mT, vT, offs, out_0, out
         nv_pairs = [pair("nv0"), pair("nv1")]
         divisor_pairs = [pair("divisor0"), pair("divisor1")]
         inverse_pairs = [pair("inverse0"), divisor_pairs[0]]
-        nv, divisor, inverse = halves(nv_pairs), halves(divisor_pairs), halves(inverse_pairs)
+        nv, inverse = halves(nv_pairs), halves(inverse_pairs)
         v_picked = [sb("v_picked0", [P, N], F32, tag="diff2")] + [sb("v_picked%d" % k, [P, N], F32) for k in (1, 2, 3)]
         m_picked = [sb("m_picked0", [P, N], F32), inverse[0], sb("m_picked2", [P, N], F32), sb("m_picked3", [P, N], F32)]
         dw = []
@@ -257,11 +257,8 @@ def tile_attend_glch_adam_kernel(tc, xT, wT, y, wt, xm, mT, vT, offs, out_0, out
             nc.scalar.activation(roots[:], nv_pairs[h][:], ACT.Abs_reciprocal_sqrt, bias=tiny_col[:])
 
         def new_divisors(h, roots):
-            for k in (2 * h, 2 * h + 1):
-                root = roots[:, (k % 2) * N:(k % 2 + 1) * N]
-                nc.gpsimd.tensor_scalar(root, root, 2.0 * EPS, 1.0, ALU.mult, ALU.add)
-            for k in (2 * h, 2 * h + 1):
-                nc.gpsimd.tensor_tensor(divisor[k][:], roots[:, (k % 2) * N:(k % 2 + 1) * N], nv[k][:], ALU.mult)
+            nc.gpsimd.tensor_scalar(roots[:], roots[:], 2.0 * EPS, 1.0, ALU.mult, ALU.add)
+            nc.gpsimd.tensor_tensor(divisor_pairs[h][:], roots[:], nv_pairs[h][:], ALU.mult)
 
         def second_roots(h):
             nc.scalar.activation(
@@ -274,17 +271,17 @@ def tile_attend_glch_adam_kernel(tc, xT, wT, y, wt, xm, mT, vT, offs, out_0, out
         gather_scaled_on_vector(v_picked[1], v_pairs[0], RHO)
         square(0)
         square(1)
-        gather_on_scalar(v_picked[2], v_old[2], scale=RHO)
         square(2)
         square(3)
+        gather_on_scalar(v_picked[2], v_old[2], scale=RHO)
         new_v(0)
         new_v(1)
+        gather_scaled_on_vector(v_picked[3], v_pairs[1], RHO)
+        new_v(3)
         new_v(2)
         gather_on_vector(m_picked[0], m_old[0])
         new_m(0)
-        gather_scaled_on_vector(v_picked[3], v_pairs[1], RHO)
-        new_v(3)
-        roots = [sb("root0", [P, 2 * N], F32, tag="v_pair1"), pair("root1")]
+        roots = [sb("root0", [P, 2 * N], F32, tag="v_pair1"), sb("root1", [P, 2 * N], F32, tag="m_picked0")]
         first_roots(0, roots[0])
         scatter_on_scalar(m_new[0], nm[0], -BETA, 0, HALF)
         first_roots(1, roots[1])
@@ -298,7 +295,7 @@ def tile_attend_glch_adam_kernel(tc, xT, wT, y, wt, xm, mT, vT, offs, out_0, out
         second_roots(0)
         scatter_on_scalar(m_new[1], nm[1], -BETA, HALF, N)
         second_roots(1)
-        for k in (1, 2, 3):
+        for k in (1, 2):
             scatter_on_vector(v_new[k], nv[k])
         new_step(0)
         new_step(1)
@@ -309,6 +306,7 @@ def tile_attend_glch_adam_kernel(tc, xT, wT, y, wt, xm, mT, vT, offs, out_0, out
             gather_on_vector(m_picked[k], m_old[k])
         for k in (2, 3):
             new_m(k)
+        scatter_on_vector(v_new[3], nv[3])
         for k, lo, hi in ((2, 0, LONG), (3, 0, N - LONG), (2, LONG, N), (3, N - LONG, N)):
             scatter_on_scalar(m_new[k], nm[k], -BETA, lo, hi)
         for k in (2, 3):
@@ -316,6 +314,6 @@ def tile_attend_glch_adam_kernel(tc, xT, wT, y, wt, xm, mT, vT, offs, out_0, out
 
         for out, windows, k in (
                 (out_2, v_new, 0), (out_1, m_new, 0), (out_2, v_new, 1), (out_1, m_new, 1), (out_2, v_new, 2),
-                (out_0, step, 0), (out_2, v_new, 3), (out_0, step, 1), (out_0, step, 2), (out_1, m_new, 2),
-                (out_0, step, 3), (out_1, m_new, 3)):
+                (out_0, step, 0), (out_0, step, 1), (out_2, v_new, 3), (out_0, step, 2), (out_1, m_new, 2),
+                (out_1, m_new, 3), (out_0, step, 3)):
             nc.sync.dma_start(out[k * P:(k + 1) * P, :], windows[k][:])

@@ -97,11 +97,11 @@ def tile_attend_glch_adam_kernel(tc, xT, wT, y, wt, xm, mT, vT, offs, out_0, out
         load_band(m_old, mT, 0)
         load_band(m_new, mT, 0)
         load_band(v_new, vT, 0)
-        load_band(m_new, mT, 1)
+        load_band(m_new, mT, 2)
         load_band(m_old, mT, 1)
-        for k in (1, 2):
+        for k in (2, 1):
             load_band(v_new, vT, k)
-        for k in (2, 3):
+        for k in (1, 3):
             load_band(m_new, mT, k)
         nc.sync.dma_start(
             m_pair[:].rearrange("p (b t) -> p b t", b=2), mT[2 * P:, :].rearrange("(b p) t -> p b t", b=2))
@@ -197,8 +197,9 @@ def tile_attend_glch_adam_kernel(tc, xT, wT, y, wt, xm, mT, vT, offs, out_0, out
                 woven(g_bf[:, c * CHUNK:(c + 1) * CHUNK, :]), by_places(ths[c - 2][:]),
                 wt_bank[:, :, 0:1].unsqueeze(1).to_broadcast([P, CHUNK // RUN, PACK, RUN]), ALU.mult)
 
-        eps_col = sb("eps_col", [P, 1], F32, tag="diff3")
-        nc.scalar.activation(eps_col[:], one[:], ACT.Abs_reciprocal_sqrt, scale=(RATE / EPS) ** 4)
+        eps_cols = diffs[3][:, 0, :]
+        nc.scalar.activation(eps_cols[:, 0:1], one[:], ACT.Abs_reciprocal_sqrt, scale=(RATE / EPS) ** 4)
+        nc.scalar.activation(eps_cols[:, 1:2], one[:], ACT.Abs_reciprocal_sqrt, scale=(RATE / EPS) ** 2)
 
         xm_codes = [sb("xm_codes%d" % h, [P, 2 * P], U32) for h in range(2)]
         xm_scales = [sb("xm_scales%d" % h, [P, 2 * P], U8) for h in range(2)]
@@ -257,63 +258,73 @@ def tile_attend_glch_adam_kernel(tc, xT, wT, y, wt, xm, mT, vT, offs, out_0, out
             nc.scalar.activation(roots[:], nv_pairs[h][:], ACT.Abs_reciprocal_sqrt, bias=tiny_col[:])
 
         def new_divisors(h, roots):
-            nc.gpsimd.tensor_scalar(roots[:], roots[:], 2.0 * EPS, 1.0, ALU.mult, ALU.add)
+            if h == 0:
+                nc.gpsimd.tensor_scalar(roots[:], roots[:], 2.0 * EPS, 1.0, ALU.mult, ALU.add)
             nc.gpsimd.tensor_tensor(divisor_pairs[h][:], roots[:], nv_pairs[h][:], ALU.mult)
 
         def second_roots(h):
-            nc.scalar.activation(
-                inverse_pairs[h][:], divisor_pairs[h][:], ACT.Abs_reciprocal_sqrt, bias=eps_col[:], scale=1.0 / RATE ** 2)
+            if h == 0:
+                nc.scalar.activation(
+                    inverse_pairs[0][:], divisor_pairs[0][:], ACT.Abs_reciprocal_sqrt, bias=eps_cols[:, 0:1],
+                    scale=1.0 / RATE ** 2)
+                return
+            for k, unit in ((2, 1.0 - RHO), (3, 1.0)):
+                nc.scalar.activation(
+                    inverse[k][:], divisor_pairs[1][:, (k - 2) * N:(k - 1) * N], ACT.Abs_reciprocal_sqrt,
+                    bias=eps_cols[:, 1:2], scale=math.sqrt(unit) / RATE)
 
-        def new_step(k):
-            nc.gpsimd.tensor_tensor(inverse[k][:], inverse[k][:], nm[k][:], ALU.mult)
+        def times_m(out, k):
+            nc.gpsimd.tensor_tensor(out[:], inverse[k][:], nm[k][:], ALU.mult)
 
         gather_on_scalar(v_picked[0], v_old[0], scale=RHO)
         gather_scaled_on_vector(v_picked[1], v_pairs[0], RHO)
         square(0)
         square(1)
-        square(2)
+        gather_on_scalar(v_picked[2], v_old[2], scale=RHO / (1.0 - RHO))
+        nc.scalar.activation(nm[2][:], dw[2][:], ACT.Copy, scale=-1.0)
         square(3)
-        gather_on_scalar(v_picked[2], v_old[2], scale=RHO)
         new_v(0)
         new_v(1)
+        nc.gpsimd.tensor_tensor(nv[2][:], nm[2][:], nm[2][:], ALU.mult)
+        new_v(2)
         gather_scaled_on_vector(v_picked[3], v_pairs[1], RHO)
         new_v(3)
-        new_v(2)
         gather_on_vector(m_picked[0], m_old[0])
         new_m(0)
         roots = [sb("root0", [P, 2 * N], F32, tag="v_pair1"), sb("root1", [P, 2 * N], F32, tag="m_picked0")]
         first_roots(0, roots[0])
-        scatter_on_scalar(m_new[0], nm[0], -BETA, 0, HALF)
+        scatter_on_scalar(m_new[0], nm[0], -BETA, 0, LONG)
         first_roots(1, roots[1])
-        scatter_on_scalar(m_new[0], nm[0], -BETA, HALF, N)
+        scatter_on_scalar(m_new[0], nm[0], -BETA, LONG, N)
         scatter_on_vector(v_new[0], nv[0])
         new_divisors(0, roots[0])
         new_divisors(1, roots[1])
         gather_on_vector(m_picked[1], m_old[1])
         new_m(1)
-        scatter_on_scalar(m_new[1], nm[1], -BETA, 0, HALF)
+        scatter_on_scalar(v_new[2], nv[2], 1.0 - RHO, 0, HALF)
         second_roots(0)
-        scatter_on_scalar(m_new[1], nm[1], -BETA, HALF, N)
+        scatter_on_scalar(v_new[2], nv[2], 1.0 - RHO, HALF, N)
         second_roots(1)
-        for k in (1, 2):
-            scatter_on_vector(v_new[k], nv[k])
-        new_step(0)
-        new_step(1)
+        scatter_on_vector(v_new[1], nv[1])
+        times_m(inverse[0], 0)
         for lo in (0, HALF):
-            for k in (0, 1):
-                scatter_on_scalar(step[k], inverse[k], 1.0, lo, lo + HALF)
-        for k in (2, 3):
+            scatter_on_scalar(m_new[1], nm[1], -BETA, lo, lo + HALF)
+            scatter_on_scalar(step[0], inverse[0], 1.0, lo, lo + HALF)
+        for k in (3, 2):
             gather_on_vector(m_picked[k], m_old[k])
-        for k in (2, 3):
-            new_m(k)
+        nc.gpsimd.tensor_tensor(nm[2][:], nm[2][:], m_picked[2][:], ALU.subtract)
+        new_m(3)
         scatter_on_vector(v_new[3], nv[3])
-        for k, lo, hi in ((2, 0, LONG), (3, 0, N - LONG), (2, LONG, N), (3, N - LONG, N)):
+        times_m(m_picked[3], 1)
+        scatter_on_vector(step[1], m_picked[3])
+        for k, lo, hi in ((3, 0, LONG), (2, 0, N - LONG), (3, LONG, N), (2, N - LONG, N)):
             scatter_on_scalar(m_new[k], nm[k], -BETA, lo, hi)
-        for k in (2, 3):
-            nc.vector.tensor_tensor(step[k][:].indirect(offsets[:]), inverse[k][:], nm[k][:], ALU.mult)
+        for k, product in ((3, m_picked[2]), (2, inverse[1])):
+            times_m(product, k)
+            nc.vector.tensor_tensor(step[k][:].indirect(offsets[:]), inverse[k][:], product[:], ALU.mult)
 
         for out, windows, k in (
-                (out_2, v_new, 0), (out_1, m_new, 0), (out_2, v_new, 1), (out_1, m_new, 1), (out_2, v_new, 2),
-                (out_0, step, 0), (out_0, step, 1), (out_2, v_new, 3), (out_0, step, 2), (out_1, m_new, 2),
-                (out_1, m_new, 3), (out_0, step, 3)):
+                (out_2, v_new, 0), (out_1, m_new, 0), (out_2, v_new, 1), (out_2, v_new, 2), (out_2, v_new, 3),
+                (out_1, m_new, 1), (out_0, step, 0), (out_0, step, 1), (out_1, m_new, 3), (out_0, step, 3),
+                (out_1, m_new, 2), (out_0, step, 2)):
             nc.sync.dma_start(out[k * P:(k + 1) * P, :], windows[k][:])

@@ -228,7 +228,8 @@ def tile_attend_glch_adam_kernel(tc, xT, wT, y, wt, xm, mT, vT, offs, out_0, out
         inverse_pairs = [pair("inverse0"), divisor_pairs[0]]
         nv, inverse = halves(nv_pairs), halves(inverse_pairs)
         v_picked = [sb("v_picked0", [P, N], F32, tag="diff2")] + [sb("v_picked%d" % k, [P, N], F32) for k in (1, 2, 3)]
-        m_picked = [sb("m_picked0", [P, N], F32), inverse[0], sb("m_picked2", [P, N], F32), sb("m_picked3", [P, N], F32)]
+        late_roots = pair("root1")
+        m_picked = [late_roots[:, HALF:HALF + N], inverse[0], sb("m_picked2", [P, N], F32), sb("m_picked3", [P, N], F32)]
         dw = []
         for k in range(BANDS):
             rows = slice((k % 2) * P, (k % 2 + 1) * P)
@@ -254,8 +255,8 @@ def tile_attend_glch_adam_kernel(tc, xT, wT, y, wt, xm, mT, vT, offs, out_0, out
             nc.vector.scalar_tensor_tensor(
                 nm[k][:], dw[k][:], -(1.0 - BETA) / BETA, m_picked[k][:], ALU.mult, ALU.subtract)
 
-        def first_roots(h, roots):
-            nc.scalar.activation(roots[:], nv_pairs[h][:], ACT.Abs_reciprocal_sqrt, bias=tiny_col[:])
+        def first_roots(out, squares):
+            nc.scalar.activation(out[:], squares[:], ACT.Abs_reciprocal_sqrt, bias=tiny_col[:])
 
         def new_divisors(h, roots):
             if h == 0:
@@ -291,19 +292,20 @@ def tile_attend_glch_adam_kernel(tc, xT, wT, y, wt, xm, mT, vT, offs, out_0, out
         new_v(3)
         gather_on_vector(m_picked[0], m_old[0])
         new_m(0)
-        roots = [sb("root0", [P, 2 * N], F32, tag="v_pair1"), sb("root1", [P, 2 * N], F32, tag="m_picked0")]
-        first_roots(0, roots[0])
+        roots = [sb("root0", [P, 2 * N], F32, tag="v_pair1"), late_roots]
+        first_roots(roots[0], nv_pairs[0])
         scatter_on_scalar(m_new[0], nm[0], -BETA, 0, LONG)
-        first_roots(1, roots[1])
+        for h in range(2):
+            first_roots(late_roots[:, h * N:(h + 1) * N], nv[2 + h])
         scatter_on_scalar(m_new[0], nm[0], -BETA, LONG, N)
         scatter_on_vector(v_new[0], nv[0])
         new_divisors(0, roots[0])
         new_divisors(1, roots[1])
         gather_on_vector(m_picked[1], m_old[1])
         new_m(1)
-        scatter_on_scalar(v_new[2], nv[2], 1.0 - RHO, 0, HALF)
+        scatter_on_scalar(v_new[2], nv[2], 1.0 - RHO, 0, LONG)
         second_roots(0)
-        scatter_on_scalar(v_new[2], nv[2], 1.0 - RHO, HALF, N)
+        scatter_on_scalar(v_new[2], nv[2], 1.0 - RHO, LONG, N)
         second_roots(1)
         scatter_on_vector(v_new[1], nv[1])
         times_m(inverse[0], 0)

import math
from contextlib import ExitStack

import concourse.mybir as mybir
from concourse.masks import make_identity

N, T, D, R = 512, 1024, 512, 512
LR, BETA, RHO, EPS = 0.1, 0.5, 0.9, 0.001
FLOPS = 2 * 2 * R * D * N

F32 = mybir.dt.float32
BF16 = mybir.dt.bfloat16
U32 = mybir.dt.uint32
U16 = mybir.dt.uint16
U8 = mybir.dt.uint8
E4M3 = mybir.dt.float8_e4m3fn_x4
E5M2 = mybir.dt.float8_e5m2_x4
ACT = mybir.ActivationFunctionType
ALU = mybir.AluOpType

P = 128
PACK = 4
BANDS = D // P
CHUNK = 128
CHUNKS = N // CHUNK
RUN = 4
LIST_ROWS = 16

W_GATHER_ON_SCALAR = 192
W_WEAVE_ON_SCALAR = 128
X_CAST_ON_SCALAR = 20
G_WEIGH_ON_GPSIMD = 96

HALF = N // 2
LONG = 384

TINY = 2.0 ** -80
RATE = LR * BETA


def tile_attend_glch_adam_kernel(tc, xT, wT, y, wt, xm, mT, vT, offs, out_0, out_1, out_2):
    nc = tc.nc
    with ExitStack() as ctx:
        keep = ctx.enter_context(tc.tile_pool(name="keep", bufs=1))
        psum = ctx.enter_context(tc.psum_pool(name="psum", bufs=1))

        def sb(name, shape, dtype, tag=None):
            return keep.tile(shape, dtype, name=name, tag=tag or name, align_bytes=64)

        def four(name, width):
            return [sb("%s%d" % (name, k), [P, width], F32) for k in range(BANDS)]

        def woven(tile):
            return tile.rearrange("p (c i) t -> p c t i", i=RUN)

        def by_places(tile):
            return tile.rearrange("p t (c i) -> p c t i", i=RUN)

        w_rows = wT.rearrange("(p j) t -> j p t", j=PACK)
        w_raw = four("w_raw", T)
        nc.sync.dma_start(w_raw[0][:], w_rows[0])
        offsets = keep.tile([P, N // LIST_ROWS], U16, name="offsets")
        nc.sync.dma_start(offsets[:], offs)
        nc.sync.dma_start(w_raw[1][:], w_rows[1])
        wt_row = sb("wt_row", [P, R], F32)
        nc.gpsimd.memset(wt_row[:], 0.0)
        nc.sync.dma_start(wt_row[0:1, :], wt[0].rearrange("r o -> o r"))
        for j in range(2, PACK):
            nc.sync.dma_start(w_raw[j][:], w_rows[j])
        x_rows = xT[0].rearrange("(p j) r -> p j r", j=PACK)
        x_raw = [sb("x_raw%d" % h, [P, PACK, R // 2], F32) for h in range(2)]
        for h in range(2):
            nc.sync.dma_start(x_raw[h][:], x_rows[:, :, h * (R // 2):(h + 1) * (R // 2)])
        y_rows = y[0].rearrange("(p t) i -> p t i", t=PACK)
        y_sb = [sb("y_sb%d" % h, [P, PACK, N // 2], F32) for h in range(2)]
        xm_rows = xm[0].rearrange("(p t) d -> p t d", t=PACK)
        xm_raw = [sb("xm_raw%d" % h, [P, PACK, D // 2], F32) for h in range(2)]
        m_new, v_new, step = [four(name, T) for name in ("m_new", "v_new", "step")]
        m_pair = sb("m_pair", [P, 2 * T], F32)
        m_old = [sb("m_old0", [P, T], F32), sb("m_old1", [P, T], F32), m_pair[:, :T], m_pair[:, T:]]
        v_pairs = [sb("v_pair%d" % h, [P, 2 * T], F32) for h in range(2)]
        v_old = [v_pairs[0][:, T:], v_pairs[0][:, :T], v_pairs[1][:, T:], v_pairs[1][:, :T]]

        def load_band(tiles, table, k):
            nc.sync.dma_start(tiles[k][:, :], table[k * P:(k + 1) * P, :])

        def load_xm(h):
            nc.sync.dma_start(xm_raw[h][:], xm_rows[:, :, h * (D // 2):(h + 1) * (D // 2)])

        load_xm(0)
        for h in range(2):
            nc.sync.dma_start(y_sb[h][:], y_rows[:, :, h * (N // 2):(h + 1) * (N // 2)])
        load_band(v_old, vT, 0)
        load_xm(1)
        for k in (1, 2, 3):
            load_band(v_old, vT, k)
        load_band(m_old, mT, 0)
        load_band(m_new, mT, 0)
        load_band(v_new, vT, 0)
        load_band(m_new, mT, 2)
        load_band(m_old, mT, 1)
        for k in (2, 1):
            load_band(v_new, vT, k)
        for k in (1, 3):
            load_band(m_new, mT, k)
        nc.sync.dma_start(
            m_pair[:].rearrange("p (b t) -> p b t", b=2), mT[2 * P:, :].rearrange("(b p) t -> p b t", b=2))
        load_band(v_new, vT, 3)

        one = sb("one", [P, 1], F32)
        nc.vector.memset(one[:], 1.0)
        tiny_col = sb("tiny_col", [P, 1], F32)
        nc.scalar.activation(tiny_col[:], one[:], ACT.Copy, scale=TINY)
        ident = sb("ident", [P, P], F32)
        make_identity(nc, ident[:])
        for k in range(BANDS):
            nc.gpsimd.memset(step[k][:], 0.0)
        wt_bank = psum.tile([P, PACK, P], F32, name="wt_bank", tag="dw3")
        for t in range(PACK):
            nc.tensor.transpose(wt_bank[:, t, :], wt_row[:, t:R:PACK], ident[:])
        wt_words = wt_bank[:].rearrange("p t n -> p n t")[:, 0:1, :]
        wt_wide = sb("wt_wide", [P, CHUNK, PACK], F32)
        nc.scalar.activation(wt_wide[:], wt_words.to_broadcast([P, CHUNK, PACK]), ACT.Copy)

        def slots(lo, hi):
            return offsets[:, lo // LIST_ROWS:hi // LIST_ROWS]

        def gather_on_scalar(dst, window, lo=0, hi=N, scale=1.0):
            nc.scalar.activation(dst[:, lo:hi], window[:, :].indirect(slots(lo, hi)), ACT.Copy, scale=scale)

        def gather_on_vector(dst, window, lo=0, hi=N):
            nc.vector.tensor_copy(dst[:, lo:hi], window[:, :].indirect(slots(lo, hi)))

        def gather_scaled_on_vector(dst, pair, scale):
            nc.vector.tensor_scalar(dst[:], pair[:].indirect(offsets[:]), scale, 0.0, ALU.mult, ALU.add)

        def quantise(codes, scales, fmt, src):
            nc.vector.quantize_mx(out=codes.bitcast(fmt), scales=scales, in_=src)

        w_places = sb("w_places", [P, PACK, N], BF16)
        gather_on_vector(w_places[:, 0, :], w_raw[0])
        gather_on_scalar(w_places[:, 1, :], w_raw[1])
        gather_on_vector(w_places[:, 2, :], w_raw[2])
        gather_on_scalar(w_places[:, 3, :], w_raw[3], 0, W_GATHER_ON_SCALAR)
        gather_on_vector(w_places[:, 3, :], w_raw[3], W_GATHER_ON_SCALAR, N)
        w_bf = sb("w_bf", [P, N, PACK], BF16)
        nc.scalar.copy(woven(w_bf[:, :W_WEAVE_ON_SCALAR, :]), by_places(w_places[:, :, :W_WEAVE_ON_SCALAR]))
        for lo, hi in ((W_WEAVE_ON_SCALAR, W_GATHER_ON_SCALAR), (W_GATHER_ON_SCALAR, N // 2), (N // 2, N)):
            nc.vector.tensor_copy(woven(w_bf[:, lo:hi, :]), by_places(w_places[:, :, lo:hi]))
        w_codes = sb("w_codes", [P, N], U32)
        w_scales = sb("w_scales", [P, N], U8)
        for lo in (0, N // 2):
            cols = slice(lo, lo + N // 2)
            quantise(w_codes[:, cols], w_scales[:, cols], E4M3, w_bf[:, cols, :].rearrange("p i t -> p (i t)"))

        x_bf = sb("x_bf", [P, PACK, P, PACK], BF16)

        def x_views(h, lo, hi):
            dst = x_bf[:, :, h * (P // 2) + lo:h * (P // 2) + hi, :].rearrange("p t m j -> p m j t")
            return dst, x_raw[h][:].rearrange("p j (m t) -> p m j t", t=PACK)[:, lo:hi, :, :]

        nc.scalar.activation(*x_views(0, 0, P // 2), ACT.Copy)
        nc.scalar.activation(*x_views(1, 0, X_CAST_ON_SCALAR), ACT.Copy)
        nc.vector.tensor_copy(*x_views(1, X_CAST_ON_SCALAR, P // 2))
        x_codes = sb("x_codes", [P, R], U32)
        x_scales = sb("x_scales", [P, R], U8)
        quantise(x_codes[:], x_scales[:], E4M3, x_bf[:].rearrange("p t m j -> p (t m j)"))

        g_codes = sb("g_codes", [P, N], U32)
        g_scales = sb("g_scales", [P, N], U8)
        g_bf = sb("g_bf", [P, N, PACK], BF16)
        diffs = [sb("diff%d" % c, [P, PACK, CHUNK], F32) for c in range(CHUNKS)]
        for c in range(CHUNKS):
            cols = slice(c * CHUNK, (c + 1) * CHUNK)
            a = psum.tile([P, PACK, CHUNK], F32, name="a%d" % c)[:]
            for t in range(PACK):
                rows = slice(t * P, (t + 1) * P)
                nc.tensor.matmul_mx(
                    out=a[:, t, :],
                    lhsT=x_codes[:, rows].bitcast(E4M3), lhsT_scale=x_scales[:, rows],
                    rhs=w_codes[:, cols].bitcast(E4M3), rhs_scale=w_scales[:, cols],
                    start=True, stop=True)
            y_part = y_sb[c // 2][:, :, (c % 2) * CHUNK:(c % 2 + 1) * CHUNK]
            nc.vector.tensor_tensor(diffs[c][:], a, y_part, ALU.subtract)
        for c, width in ((0, CHUNK), (1, G_WEIGH_ON_GPSIMD)):
            lo = c * CHUNK
            th = sb("th%d" % c, [P, CHUNK, PACK], F32)
            nc.scalar.activation(woven(th[:]), by_places(diffs[c][:]), ACT.Tanh)
            nc.gpsimd.tensor_tensor(g_bf[:, lo:lo + width, :], th[:, :width, :], wt_wide[:, :width, :], ALU.mult)
        nc.vector.tensor_tensor(
            g_bf[:, lo + width:lo + CHUNK, :], th[:, width:, :], wt_words.to_broadcast([P, CHUNK - width, PACK]),
            ALU.mult)
        ths = [sb("th%d" % c, [P, PACK, CHUNK], F32) for c in (2, 3)]
        for c in (2, 3):
            nc.scalar.activation(ths[c - 2][:], diffs[c][:], ACT.Tanh)
            nc.vector.tensor_tensor(
                woven(g_bf[:, c * CHUNK:(c + 1) * CHUNK, :]), by_places(ths[c - 2][:]),
                wt_bank[:, :, 0:1].unsqueeze(1).to_broadcast([P, CHUNK // RUN, PACK, RUN]), ALU.mult)

        eps_cols = diffs[3][:, 0, :]
        nc.scalar.activation(eps_cols[:, 0:1], one[:], ACT.Abs_reciprocal_sqrt, scale=(RATE / EPS) ** 4)
        nc.scalar.activation(eps_cols[:, 1:2], one[:], ACT.Abs_reciprocal_sqrt, scale=(RATE / EPS) ** 2)

        xm_codes = [sb("xm_codes%d" % h, [P, 2 * P], U32) for h in range(2)]
        xm_scales = [sb("xm_scales%d" % h, [P, 2 * P], U8) for h in range(2)]

        def quantise_xm(h, xm_bf):
            quantise(xm_codes[h][:], xm_scales[h][:], E4M3, xm_bf[:].rearrange("p d t -> p (d t)"))

        xm_early = sb("xm_bf0", [P, 2 * P, PACK], BF16)
        nc.scalar.activation(woven(xm_early[:, :P, :]), by_places(xm_raw[0][:, :, :P]), ACT.Copy)
        nc.vector.tensor_copy(woven(xm_early[:, P:, :]), by_places(xm_raw[0][:, :, P:]))
        quantise_xm(0, xm_early)
        quantise(g_codes[:], g_scales[:], E5M2, g_bf[:].rearrange("p i t -> p (i t)"))
        xm_late = sb("xm_bf1", [P, 2 * P, PACK], BF16, tag="th3")
        nc.vector.tensor_copy(woven(xm_late[:]), by_places(xm_raw[1][:]))
        quantise_xm(1, xm_late)

        def halves(pairs):
            return [pairs[k // 2][:, (k % 2) * N:(k % 2 + 1) * N] for k in range(BANDS)]

        def pair(name):
            return sb(name, [P, 2 * N], F32)

        nm = four("nm", N)
        nv_pairs = [pair("nv0"), pair("nv1")]
        divisor_pairs = [pair("divisor0"), pair("divisor1")]
        inverse_pairs = [pair("inverse0"), divisor_pairs[0]]
        nv, inverse = halves(nv_pairs), halves(inverse_pairs)
        v_picked = [sb("v_picked0", [P, N], F32, tag="diff2")] + [sb("v_picked%d" % k, [P, N], F32) for k in (1, 2, 3)]
        late_roots = pair("root1")
        m_picked = [late_roots[:, HALF:HALF + N], inverse[0], sb("m_picked2", [P, N], F32), sb("m_picked3", [P, N], F32)]
        dw = []
        for k in range(BANDS):
            rows = slice((k % 2) * P, (k % 2 + 1) * P)
            bank = psum.tile([P, N], F32, name="dw%d" % k)
            nc.tensor.matmul_mx(
                out=bank[:], lhsT=xm_codes[k // 2][:, rows].bitcast(E4M3), lhsT_scale=xm_scales[k // 2][:, rows],
                rhs=g_codes[:].bitcast(E5M2), rhs_scale=g_scales[:], start=True, stop=True)
            dw.append(bank)

        def scatter_on_scalar(window, values, scale, lo, hi):
            nc.scalar.activation(window[:].indirect(slots(lo, hi)), values[:, lo:hi], ACT.Copy, scale=scale)

        def scatter_on_vector(window, values):
            nc.vector.tensor_copy(window[:].indirect(offsets[:]), values[:])

        def square(k):
            nc.scalar.activation(nv[k][:], dw[k][:], ACT.Square, scale=math.sqrt(1.0 - RHO))

        def new_v(k):
            nc.gpsimd.tensor_tensor(nv[k][:], nv[k][:], v_picked[k][:], ALU.add)

        def new_m(k):
            nc.vector.scalar_tensor_tensor(
                nm[k][:], dw[k][:], -(1.0 - BETA) / BETA, m_picked[k][:], ALU.mult, ALU.subtract)

        def first_roots(out, squares):
            nc.scalar.activation(out[:], squares[:], ACT.Abs_reciprocal_sqrt, bias=tiny_col[:])

        def new_divisors(h, roots):
            if h == 0:
                nc.gpsimd.tensor_scalar(roots[:], roots[:], 2.0 * EPS, 1.0, ALU.mult, ALU.add)
            nc.gpsimd.tensor_tensor(divisor_pairs[h][:], roots[:], nv_pairs[h][:], ALU.mult)

        def second_roots(h):
            if h == 0:
                nc.scalar.activation(
                    inverse_pairs[0][:], divisor_pairs[0][:], ACT.Abs_reciprocal_sqrt, bias=eps_cols[:, 0:1],
                    scale=1.0 / RATE ** 2)
                return
            for k, unit in ((2, 1.0 - RHO), (3, 1.0)):
                nc.scalar.activation(
                    inverse[k][:], divisor_pairs[1][:, (k - 2) * N:(k - 1) * N], ACT.Abs_reciprocal_sqrt,
                    bias=eps_cols[:, 1:2], scale=math.sqrt(unit) / RATE)

        def times_m(out, k):
            nc.gpsimd.tensor_tensor(out[:], inverse[k][:], nm[k][:], ALU.mult)

        gather_on_scalar(v_picked[0], v_old[0], scale=RHO)
        gather_scaled_on_vector(v_picked[1], v_pairs[0], RHO)
        square(0)
        square(1)
        gather_on_scalar(v_picked[2], v_old[2], scale=RHO / (1.0 - RHO))
        nc.scalar.activation(nm[2][:], dw[2][:], ACT.Copy, scale=-1.0)
        square(3)
        new_v(0)
        new_v(1)
        nc.gpsimd.tensor_tensor(nv[2][:], nm[2][:], nm[2][:], ALU.mult)
        new_v(2)
        gather_scaled_on_vector(v_picked[3], v_pairs[1], RHO)
        new_v(3)
        gather_on_vector(m_picked[0], m_old[0])
        new_m(0)
        roots = [sb("root0", [P, 2 * N], F32, tag="v_pair1"), late_roots]
        first_roots(roots[0], nv_pairs[0])
        scatter_on_scalar(m_new[0], nm[0], -BETA, 0, LONG)
        for h in range(2):
            first_roots(late_roots[:, h * N:(h + 1) * N], nv[2 + h])
        scatter_on_scalar(m_new[0], nm[0], -BETA, LONG, N)
        scatter_on_vector(v_new[0], nv[0])
        new_divisors(0, roots[0])
        new_divisors(1, roots[1])
        gather_on_vector(m_picked[1], m_old[1])
        new_m(1)
        scatter_on_scalar(v_new[2], nv[2], 1.0 - RHO, 0, LONG)
        second_roots(0)
        scatter_on_scalar(v_new[2], nv[2], 1.0 - RHO, LONG, N)
        second_roots(1)
        scatter_on_vector(v_new[1], nv[1])
        times_m(inverse[0], 0)
        for lo in (0, HALF):
            scatter_on_scalar(m_new[1], nm[1], -BETA, lo, lo + HALF)
            scatter_on_scalar(step[0], inverse[0], 1.0, lo, lo + HALF)
        for k in (3, 2):
            gather_on_vector(m_picked[k], m_old[k])
        nc.gpsimd.tensor_tensor(nm[2][:], nm[2][:], m_picked[2][:], ALU.subtract)
        new_m(3)
        scatter_on_vector(v_new[3], nv[3])
        times_m(m_picked[3], 1)
        scatter_on_vector(step[1], m_picked[3])
        for k, lo, hi in ((3, 0, LONG), (2, 0, N - LONG), (3, LONG, N), (2, N - LONG, N)):
            scatter_on_scalar(m_new[k], nm[k], -BETA, lo, hi)
        for k, product in ((3, m_picked[2]), (2, inverse[1])):
            times_m(product, k)
            nc.vector.tensor_tensor(step[k][:].indirect(offsets[:]), inverse[k][:], product[:], ALU.mult)

        for out, windows, k in (
                (out_2, v_new, 0), (out_1, m_new, 0), (out_2, v_new, 1), (out_2, v_new, 2), (out_2, v_new, 3),
                (out_1, m_new, 1), (out_0, step, 0), (out_0, step, 1), (out_1, m_new, 3), (out_0, step, 3),
                (out_1, m_new, 2), (out_0, step, 2)):
            nc.sync.dma_start(out[k * P:(k + 1) * P, :], windows[k][:])
